import numpy as np
import ml_dtypes


def mxq(x, axis, fmt="e4m3"):
    dtype, down = {"e4m3": (ml_dtypes.float8_e4m3fn, 7), "e5m2": (ml_dtypes.float8_e5m2, 14)}[fmt]
    v = np.moveaxis(np.asarray(x, np.float32).astype(ml_dtypes.bfloat16).astype(np.float64), axis, -1)
    blocks = v.reshape(v.shape[:-1] + (-1, 32))
    amax = np.abs(blocks).max(-1, keepdims=True)
    byte = np.maximum(np.where(amax > 0, np.frexp(amax)[1] - 1 + 127, 0) - down, 1)
    scale = np.exp2(byte - 127.0)
    codes = (blocks / scale).astype(np.float32).astype(dtype).astype(np.float64)
    return np.moveaxis((codes * scale).reshape(v.shape), -1, axis)


WIDE = False


def mx_kscale(k):
    if not WIDE:
        return np.ones(k)
    levels = np.array([10, -10, 5, -5, 0])
    if k % 512:
        return np.exp2(np.random.permutation(np.resize(levels, k // 32))).repeat(32)
    a = np.empty((k // 512, 16))
    for p in range(k // 512):
        a[p, :8] = np.random.permutation(np.resize(levels, 8))
        for g in range(8):
            far = levels[np.abs(levels - a[p, g]) >= 10]
            a[p, g + 8] = far[np.random.randint(len(far))]
    return np.exp2(a.ravel()).repeat(32)


def f64(x):
    return np.asarray(x).astype(np.float64)


def striped(idx):
    return np.tile(idx.reshape(-1, 16).T, (8, 1)).astype(np.uint16)


def unstriped(offs):
    return offs[:16].T.reshape(-1).astype(np.int64)


E2M1 = np.array([0.0, 0.5, 1.0, 1.5, 2.0, 3.0, 4.0, 6.0, -0.0, -0.5, -1.0, -1.5, -2.0, -3.0, -4.0, -6.0])


def pack_weight(w, fmt):
    k, n = w.shape
    w = f64(np.asarray(w, np.float32).astype(ml_dtypes.bfloat16)).reshape(k // 32, 32, n)
    amax = np.abs(w).max(1)
    if fmt == "e4m3":
        byte = np.frexp(amax)[1] - 1 + 127 - 7
    else:
        mant, ex = np.frexp(amax / 6.0)
        byte = np.where(mant > 0.5, ex, ex - 1) + 127
    byte = np.clip(np.where(amax > 0, byte, 1), 1, 254)
    scaled = (w * np.exp2(127.0 - byte)[:, None, :]).reshape(k, n).astype(np.float32)
    by_word = np.ascontiguousarray(scaled.reshape(k // 512, 128, 4, n).transpose(0, 1, 3, 2))
    if fmt == "e4m3":
        words = by_word.astype(ml_dtypes.float8_e4m3fn).view(np.uint8)
    else:
        c = by_word.astype(ml_dtypes.float4_e2m1fn).view(np.uint8) & 0xF
        words = (c[..., 0::2] | (c[..., 1::2] << 4)).reshape(k // 512, 128, 2 * n)
    return np.ascontiguousarray(words), np.ascontiguousarray(byte.astype(np.uint8).reshape(k // 512, 16, n))


def unpack_weight(words, scales, fmt):
    g, _, n = scales.shape
    words = np.ascontiguousarray(words).reshape(g, 128, n, -1)
    if fmt == "e4m3":
        vals = words.view(ml_dtypes.float8_e4m3fn).astype(np.float64)
    else:
        nib = np.empty((g, 128, n, 4), np.uint8)
        nib[..., 0::2] = words & 0xF
        nib[..., 1::2] = words >> 4
        vals = E2M1[nib]
    vals = vals * np.repeat(np.exp2(scales.astype(np.float64) - 127.0), 8, axis=1)[..., None]
    return vals.transpose(0, 1, 3, 2).reshape(g * 512, n)


def d_silu(v):
    s = 1.0 / (1.0 + np.exp(-np.maximum(v, -700.0)))
    return s * (1.0 + v * (1.0 - s))


K, T, G, C1, E, C2, H = 512, 1024, 2, 512, 4, 256, 512
N = 1024


def by_expert(wq, xq, E, C):
    return np.concatenate([wq[e].T @ xq[:, e * C:(e + 1) * C] for e in range(E)], axis=1)


def setup_inputs():
    n = np.random.standard_normal
    v = mx_kscale(N)
    u = mx_kscale(H)
    slots1 = np.random.permutation(T)
    slots2 = np.concatenate([q * C1 + np.random.permutation(C1) for q in range(G)])
    dy = pack_weight(n((N, T)) * v[:, None], "e4m3")
    wet = [pack_weight(m, "e2m1") for m in n((E, N, H)) / np.sqrt(N) / v[None, :, None] * u]
    wgt = [pack_weight(m, "e2m1") for m in n((G, H, K)) / np.sqrt(H) / u[None, :, None]]
    return {
        "dy_words": dy[0],
        "dy_scales": dy[1],
        "wet_words": np.stack([m[0] for m in wet]),
        "wet_scales": np.stack([m[1] for m in wet]),
        "wgt_words": np.stack([m[0] for m in wgt]),
        "wgt_scales": np.stack([m[1] for m in wgt]),
        "a": (n((H, T))).astype(np.float32),
        "gate": (np.tile(np.random.uniform(0.2, 1.0, T), (128, 1))).astype(np.float32),
        "offs": striped(slots1),
        "offs2": striped(slots2),
        "dst": striped(slots1[slots2]),
    }


def reference(dy_words, dy_scales, wet_words, wet_scales, wgt_words, wgt_scales, a, gate, offs, offs2, dst):
    wet = np.stack([unpack_weight(wet_words[e], wet_scales[e], "e2m1") for e in range(E)])
    wgt = np.stack([unpack_weight(wgt_words[e], wgt_scales[e], "e2m1") for e in range(G)])
    gq = unpack_weight(dy_words, dy_scales, "e4m3")[:, unstriped(dst)]
    z = f64(gate[:1]) * by_expert(wet, gq, E, C2)
    da = np.zeros((H, T))
    da[:, unstriped(offs2)] = z
    dx = by_expert(wgt, mxq(da * d_silu(f64(a)), 0, "e4m3"), G, C1)
    out = np.zeros((K, T))
    out[:, unstriped(offs)] = dx
    return out

@@ -1,0 +1,181 @@
+from contextlib import ExitStack
+
+import concourse.mybir as mybir
+from concourse.masks import make_identity
+
+K, T, G, C1, E, C2, H, N = 512, 1024, 2, 512, 4, 256, 512, 1024
+FLOPS = 2 * T * N * H + 2 * T * H * K
+
+F32 = mybir.dt.float32
+BF16 = mybir.dt.bfloat16
+I32 = mybir.dt.int32
+U32 = mybir.dt.uint32
+U16 = mybir.dt.uint16
+U8 = mybir.dt.uint8
+FP8X4 = mybir.dt.float8_e4m3fn_x4
+FP4X4 = mybir.dt.float4_e2m1fn_x4
+ACT = mybir.ActivationFunctionType
+ALU = mybir.AluOpType
+
+P = 128
+PACK = 4
+PASSES = N // (P * PACK)
+LIST = 16
+
+
+def tile_moe_hib_silu_kernel(tc, dy_words, dy_scales, wet_words, wet_scales, wgt_words, wgt_scales, a, gate, offs, offs2, dst, out):
+    nc = tc.nc
+    with ExitStack() as ctx:
+        lists = ctx.enter_context(tc.tile_pool(name="lists", bufs=1))
+        keep = ctx.enter_context(tc.tile_pool(name="keep", bufs=1))
+        ring = ctx.enter_context(tc.tile_pool(name="ring", bufs=4))
+        ps1 = ctx.enter_context(tc.psum_pool(name="ps1", bufs=3))
+        pst = ctx.enter_context(tc.psum_pool(name="pst", bufs=3))
+        ps2 = ctx.enter_context(tc.psum_pool(name="ps2", bufs=2))
+
+        dst_t = lists.tile([P, T // LIST], U16, name="dst_t")
+        offs2_t = lists.tile([P, T // LIST], U16, name="offs2_t")
+        offs_t = lists.tile([P, T // LIST], U16, name="offs_t")
+
+        dyw = [keep.tile([P, T], I32, name="dyw%d" % s, align_bytes=64) for s in range(PASSES)]
+        dys = keep.tile([P, PASSES, T], U8, name="dys", align_bytes=64)
+        wetw = keep.tile([P, E * PASSES, 2 * H], U8, name="wetw", align_bytes=64)
+        wets = keep.tile([P, E * PASSES, H], U8, name="wets", align_bytes=64)
+        wgtw = keep.tile([P, G, 2 * K], U8, name="wgtw", align_bytes=64)
+        wgts = keep.tile([P, G, K], U8, name="wgts", align_bytes=64)
+        gate_rows = keep.tile([P, P], F32, name="gate_rows")
+        gate_col = keep.tile([P, T // P], F32, name="gate_col")
+        ident = keep.tile([P, P], F32, name="ident")
+        a_t = [keep.tile([P, PACK, C1], F32, name="a%d" % f) for f in range(G)]
+        ds = [keep.tile([P, PACK, C1], F32, name="ds%d" % f) for f in range(G)]
+
+        nc.vector.memset(dys[:].bitcast(I32), 0)
+        nc.vector.memset(wets[:].bitcast(I32), 0)
+        nc.vector.memset(wgts[:].bitcast(I32), 0)
+        make_identity(nc, ident[:])
+
+        nc.sync.dma_start(dst_t[:], dst)
+        for s in range(PASSES):
+            nc.sync.dma_start(dyw[s][:], dy_words[s].rearrange("p t d -> p (t d)").bitcast(I32))
+        for q in range(4):
+            nc.sync.dma_start(dys[32 * q:32 * q + 4].bitcast(I32), dy_scales[:, 4 * q:4 * q + 4, :].rearrange("s b t -> b s t").bitcast(I32))
+        for q in range(4):
+            nc.sync.dma_start(wets[32 * q:32 * q + 4].bitcast(I32), wet_scales[:, :, 4 * q:4 * q + 4, :].rearrange("e s b i -> b (e s) i").bitcast(I32))
+        nc.sync.dma_start(wetw[:, 0:PASSES, :].bitcast(I32), wet_words[0].rearrange("s p c -> p s c").bitcast(I32))
+        nc.sync.dma_start(gate_rows[:], gate[0:16, :].rearrange("c (b p) -> (c b) p", p=P))
+        nc.sync.dma_start(wetw[:, PASSES:, :].bitcast(I32), wet_words[1:].rearrange("e s p c -> p (e s) c").bitcast(I32))
+        nc.sync.dma_start(offs2_t[:], offs2)
+        a_rows = a.rearrange("(p r) j -> p r j", r=PACK)
+        for f in range(G):
+            nc.sync.dma_start(a_t[f][:], a_rows[:, :, f * C1:(f + 1) * C1])
+        nc.sync.dma_start(wgtw[:].bitcast(I32), wgt_words.rearrange("f s p c -> p (f s) c").bitcast(I32))
+        for q in range(4):
+            nc.sync.dma_start(wgts[32 * q:32 * q + 4].bitcast(I32), wgt_scales[:, :, 4 * q:4 * q + 4, :].rearrange("f s b k -> b (f s) k").bitcast(I32))
+        nc.sync.dma_start(offs_t[:], offs)
+
+        gate_ps = pst.tile([P, PACK, P], F32, name="turned")
+        nc.tensor.transpose(gate_ps[:, 0, :], gate_rows[:], ident[:])
+        nc.scalar.activation(gate_col[:], gate_ps[:, 0, 0:T // P], ACT.Copy)
+
+        gw = [keep.tile([P, T], U32, name="gw%d" % s, align_bytes=64) for s in range(PASSES)]
+        gs = keep.tile([P, PASSES, T], U8, name="gs", align_bytes=64)
+        zs = [keep.tile([P, PACK, C1], F32, name="zs%d" % f) for f in range(G)]
+
+        def gather_words(s, lo, hi):
+            nc.vector.tensor_copy(gw[s][:, lo:hi], dyw[s][:].bitcast(U32).indirect(dst_t[:, lo // LIST:hi // LIST]))
+
+        def gather_scales(s, lo, hi):
+            nc.vector.tensor_copy(gs[:, s, lo:hi], dys[:, s, :].indirect(dst_t[:, lo // LIST:hi // LIST]))
+
+        def first_product(b):
+            e = b * P // C2
+            cols = slice(b * P, (b + 1) * P)
+            acc = ps1.tile([P, H], F32, name="acc")
+            for s in range(PASSES):
+                nc.tensor.matmul_mx(
+                    out=acc[:],
+                    lhsT=gw[s][:, cols].bitcast(FP8X4), lhsT_scale=gs[:, s, cols],
+                    rhs=wetw[:, e * PASSES + s, :].bitcast(FP4X4), rhs_scale=wets[:, e * PASSES + s, :],
+                    start=(s == 0), stop=(s == PASSES - 1))
+            zt = ring.tile([P, PACK, P], F32, name="zt")
+            nc.scalar.activation(zt[:], acc[:].rearrange("m (p r) -> m r p", r=PACK), ACT.Copy, scale=gate_col[:, b:b + 1])
+            return zt
+
+        def turn(b, zt):
+            f, u = divmod(b * P, C1)
+            turned = pst.tile([P, PACK, P], F32, name="turned")
+            for r in range(PACK):
+                nc.tensor.transpose(turned[:, r, :], zt[:, r, :], ident[:])
+            nc.scalar.activation(zs[f][:, :, u:u + P], turned[:], ACT.Copy)
+
+        for s in range(PASSES):
+            for f in range(G):
+                gather_words(s, f * C1, (f + 1) * C1)
+        for e in range(E):
+            for s in range(PASSES):
+                gather_scales(s, e * C2, (e + 1) * C2)
+        for e in range(E):
+            zts = [first_product(b) for b in (2 * e, 2 * e + 1)]
+            for b in (2 * e, 2 * e + 1):
+                turn(b, zts[b - 2 * e])
+
+        zw = [[keep.tile([P, T], F32, name="zw%d_%d" % (f, r)) for r in range(PACK)] for f in range(G)]
+        ow = [keep.tile([P, T], F32, name="ow%d" % c) for c in range(K // P)]
+        dxs = [keep.tile([P, K // P, C1], F32, name="dxs%d" % f) for f in range(G)]
+
+        def sigmoid(f, r, dest):
+            nc.scalar.activation(dest[:, r, :], a_t[f][:, r, :], ACT.Sigmoid)
+
+        def one_less_silu(f, r, dest):
+            nc.scalar.activation(dest[:, r, :], a_t[f][:, r, :], ACT.Silu, scale=-1.0)
+            nc.scalar.activation(dest[:, r, :], dest[:, r, :], ACT.Identity, scale=-1.0, bias=1.0)
+
+        def derivative(f):
+            first, second = (sigmoid, one_less_silu) if f == 0 else (one_less_silu, sigmoid)
+            for r in range(PACK):
+                first(f, r, ds[f])
+            for r in range(PACK):
+                second(f, r, a_t[f])
+                nc.gpsimd.tensor_tensor(ds[f][:, r, :], ds[f][:, r, :], a_t[f][:, r, :], ALU.mult)
+
+        def scatter_z(f, r, lo, hi):
+            ix = offs2_t[:, (f * C1 + lo) // LIST:(f * C1 + hi) // LIST]
+            nc.vector.tensor_copy(zw[f][r][:].indirect(ix), zs[f][:, r, lo:hi])
+
+        def second_product(f):
+            planes = keep.tile([P, PACK, C1], BF16, name="planes%d" % f)
+            for r in range(PACK):
+                nc.gpsimd.tensor_tensor(planes[:, r, :], zw[f][r][:, f * C1:(f + 1) * C1], ds[f][:, r, :], ALU.mult)
+            grouped = keep.tile([P, C1, PACK], BF16, name="grouped%d" % f, align_bytes=64)
+            nc.scalar.copy(grouped[:], planes[:].rearrange("p r j -> p j r"))
+            codes = keep.tile([P, C1], U32, name="codes%d" % f, align_bytes=64)
+            scales = keep.tile([P, C1], U8, name="scales%d" % f, align_bytes=64)
+            nc.vector.quantize_mx(out=codes[:].bitcast(FP8X4), scales=scales[:], in_=grouped[:].rearrange("p j r -> p (j r)"))
+            for c in range(K // P):
+                acc2 = ps2.tile([P, C1], F32, name="acc2")
+                nc.tensor.matmul_mx(
+                    out=acc2[:],
+                    lhsT=wgtw[:, f, 2 * P * c:2 * P * (c + 1)].bitcast(FP4X4), lhsT_scale=wgts[:, f, P * c:P * (c + 1)],
+                    rhs=codes[:].bitcast(FP8X4), rhs_scale=scales[:],
+                    start=True, stop=True)
+                nc.scalar.activation(dxs[f][:, c, :], acc2[:], ACT.Copy)
+
+        def scatter_dx(f, c):
+            ix = offs_t[:, f * C1 // LIST:(f + 1) * C1 // LIST]
+            nc.vector.tensor_copy(ow[c][:].indirect(ix), dxs[f][:, c, :])
+
+        derivative(0)
+        for r in range(PACK):
+            scatter_z(0, r, 0, C2)
+        for r in range(PACK):
+            scatter_z(0, r, C2, C1)
+        second_product(0)
+        derivative(1)
+        for r in range(PACK):
+            scatter_z(1, r, 0, C1)
+        second_product(1)
+        for c in range(K // P):
+            scatter_dx(0, c)
+        for c in range(K // P):
+            scatter_dx(1, c)
+            nc.sync.dma_start(out[c * P:(c + 1) * P, :], ow[c][:])

@@ -37,45 +37,48 @@ def tile_moe_hib_silu_kernel(tc, dy_words, dy_scales, wet_words, wet_scales, wgt
         offs2_t = lists.tile([P, T // LIST], U16, name="offs2_t")
         offs_t = lists.tile([P, T // LIST], U16, name="offs_t")
 
-        dyw = [keep.tile([P, T], I32, name="dyw%d" % s, align_bytes=64) for s in range(PASSES)]
-        dys = keep.tile([P, PASSES, T], U8, name="dys", align_bytes=64)
-        wetw = keep.tile([P, E * PASSES, 2 * H], U8, name="wetw", align_bytes=64)
+        dyw = [keep.tile([P, T], I32, name="dyw%d" % s, tag="after_words%d" % s, align_bytes=64) for s in range(PASSES)]
+        dys = keep.tile([P, PASSES, T], U8, name="dys", tag="after_scales", align_bytes=64)
+        wet_first = keep.tile([P, PASSES, 2 * H], U8, name="wet_first", align_bytes=64)
         wets = keep.tile([P, E * PASSES, H], U8, name="wets", align_bytes=64)
-        wgtw = keep.tile([P, G, 2 * K], U8, name="wgtw", align_bytes=64)
-        wgts = keep.tile([P, G, K], U8, name="wgts", align_bytes=64)
-        gate_rows = keep.tile([P, P], F32, name="gate_rows")
+        gate_rows = keep.tile([P, P], F32, name="gate_rows", tag="after_gate", align_bytes=64)
         gate_col = keep.tile([P, T // P], F32, name="gate_col")
         ident = keep.tile([P, P], F32, name="ident")
-        a_t = [keep.tile([P, PACK, C1], F32, name="a%d" % f) for f in range(G)]
+        a_t = [keep.tile([P, PACK, C1], F32, name="a0")]
         ds = [keep.tile([P, PACK, C1], F32, name="ds%d" % f) for f in range(G)]
 
         nc.vector.memset(dys[:].bitcast(I32), 0)
         nc.vector.memset(wets[:].bitcast(I32), 0)
-        nc.vector.memset(wgts[:].bitcast(I32), 0)
         make_identity(nc, ident[:])
 
-        nc.sync.dma_start(dst_t[:], dst)
-        for s in range(PASSES):
-            nc.sync.dma_start(dyw[s][:], dy_words[s].rearrange("p t d -> p (t d)").bitcast(I32))
-        for q in range(4):
-            nc.sync.dma_start(dys[32 * q:32 * q + 4].bitcast(I32), dy_scales[:, 4 * q:4 * q + 4, :].rearrange("s b t -> b s t").bitcast(I32))
-        for q in range(4):
-            nc.sync.dma_start(wets[32 * q:32 * q + 4].bitcast(I32), wet_scales[:, :, 4 * q:4 * q + 4, :].rearrange("e s b i -> b (e s) i").bitcast(I32))
-        nc.sync.dma_start(wetw[:, 0:PASSES, :].bitcast(I32), wet_words[0].rearrange("s p c -> p s c").bitcast(I32))
-        nc.sync.dma_start(gate_rows[:], gate[0:16, :].rearrange("c (b p) -> (c b) p", p=P))
-        nc.sync.dma_start(wetw[:, PASSES:, :].bitcast(I32), wet_words[1:].rearrange("e s p c -> p (e s) c").bitcast(I32))
-        nc.sync.dma_start(offs2_t[:], offs2)
+        def load_words(tile, words):
+            nc.sync.dma_start(tile.bitcast(I32), words.bitcast(I32))
+
+        def load_scales(plane, scales, queues):
+            for q in range(4):
+                queues[q].dma_start(plane[32 * q:32 * q + 4].bitcast(I32), scales[:, 4 * q:4 * q + 4, :].rearrange("s b t -> b s t").bitcast(I32))
+
         a_rows = a.rearrange("(p r) j -> p r j", r=PACK)
-        for f in range(G):
-            nc.sync.dma_start(a_t[f][:], a_rows[:, :, f * C1:(f + 1) * C1])
-        nc.sync.dma_start(wgtw[:].bitcast(I32), wgt_words.rearrange("f s p c -> p (f s) c").bitcast(I32))
-        for q in range(4):
-            nc.sync.dma_start(wgts[32 * q:32 * q + 4].bitcast(I32), wgt_scales[:, :, 4 * q:4 * q + 4, :].rearrange("f s b k -> b (f s) k").bitcast(I32))
+        wet_rows = wet_words.rearrange("e s p c -> p (e s) c")
+        side = (nc.scalar, nc.gpsimd, nc.scalar, nc.gpsimd)
+        load_words(dyw[0][:], dy_words[0].rearrange("p t d -> p (t d)"))
+        nc.sync.dma_start(dst_t[:], dst)
+        load_words(dyw[1][:], dy_words[1].rearrange("p t d -> p (t d)"))
+        load_scales(dys, dy_scales, side)
+        load_scales(wets, wet_scales.rearrange("e s b i -> (e s) b i"), side)
+        nc.scalar.dma_start(gate_rows[:], gate[0:16, :].rearrange("c (b p) -> (c b) p", p=P))
+        load_words(wet_first[:], wet_rows[:, 0:PASSES, :])
+        nc.sync.dma_start(a_t[0][:], a_rows[:, :, 0:C1])
+        nc.sync.dma_start(offs2_t[:], offs2)
         nc.sync.dma_start(offs_t[:], offs)
 
         gate_ps = pst.tile([P, PACK, P], F32, name="turned")
         nc.tensor.transpose(gate_ps[:, 0, :], gate_rows[:], ident[:])
         nc.scalar.activation(gate_col[:], gate_ps[:, 0, 0:T // P], ACT.Copy)
+
+        wet_rest = keep.tile([P, (E - 1) * PASSES, 2 * H], U8, name="wet_rest", tag="after_gate", align_bytes=64)
+        load_words(wet_rest[:], wet_rows[:, PASSES:, :])
+        wetw = [wet_first[:]] + [wet_rest[:, PASSES * e:PASSES * (e + 1), :] for e in range(E - 1)]
 
         gw = [keep.tile([P, T], U32, name="gw%d" % s, align_bytes=64) for s in range(PASSES)]
         gs = keep.tile([P, PASSES, T], U8, name="gs", align_bytes=64)
@@ -95,7 +98,7 @@ def tile_moe_hib_silu_kernel(tc, dy_words, dy_scales, wet_words, wet_scales, wgt
                 nc.tensor.matmul_mx(
                     out=acc[:],
                     lhsT=gw[s][:, cols].bitcast(FP8X4), lhsT_scale=gs[:, s, cols],
-                    rhs=wetw[:, e * PASSES + s, :].bitcast(FP4X4), rhs_scale=wets[:, e * PASSES + s, :],
+                    rhs=wetw[e][:, s, :].bitcast(FP4X4), rhs_scale=wets[:, e * PASSES + s, :],
                     start=(s == 0), stop=(s == PASSES - 1))
             zt = ring.tile([P, PACK, P], F32, name="zt")
             nc.scalar.activation(zt[:], acc[:].rearrange("m (p r) -> m r p", r=PACK), ACT.Copy, scale=gate_col[:, b:b + 1])
@@ -108,45 +111,57 @@ def tile_moe_hib_silu_kernel(tc, dy_words, dy_scales, wet_words, wet_scales, wgt
                 nc.tensor.transpose(turned[:, r, :], zt[:, r, :], ident[:])
             nc.scalar.activation(zs[f][:, :, u:u + P], turned[:], ACT.Copy)
 
-        for s in range(PASSES):
-            for f in range(G):
-                gather_words(s, f * C1, (f + 1) * C1)
-        for e in range(E):
-            for s in range(PASSES):
-                gather_scales(s, e * C2, (e + 1) * C2)
-        for e in range(E):
+        def expert(e):
             zts = [first_product(b) for b in (2 * e, 2 * e + 1)]
             for b in (2 * e, 2 * e + 1):
                 turn(b, zts[b - 2 * e])
 
-        zw = [[keep.tile([P, T], F32, name="zw%d_%d" % (f, r)) for r in range(PACK)] for f in range(G)]
-        ow = [keep.tile([P, T], F32, name="ow%d" % c) for c in range(K // P)]
+        for s in range(PASSES):
+            gather_words(s, 0, C1)
+        for lo, hi in ((0, P), (P, C1)):
+            for s in range(PASSES):
+                gather_scales(s, lo, hi)
+        for s in range(PASSES):
+            gather_words(s, C1, T)
+        for s in range(PASSES):
+            gather_scales(s, C1, T)
+
+        a_t.append(keep.tile([P, PACK, C1], F32, name="a1", tag="after_words0", align_bytes=64))
+        wgtw = keep.tile([P, G, 2 * K], U8, name="wgtw", tag="after_words1", align_bytes=64)
+        wgts = keep.tile([P, G, K], U8, name="wgts", tag="after_scales", align_bytes=64)
+        nc.sync.dma_start(a_t[1][:], a_rows[:, :, C1:2 * C1])
+        load_words(wgtw[:], wgt_words.rearrange("f s p c -> p (f s) c"))
+        nc.gpsimd.memset(wgts[:].bitcast(I32), 0)
+        load_scales(wgts, wgt_scales.rearrange("f s b k -> (f s) b k"), [nc.sync] * 4)
+
         dxs = [keep.tile([P, K // P, C1], F32, name="dxs%d" % f) for f in range(G)]
 
-        def sigmoid(f, r, dest):
-            nc.scalar.activation(dest[:, r, :], a_t[f][:, r, :], ACT.Sigmoid)
-
-        def one_less_silu(f, r, dest):
-            nc.scalar.activation(dest[:, r, :], a_t[f][:, r, :], ACT.Silu, scale=-1.0)
-            nc.scalar.activation(dest[:, r, :], dest[:, r, :], ACT.Identity, scale=-1.0, bias=1.0)
+        def activations(f):
+            funcs = ((ACT.Sigmoid, 1.0), (ACT.Silu, -1.0))
+            first, second = funcs if f == 0 else funcs[::-1]
+            for r in range(PACK):
+                nc.scalar.activation(ds[f][:, r, :], a_t[f][:, r, :], first[0], scale=first[1])
+            for r in range(PACK):
+                nc.scalar.activation(a_t[f][:, r, :], a_t[f][:, r, :], second[0], scale=second[1])
 
         def derivative(f):
-            first, second = (sigmoid, one_less_silu) if f == 0 else (one_less_silu, sigmoid)
+            silu = a_t[f] if f == 0 else ds[f]
             for r in range(PACK):
-                first(f, r, ds[f])
-            for r in range(PACK):
-                second(f, r, a_t[f])
+                nc.gpsimd.tensor_scalar(silu[:, r, :], silu[:, r, :], -1.0, 1.0, ALU.mult, ALU.add)
                 nc.gpsimd.tensor_tensor(ds[f][:, r, :], ds[f][:, r, :], a_t[f][:, r, :], ALU.mult)
 
-        def scatter_z(f, r, lo, hi):
-            ix = offs2_t[:, (f * C1 + lo) // LIST:(f * C1 + hi) // LIST]
-            nc.vector.tensor_copy(zw[f][r][:].indirect(ix), zs[f][:, r, lo:hi])
+        def window(name, tag):
+            return keep.tile([P, T], F32, name=name, tag=tag, align_bytes=64)
 
-        def second_product(f):
+        def scatter_z(zw, f, r, lo, hi):
+            ix = offs2_t[:, (f * C1 + lo) // LIST:(f * C1 + hi) // LIST]
+            nc.vector.tensor_copy(zw[r][:].indirect(ix), zs[f][:, r, lo:hi])
+
+        def second_product(zw, f):
             planes = keep.tile([P, PACK, C1], BF16, name="planes%d" % f)
             for r in range(PACK):
-                nc.gpsimd.tensor_tensor(planes[:, r, :], zw[f][r][:, f * C1:(f + 1) * C1], ds[f][:, r, :], ALU.mult)
-            grouped = keep.tile([P, C1, PACK], BF16, name="grouped%d" % f, align_bytes=64)
+                nc.gpsimd.tensor_tensor(planes[:, r, :], zw[r][:, f * C1:(f + 1) * C1], ds[f][:, r, :], ALU.mult)
+            grouped = keep.tile([P, C1, PACK], BF16, name="grouped%d" % f, tag="after_quantize%d" % f, align_bytes=64)
             nc.scalar.copy(grouped[:], planes[:].rearrange("p r j -> p j r"))
             codes = keep.tile([P, C1], U32, name="codes%d" % f, align_bytes=64)
             scales = keep.tile([P, C1], U8, name="scales%d" % f, align_bytes=64)
@@ -164,16 +179,27 @@ def tile_moe_hib_silu_kernel(tc, dy_words, dy_scales, wet_words, wet_scales, wgt
             ix = offs_t[:, f * C1 // LIST:(f + 1) * C1 // LIST]
             nc.vector.tensor_copy(ow[c][:].indirect(ix), dxs[f][:, c, :])
 
+        last = PACK - 1
+        expert(0)
+        expert(1)
+        activations(0)
         derivative(0)
-        for r in range(PACK):
-            scatter_z(0, r, 0, C2)
-        for r in range(PACK):
-            scatter_z(0, r, C2, C1)
-        second_product(0)
+        expert(2)
+        expert(3)
+        activations(1)
+        zw0 = [window("zw0_%d" % r, "zw0_%d" % r) for r in range(PACK)]
+        for lo, hi in ((0, P), (P, C2), (C2, C1)):
+            for r in range(PACK):
+                scatter_z(zw0, 0, r, lo, hi)
+        second_product(zw0, 0)
         derivative(1)
-        for r in range(PACK):
-            scatter_z(1, r, 0, C1)
-        second_product(1)
+        zw1 = [window("zw1_%d" % r, "zw1_%d" % r if r < last else "after_quantize0") for r in range(PACK)]
+        for lo, hi in ((0, C2), (C2, C1)):
+            for r in range(last):
+                scatter_z(zw1, 1, r, lo, hi)
+        scatter_z(zw1, 1, last, 0, C1)
+        second_product(zw1, 1)
+        ow = [window("ow%d" % c, "ow%d" % c if c < last else "after_quantize1") for c in range(K // P)]
         for c in range(K // P):
             scatter_dx(0, c)
         for c in range(K // P):

@@ -39,7 +39,7 @@ def tile_moe_hib_silu_kernel(tc, dy_words, dy_scales, wet_words, wet_scales, wgt
 
         dyw = [keep.tile([P, T], I32, name="dyw%d" % s, tag="after_words%d" % s, align_bytes=64) for s in range(PASSES)]
         dys = keep.tile([P, PASSES, T], U8, name="dys", tag="after_scales", align_bytes=64)
-        wet_first = keep.tile([P, PASSES, 2 * H], U8, name="wet_first", align_bytes=64)
+        wet_first = keep.tile([P, PASSES, 2 * H], U8, name="wet_first", tag="after_first_expert", align_bytes=64)
         wets = keep.tile([P, E * PASSES, H], U8, name="wets", align_bytes=64)
         gate_rows = keep.tile([P, P], F32, name="gate_rows", tag="after_gate", align_bytes=64)
         gate_col = keep.tile([P, T // P], F32, name="gate_col")
@@ -81,7 +81,6 @@ def tile_moe_hib_silu_kernel(tc, dy_words, dy_scales, wet_words, wet_scales, wgt
         wetw = [wet_first[:]] + [wet_rest[:, PASSES * e:PASSES * (e + 1), :] for e in range(E - 1)]
 
         gw = [keep.tile([P, T], U32, name="gw%d" % s, align_bytes=64) for s in range(PASSES)]
-        gs = keep.tile([P, PASSES, T], U8, name="gs", align_bytes=64)
         zs = [keep.tile([P, PACK, C1], F32, name="zs%d" % f) for f in range(G)]
 
         def gather_words(s, lo, hi):
@@ -116,21 +115,20 @@ def tile_moe_hib_silu_kernel(tc, dy_words, dy_scales, wet_words, wet_scales, wgt
             for b in (2 * e, 2 * e + 1):
                 turn(b, zts[b - 2 * e])
 
-        for s in range(PASSES):
-            gather_words(s, 0, C1)
+        gather_words(0, 0, C1)
+        gather_words(0, C1, T)
+        gather_words(1, 0, C1)
+        gs = keep.tile([P, PASSES, T], U8, name="gs", tag="after_words0", align_bytes=64)
         for lo, hi in ((0, P), (P, C1)):
             for s in range(PASSES):
                 gather_scales(s, lo, hi)
-        for s in range(PASSES):
-            gather_words(s, C1, T)
+        gather_words(1, C1, T)
         for s in range(PASSES):
             gather_scales(s, C1, T)
 
-        a_t.append(keep.tile([P, PACK, C1], F32, name="a1", tag="after_words0", align_bytes=64))
-        wgtw = keep.tile([P, G, 2 * K], U8, name="wgtw", tag="after_words1", align_bytes=64)
+        a_t.append(keep.tile([P, PACK, C1], F32, name="a1", tag="after_words1", align_bytes=64))
         wgts = keep.tile([P, G, K], U8, name="wgts", tag="after_scales", align_bytes=64)
         nc.sync.dma_start(a_t[1][:], a_rows[:, :, C1:2 * C1])
-        load_words(wgtw[:], wgt_words.rearrange("f s p c -> p (f s) c"))
         nc.gpsimd.memset(wgts[:].bitcast(I32), 0)
         load_scales(wgts, wgt_scales.rearrange("f s b k -> (f s) b k"), [nc.sync] * 4)
 
@@ -181,6 +179,8 @@ def tile_moe_hib_silu_kernel(tc, dy_words, dy_scales, wet_words, wet_scales, wgt
 
         last = PACK - 1
         expert(0)
+        wgtw = keep.tile([P, G, 2 * K], U8, name="wgtw", tag="after_first_expert", align_bytes=64)
+        load_words(wgtw[:], wgt_words.rearrange("f s p c -> p (f s) c"))
         expert(1)
         activations(0)
         derivative(0)

@@ -29,8 +29,8 @@ def tile_moe_hib_silu_kernel(tc, dy_words, dy_scales, wet_words, wet_scales, wgt
         lists = ctx.enter_context(tc.tile_pool(name="lists", bufs=1))
         keep = ctx.enter_context(tc.tile_pool(name="keep", bufs=1))
         ring = ctx.enter_context(tc.tile_pool(name="ring", bufs=4))
-        ps1 = ctx.enter_context(tc.psum_pool(name="ps1", bufs=3))
-        pst = ctx.enter_context(tc.psum_pool(name="pst", bufs=3))
+        ps1 = ctx.enter_context(tc.psum_pool(name="ps1", bufs=2))
+        pst = ctx.enter_context(tc.psum_pool(name="pst", bufs=4))
         ps2 = ctx.enter_context(tc.psum_pool(name="ps2", bufs=2))
 
         dst_t = lists.tile([P, T // LIST], U16, name="dst_t")
@@ -80,11 +80,14 @@ def tile_moe_hib_silu_kernel(tc, dy_words, dy_scales, wet_words, wet_scales, wgt
         load_words(wet_rest[:], wet_rows[:, PASSES:, :])
         wetw = [wet_first[:]] + [wet_rest[:, PASSES * e:PASSES * (e + 1), :] for e in range(E - 1)]
 
-        gw = [keep.tile([P, T], U32, name="gw%d" % s, align_bytes=64) for s in range(PASSES)]
+        gw = {}
         zs = [keep.tile([P, PACK, C1], F32, name="zs%d" % f) for f in range(G)]
 
         def gather_words(s, lo, hi):
-            nc.vector.tensor_copy(gw[s][:, lo:hi], dyw[s][:].bitcast(U32).indirect(dst_t[:, lo // LIST:hi // LIST]))
+            f = lo // C1
+            tag = "after_scales" if (s, f) == (1, 1) else "gw%d_%d" % (s, f)
+            gw[s, f] = keep.tile([P, C1], U32, name="gw%d_%d" % (s, f), tag=tag, align_bytes=64)
+            nc.vector.tensor_copy(gw[s, f][:], dyw[s][:].bitcast(U32).indirect(dst_t[:, lo // LIST:hi // LIST]))
 
         def gather_scales(s, lo, hi):
             nc.vector.tensor_copy(gs[:, s, lo:hi], dys[:, s, :].indirect(dst_t[:, lo // LIST:hi // LIST]))
@@ -96,7 +99,7 @@ def tile_moe_hib_silu_kernel(tc, dy_words, dy_scales, wet_words, wet_scales, wgt
             for s in range(PASSES):
                 nc.tensor.matmul_mx(
                     out=acc[:],
-                    lhsT=gw[s][:, cols].bitcast(FP8X4), lhsT_scale=gs[:, s, cols],
+                    lhsT=gw[s, b * P // C1][:, b * P % C1:b * P % C1 + P].bitcast(FP8X4), lhsT_scale=gs[:, s, cols],
                     rhs=wetw[e][:, s, :].bitcast(FP4X4), rhs_scale=wets[:, e * PASSES + s, :],
                     start=(s == 0), stop=(s == PASSES - 1))
             zt = ring.tile([P, PACK, P], F32, name="zt")
@@ -122,15 +125,12 @@ def tile_moe_hib_silu_kernel(tc, dy_words, dy_scales, wet_words, wet_scales, wgt
         for lo, hi in ((0, P), (P, C1)):
             for s in range(PASSES):
                 gather_scales(s, lo, hi)
-        gather_words(1, C1, T)
         for s in range(PASSES):
             gather_scales(s, C1, T)
+        gather_words(1, C1, T)
 
         a_t.append(keep.tile([P, PACK, C1], F32, name="a1", tag="after_words1", align_bytes=64))
-        wgts = keep.tile([P, G, K], U8, name="wgts", tag="after_scales", align_bytes=64)
         nc.sync.dma_start(a_t[1][:], a_rows[:, :, C1:2 * C1])
-        nc.gpsimd.memset(wgts[:].bitcast(I32), 0)
-        load_scales(wgts, wgt_scales.rearrange("f s b k -> (f s) b k"), [nc.sync] * 4)
 
         dxs = [keep.tile([P, K // P, C1], F32, name="dxs%d" % f) for f in range(G)]
 
@@ -186,6 +186,9 @@ def tile_moe_hib_silu_kernel(tc, dy_words, dy_scales, wet_words, wet_scales, wgt
         derivative(0)
         expert(2)
         expert(3)
+        wgts = keep.tile([P, G, K], U8, name="wgts", tag="after_scales", align_bytes=64)
+        nc.gpsimd.memset(wgts[:].bitcast(I32), 0)
+        load_scales(wgts, wgt_scales.rearrange("f s b k -> (f s) b k"), [nc.sync] * 4)
         activations(1)
         zw0 = [window("zw0_%d" % r, "zw0_%d" % r) for r in range(PACK)]
         for lo, hi in ((0, P), (P, C2), (C2, C1)):

@@ -1,7 +1,6 @@
 from contextlib import ExitStack
 
 import concourse.mybir as mybir
-from concourse.masks import make_identity
 
 K, T, G, C1, E, C2, H, N = 512, 1024, 2, 512, 4, 256, 512, 1024
 FLOPS = 2 * T * N * H + 2 * T * H * K
@@ -23,92 +22,126 @@ PASSES = N // (P * PACK)
 LIST = 16
 
 
+SPARE = 352
+PIECE = 64
+
+
 def tile_moe_hib_silu_kernel(tc, dy_words, dy_scales, wet_words, wet_scales, wgt_words, wgt_scales, a, gate, offs, offs2, dst, out):
     nc = tc.nc
     with ExitStack() as ctx:
         lists = ctx.enter_context(tc.tile_pool(name="lists", bufs=1))
         keep = ctx.enter_context(tc.tile_pool(name="keep", bufs=1))
-        ring = ctx.enter_context(tc.tile_pool(name="ring", bufs=4))
-        ps1 = ctx.enter_context(tc.psum_pool(name="ps1", bufs=2))
-        pst = ctx.enter_context(tc.psum_pool(name="pst", bufs=4))
-        ps2 = ctx.enter_context(tc.psum_pool(name="ps2", bufs=2))
+        reuse = ctx.enter_context(tc.tile_pool(name="reuse", bufs=1))
+        ps1 = ctx.enter_context(tc.psum_pool(name="ps1", bufs=1))
+        ps2 = ctx.enter_context(tc.psum_pool(name="ps2", bufs=4))
 
-        dst_t = lists.tile([P, T // LIST], U16, name="dst_t")
-        offs2_t = lists.tile([P, T // LIST], U16, name="offs2_t")
-        offs_t = lists.tile([P, T // LIST], U16, name="offs_t")
-
-        dyw = [keep.tile([P, T], I32, name="dyw%d" % s, tag="after_words%d" % s, align_bytes=64) for s in range(PASSES)]
-        dys = keep.tile([P, PASSES, T], U8, name="dys", tag="after_scales", align_bytes=64)
-        wet_first = keep.tile([P, PASSES, 2 * H], U8, name="wet_first", tag="after_first_expert", align_bytes=64)
-        wets = keep.tile([P, E * PASSES, H], U8, name="wets", align_bytes=64)
-        gate_rows = keep.tile([P, P], F32, name="gate_rows", tag="after_gate", align_bytes=64)
-        gate_col = keep.tile([P, T // P], F32, name="gate_col")
-        ident = keep.tile([P, P], F32, name="ident")
-        a_t = [keep.tile([P, PACK, C1], F32, name="a0")]
-        ds = [keep.tile([P, PACK, C1], F32, name="ds%d" % f) for f in range(G)]
-
-        nc.vector.memset(dys[:].bitcast(I32), 0)
-        nc.vector.memset(wets[:].bitcast(I32), 0)
-        make_identity(nc, ident[:])
+        def placed(shape, dtype, name, kib):
+            return reuse.tile(shape, dtype, name=name, offset=int(kib * 1024), align_bytes=64)
 
         def load_words(tile, words):
             nc.sync.dma_start(tile.bitcast(I32), words.bitcast(I32))
 
-        def load_scales(plane, scales, queues):
+        def load_scales(plane, scales):
             for q in range(4):
-                queues[q].dma_start(plane[32 * q:32 * q + 4].bitcast(I32), scales[:, 4 * q:4 * q + 4, :].rearrange("s b t -> b s t").bitcast(I32))
+                nc.sync.dma_start(plane[32 * q:32 * q + 4].bitcast(I32), scales[:, 4 * q:4 * q + 4, :].rearrange("s b t -> b s t").bitcast(I32))
 
         a_rows = a.rearrange("(p r) j -> p r j", r=PACK)
         wet_rows = wet_words.rearrange("e s p c -> p (e s) c")
-        side = (nc.scalar, nc.gpsimd, nc.scalar, nc.gpsimd)
-        load_words(dyw[0][:], dy_words[0].rearrange("p t d -> p (t d)"))
+
+        dst_t = lists.tile([P, T // LIST], U16, name="dst_t")
+        offs2_t = lists.tile([P, T // LIST], U16, name="offs2_t")
+        offs_t = lists.tile([P, T // LIST], U16, name="offs_t")
+        dyw0 = placed([P, T], I32, "dyw0", 8)
         nc.sync.dma_start(dst_t[:], dst)
-        load_words(dyw[1][:], dy_words[1].rearrange("p t d -> p (t d)"))
-        load_scales(dys, dy_scales, side)
-        load_scales(wets, wet_scales.rearrange("e s b i -> (e s) b i"), side)
-        nc.scalar.dma_start(gate_rows[:], gate[0:16, :].rearrange("c (b p) -> (c b) p", p=P))
-        load_words(wet_first[:], wet_rows[:, 0:PASSES, :])
-        nc.sync.dma_start(a_t[0][:], a_rows[:, :, 0:C1])
+        load_words(dyw0[:], dy_words[0].rearrange("p t d -> p (t d)"))
         nc.sync.dma_start(offs2_t[:], offs2)
         nc.sync.dma_start(offs_t[:], offs)
 
-        gate_ps = pst.tile([P, PACK, P], F32, name="turned")
-        nc.tensor.transpose(gate_ps[:, 0, :], gate_rows[:], ident[:])
-        nc.scalar.activation(gate_col[:], gate_ps[:, 0, 0:T // P], ACT.Copy)
+        dys = placed([P, T + SPARE], U8, "dys", 23.5)
+        zeros = placed([P, P], F32, "zeros", 2)
+        wsc = keep.tile([P, E * PASSES, H], U8, name="wsc", align_bytes=64)
+        gs = [keep.tile([P, T], U8, name="gs%d" % s, align_bytes=64) for s in range(PASSES)]
+        gate_rows = keep.tile([P, P], F32, name="gate_rows")
+        gate_col = keep.tile([P, T // P], F32, name="gate_col")
+        ident = keep.tile([P, P], F32, name="ident")
 
-        wet_rest = keep.tile([P, (E - 1) * PASSES, 2 * H], U8, name="wet_rest", tag="after_gate", align_bytes=64)
-        load_words(wet_rest[:], wet_rows[:, PASSES:, :])
-        wetw = [wet_first[:]] + [wet_rest[:, PASSES * e:PASSES * (e + 1), :] for e in range(E - 1)]
+        nc.gpsimd.memset(dys[:].bitcast(I32), 0)
+        nc.vector.memset(wsc[:].bitcast(I32), 0)
+        nc.vector.memset(gs[1][:].bitcast(I32), 0)
+        nc.gpsimd.memset(zeros[:], 0.0)
+        nc.gpsimd.affine_select(out=ident[:], in_=zeros[:], compare_op=ALU.not_equal, fill=1.0, base=0, pattern=[[-1, P]], channel_multiplier=1)
+        nc.gpsimd.memset(gate_rows[:], 0.0)
+
+        for q in range(4):
+            nc.sync.dma_start(dys[32 * q:32 * q + 8, 0:T].bitcast(I32), dy_scales[:, 4 * q:4 * q + 4, :].bitcast(I32))
+        dyw1 = placed([P, T], I32, "dyw1", 2.4375)
+        load_words(dyw1[:], dy_words[1].rearrange("p t d -> p (t d)"))
+        dyw = (dyw0, dyw1)
+        wet_first = placed([P, PASSES, 2 * H], U8, "wet_first", 0.0625)
+        load_words(wet_first[:], wet_rows[:, 0:PASSES, :])
+        a_piece = placed([P, PIECE], F32, "a_piece", 2.125)
+        nc.sync.dma_start(a_piece[:], a_rows[:, 0, 0:PIECE])
+        silu_piece = keep.tile([P, PIECE], F32, name="silu_piece")
+        nc.scalar.activation(silu_piece[:], a_piece[:], ACT.Silu, scale=-1.0)
+        nc.sync.dma_start(gate_rows[0:T // P, :], gate[0:1, :].rearrange("c (b p) -> (c b) p", p=P))
+        load_scales(wsc, wet_scales.rearrange("e s b i -> (e s) b i"))
+
+        gate_ps = ps2.tile([P, C1], F32, name="acc2")
+        nc.tensor.transpose(gate_ps[:, 0:P], gate_rows[:], ident[:])
+        nc.scalar.activation(gate_col[:], gate_ps[:, 0:T // P], ACT.Copy)
 
         gw = {}
+
+        def gather_words(s, lo, hi, tile):
+            gw[s, lo] = tile
+            nc.vector.tensor_copy(tile[:], dyw[s][:].bitcast(U32).indirect(dst_t[:, lo // LIST:hi // LIST]))
+
+        gather_words(0, 0, C2, keep.tile([P, C2], U32, name="gw0_first", align_bytes=64))
+        nc.vector.tensor_copy(gs[0][:], dys[:].indirect(dst_t[:]))
+        for q in range(4):
+            nc.sync.dma_start(gs[1][32 * q:32 * q + 4, :].bitcast(I32), gs[0][32 * q + 4:32 * q + 8, :].bitcast(I32))
+        gather_words(1, 0, C2, keep.tile([P, C2], U32, name="gw1_first", align_bytes=64))
+        gather_words(0, C2, T, placed([P, T - C2], U32, "gw0_rest", 20.5625))
+        gather_words(1, C2, T, keep.tile([P, T - C2], U32, name="gw1_rest", align_bytes=64))
+
+        a_t = [placed([P, PACK, C1], F32, "a0", 24.5625), placed([P, PACK, C1], F32, "a1", 11.5)]
+        nc.sync.dma_start(a_t[0][:], a_rows[:, :, 0:C1])
+        wet_second = placed([P, PASSES, 2 * H], U8, "wet_second", 7.125)
+        load_words(wet_second[:], wet_rows[:, PASSES:2 * PASSES, :])
+        nc.sync.dma_start(a_t[1][:], a_rows[:, :, C1:2 * C1])
+        wet_rest = placed([P, 2 * PASSES, 2 * H], U8, "wet_rest", 2.125)
+        load_words(wet_rest[:], wet_rows[:, 2 * PASSES:, :])
+        wets = (wet_first[:], wet_second[:], wet_rest[:, 0:PASSES, :], wet_rest[:, PASSES:, :])
+        wgtw = placed([P, G, 2 * K], U8, "wgtw", 9.125)
+        load_words(wgtw[:], wgt_words.rearrange("f s p c -> p (f s) c"))
+        wgts = placed([P, G, K], U8, "wgts", 6.125)
+        nc.gpsimd.memset(wgts[:].bitcast(I32), 0)
+        load_scales(wgts, wgt_scales.rearrange("f s b k -> (f s) b k"))
+
         zs = [keep.tile([P, PACK, C1], F32, name="zs%d" % f) for f in range(G)]
-
-        def gather_words(s, lo, hi):
-            f = lo // C1
-            tag = "after_scales" if (s, f) == (1, 1) else "gw%d_%d" % (s, f)
-            gw[s, f] = keep.tile([P, C1], U32, name="gw%d_%d" % (s, f), tag=tag, align_bytes=64)
-            nc.vector.tensor_copy(gw[s, f][:], dyw[s][:].bitcast(U32).indirect(dst_t[:, lo // LIST:hi // LIST]))
-
-        def gather_scales(s, lo, hi):
-            nc.vector.tensor_copy(gs[:, s, lo:hi], dys[:, s, :].indirect(dst_t[:, lo // LIST:hi // LIST]))
+        dxs = [keep.tile([P, K // P, C1], F32, name="dxs%d" % f) for f in range(G)]
+        zt_at = (34, 36, 46, 48)
 
         def first_product(b):
             e = b * P // C2
-            cols = slice(b * P, (b + 1) * P)
-            acc = ps1.tile([P, H], F32, name="acc")
+            lo = 0 if e == 0 else C2
+            acc = ps1.tile([P, H], F32, name="acc", tag="bank%d" % (b % 4))
             for s in range(PASSES):
                 nc.tensor.matmul_mx(
                     out=acc[:],
-                    lhsT=gw[s, b * P // C1][:, b * P % C1:b * P % C1 + P].bitcast(FP8X4), lhsT_scale=gs[:, s, cols],
-                    rhs=wetw[e][:, s, :].bitcast(FP4X4), rhs_scale=wets[:, e * PASSES + s, :],
+                    lhsT=gw[s, lo][:, b * P - lo:(b + 1) * P - lo].bitcast(FP8X4), lhsT_scale=gs[s][:, b * P:(b + 1) * P],
+                    rhs=wets[e][:, s, :].bitcast(FP4X4), rhs_scale=wsc[:, e * PASSES + s, :],
                     start=(s == 0), stop=(s == PASSES - 1))
-            zt = ring.tile([P, PACK, P], F32, name="zt")
-            nc.scalar.activation(zt[:], acc[:].rearrange("m (p r) -> m r p", r=PACK), ACT.Copy, scale=gate_col[:, b:b + 1])
+            if b < PACK:
+                zt = placed([P, PACK, P], F32, "zt%d" % b, zt_at[b])[:]
+            else:
+                zt = a_t[0][:, b - PACK, :].rearrange("m (r p) -> m r p", r=PACK)
+            nc.scalar.activation(zt, acc[:].rearrange("m (p r) -> m r p", r=PACK), ACT.Copy, scale=gate_col[:, b:b + 1])
             return zt
 
         def turn(b, zt):
             f, u = divmod(b * P, C1)
-            turned = pst.tile([P, PACK, P], F32, name="turned")
+            turned = ps1.tile([P, PACK, P], F32, name="turned", tag="bank%d" % ((b + 2) % 4))
             for r in range(PACK):
                 nc.tensor.transpose(turned[:, r, :], zt[:, r, :], ident[:])
             nc.scalar.activation(zs[f][:, :, u:u + P], turned[:], ACT.Copy)
@@ -118,49 +151,18 @@ def tile_moe_hib_silu_kernel(tc, dy_words, dy_scales, wet_words, wet_scales, wgt
             for b in (2 * e, 2 * e + 1):
                 turn(b, zts[b - 2 * e])
 
-        gather_words(0, 0, C1)
-        gather_words(0, C1, T)
-        gather_words(1, 0, C1)
-        gs = keep.tile([P, PASSES, T], U8, name="gs", tag="after_words0", align_bytes=64)
-        for lo, hi in ((0, P), (P, C1)):
-            for s in range(PASSES):
-                gather_scales(s, lo, hi)
-        for s in range(PASSES):
-            gather_scales(s, C1, T)
-        gather_words(1, C1, T)
-
-        a_t.append(keep.tile([P, PACK, C1], F32, name="a1", tag="after_words1", align_bytes=64))
-        nc.sync.dma_start(a_t[1][:], a_rows[:, :, C1:2 * C1])
-
-        dxs = [keep.tile([P, K // P, C1], F32, name="dxs%d" % f) for f in range(G)]
-
-        def activations(f):
-            funcs = ((ACT.Sigmoid, 1.0), (ACT.Silu, -1.0))
-            first, second = funcs if f == 0 else funcs[::-1]
-            for r in range(PACK):
-                nc.scalar.activation(ds[f][:, r, :], a_t[f][:, r, :], first[0], scale=first[1])
-            for r in range(PACK):
-                nc.scalar.activation(a_t[f][:, r, :], a_t[f][:, r, :], second[0], scale=second[1])
-
-        def derivative(f):
-            silu = a_t[f] if f == 0 else ds[f]
-            for r in range(PACK):
-                nc.gpsimd.tensor_scalar(silu[:, r, :], silu[:, r, :], -1.0, 1.0, ALU.mult, ALU.add)
-                nc.gpsimd.tensor_tensor(ds[f][:, r, :], ds[f][:, r, :], a_t[f][:, r, :], ALU.mult)
-
-        def window(name, tag):
-            return keep.tile([P, T], F32, name=name, tag=tag, align_bytes=64)
+        def one_minus(to, silu):
+            nc.gpsimd.tensor_scalar(to, silu, -1.0, 1.0, ALU.mult, ALU.add)
 
         def scatter_z(zw, f, r, lo, hi):
             ix = offs2_t[:, (f * C1 + lo) // LIST:(f * C1 + hi) // LIST]
             nc.vector.tensor_copy(zw[r][:].indirect(ix), zs[f][:, r, lo:hi])
 
-        def second_product(zw, f):
+        def second_product(zw, f, factors, grouped):
             planes = keep.tile([P, PACK, C1], BF16, name="planes%d" % f)
             for r in range(PACK):
-                nc.gpsimd.tensor_tensor(planes[:, r, :], zw[r][:, f * C1:(f + 1) * C1], ds[f][:, r, :], ALU.mult)
-            grouped = keep.tile([P, C1, PACK], BF16, name="grouped%d" % f, tag="after_quantize%d" % f, align_bytes=64)
-            nc.scalar.copy(grouped[:], planes[:].rearrange("p r j -> p j r"))
+                nc.gpsimd.tensor_tensor(planes[:, r, :], zw[r][:, f * C1:(f + 1) * C1], factors[:, r, :], ALU.mult)
+            nc.scalar.copy(grouped[:].rearrange("p (c i) r -> p c r i", i=4), planes[:].rearrange("p r (c i) -> p c r i", i=4))
             codes = keep.tile([P, C1], U32, name="codes%d" % f, align_bytes=64)
             scales = keep.tile([P, C1], U8, name="scales%d" % f, align_bytes=64)
             nc.vector.quantize_mx(out=codes[:].bitcast(FP8X4), scales=scales[:], in_=grouped[:].rearrange("p j r -> p (j r)"))
@@ -177,32 +179,53 @@ def tile_moe_hib_silu_kernel(tc, dy_words, dy_scales, wet_words, wet_scales, wgt
             ix = offs_t[:, f * C1 // LIST:(f + 1) * C1 // LIST]
             nc.vector.tensor_copy(ow[c][:].indirect(ix), dxs[f][:, c, :])
 
+        def flat(t):
+            return t.rearrange("p r j -> p (r j)")
+
         last = PACK - 1
+        halves = (slice(0, 2), slice(2, 4))
         expert(0)
-        wgtw = keep.tile([P, G, 2 * K], U8, name="wgtw", tag="after_first_expert", align_bytes=64)
-        load_words(wgtw[:], wgt_words.rearrange("f s p c -> p (f s) c"))
+        rest0 = placed([P, PACK, C1], F32, "rest0", 36)
+        nc.scalar.activation(flat(rest0[:, 0:2, :])[:, PIECE:], flat(a_t[0][:, 0:2, :])[:, PIECE:], ACT.Silu, scale=-1.0)
+        nc.scalar.activation(rest0[:, 2:4, :], a_t[0][:, 2:4, :], ACT.Silu, scale=-1.0)
+        one_minus(rest0[:, 0, 0:PIECE], silu_piece[:])
+        one_minus(flat(rest0[:])[:, PIECE:], flat(rest0[:])[:, PIECE:])
         expert(1)
-        activations(0)
-        derivative(0)
+        ds0 = placed([P, PACK, C1], F32, "ds0", 48)
+        for h in halves:
+            nc.scalar.activation(ds0[:, h, :], a_t[0][:, h, :], ACT.Sigmoid)
+            nc.gpsimd.tensor_tensor(ds0[:, h, :], ds0[:, h, :], rest0[:, h, :], ALU.mult)
         expert(2)
         expert(3)
-        wgts = keep.tile([P, G, K], U8, name="wgts", tag="after_scales", align_bytes=64)
-        nc.gpsimd.memset(wgts[:].bitcast(I32), 0)
-        load_scales(wgts, wgt_scales.rearrange("f s b k -> (f s) b k"), [nc.sync] * 4)
-        activations(1)
-        zw0 = [window("zw0_%d" % r, "zw0_%d" % r) for r in range(PACK)]
-        for lo, hi in ((0, P), (P, C2), (C2, C1)):
-            for r in range(PACK):
-                scatter_z(zw0, 0, r, lo, hi)
-        second_product(zw0, 0)
-        derivative(1)
-        zw1 = [window("zw1_%d" % r, "zw1_%d" % r if r < last else "after_quantize0") for r in range(PACK)]
-        for lo, hi in ((0, C2), (C2, C1)):
-            for r in range(last):
-                scatter_z(zw1, 1, r, lo, hi)
+        for h in halves:
+            nc.scalar.activation(a_t[0][:, h, :], a_t[1][:, h, :], ACT.Sigmoid)
+        rest1 = keep.tile([P, PACK, C1], F32, name="rest1")
+        nc.scalar.activation(rest1[:], a_t[1][:], ACT.Silu, scale=-1.0)
+
+        zw0 = [keep.tile([P, T], F32, name="zw0_%d" % r) for r in range(PACK)]
+        cuts = (P, C2, C2, C2)
+        for r in range(PACK):
+            scatter_z(zw0, 0, r, 0, cuts[r])
+        for r in range(PACK):
+            scatter_z(zw0, 0, r, cuts[r], C1)
+        grouped0 = placed([P, C1, PACK], BF16, "grouped0", 16.75)
+        second_product(zw0, 0, ds0, grouped0)
+
+        one_minus(rest1[:], rest1[:])
+        ds1 = placed([P, PACK, C1], F32, "ds1", 11.5)
+        nc.gpsimd.tensor_tensor(ds1[:], a_t[0][:], rest1[:], ALU.mult)
+
+        zw1 = [keep.tile([P, T], F32, name="zw1_%d" % r) for r in range(last)] + [placed([P, T], F32, "zw1_last", 20.5)]
+        for r in range(last - 1):
+            scatter_z(zw1, 1, r, 0, C2)
+        scatter_z(zw1, 1, last - 1, 0, C1)
+        for r in range(last - 1):
+            scatter_z(zw1, 1, r, C2, C1)
         scatter_z(zw1, 1, last, 0, C1)
-        second_product(zw1, 1)
-        ow = [window("ow%d" % c, "ow%d" % c if c < last else "after_quantize1") for c in range(K // P)]
+        grouped1 = keep.tile([P, C1, PACK], BF16, name="grouped1", tag="grouped1", align_bytes=64)
+        second_product(zw1, 1, ds1, grouped1)
+
+        ow = [keep.tile([P, T], F32, name="ow%d" % c, tag="ow%d" % c if c < last else "grouped1", align_bytes=64) for c in range(K // P)]
         for c in range(K // P):
             scatter_dx(0, c)
         for c in range(K // P):

@@ -23,7 +23,6 @@ LIST = 16
 
 
 SPARE = 352
-PIECE = 64
 
 
 def tile_moe_hib_silu_kernel(tc, dy_words, dy_scales, wet_words, wet_scales, wgt_words, wgt_scales, a, gate, offs, offs2, dst, out):
@@ -61,7 +60,7 @@ def tile_moe_hib_silu_kernel(tc, dy_words, dy_scales, wet_words, wet_scales, wgt
         zeros = placed([P, P], F32, "zeros", 2)
         wsc = keep.tile([P, E * PASSES, H], U8, name="wsc", align_bytes=64)
         gs = [keep.tile([P, T], U8, name="gs%d" % s, align_bytes=64) for s in range(PASSES)]
-        gate_rows = keep.tile([P, P], F32, name="gate_rows")
+        gate_rows = placed([P, P], F32, "gate_rows", 68)
         gate_col = keep.tile([P, T // P], F32, name="gate_col")
         ident = keep.tile([P, P], F32, name="ident")
 
@@ -79,10 +78,6 @@ def tile_moe_hib_silu_kernel(tc, dy_words, dy_scales, wet_words, wet_scales, wgt
         dyw = (dyw0, dyw1)
         wet_first = placed([P, PASSES, 2 * H], U8, "wet_first", 0.0625)
         load_words(wet_first[:], wet_rows[:, 0:PASSES, :])
-        a_piece = placed([P, PIECE], F32, "a_piece", 2.125)
-        nc.sync.dma_start(a_piece[:], a_rows[:, 0, 0:PIECE])
-        silu_piece = keep.tile([P, PIECE], F32, name="silu_piece")
-        nc.scalar.activation(silu_piece[:], a_piece[:], ACT.Silu, scale=-1.0)
         nc.sync.dma_start(gate_rows[0:T // P, :], gate[0:1, :].rearrange("c (b p) -> (c b) p", p=P))
         load_scales(wsc, wet_scales.rearrange("e s b i -> (e s) b i"))
 
@@ -90,6 +85,8 @@ def tile_moe_hib_silu_kernel(tc, dy_words, dy_scales, wet_words, wet_scales, wgt
         nc.tensor.transpose(gate_ps[:, 0:P], gate_rows[:], ident[:])
         nc.scalar.activation(gate_col[:], gate_ps[:, 0:T // P], ACT.Copy)
 
+        a0 = [placed([P, 2, C1], F32, "a0_first", 68), placed([P, 2, C1], F32, "a0_second", 7.125)]
+        nc.sync.dma_start(a0[0][:], a_rows[:, 0:2, 0:C1])
         gw = {}
 
         def gather_words(s, lo, hi, tile):
@@ -104,15 +101,15 @@ def tile_moe_hib_silu_kernel(tc, dy_words, dy_scales, wet_words, wet_scales, wgt
         gather_words(0, C2, T, placed([P, T - C2], U32, "gw0_rest", 20.5625))
         gather_words(1, C2, T, keep.tile([P, T - C2], U32, name="gw1_rest", align_bytes=64))
 
-        a_t = [placed([P, PACK, C1], F32, "a0", 24.5625), placed([P, PACK, C1], F32, "a1", 11.5)]
-        nc.sync.dma_start(a_t[0][:], a_rows[:, :, 0:C1])
-        wet_second = placed([P, PASSES, 2 * H], U8, "wet_second", 7.125)
+        a1 = placed([P, PACK, C1], F32, "a1", 11.5)
+        wet_second = placed([P, PASSES, 2 * H], U8, "wet_second", 24.5625)
         load_words(wet_second[:], wet_rows[:, PASSES:2 * PASSES, :])
-        nc.sync.dma_start(a_t[1][:], a_rows[:, :, C1:2 * C1])
+        nc.sync.dma_start(a0[1][:], a_rows[:, 2:4, 0:C1])
+        nc.sync.dma_start(a1[:], a_rows[:, :, C1:2 * C1])
         wet_rest = placed([P, 2 * PASSES, 2 * H], U8, "wet_rest", 2.125)
         load_words(wet_rest[:], wet_rows[:, 2 * PASSES:, :])
         wets = (wet_first[:], wet_second[:], wet_rest[:, 0:PASSES, :], wet_rest[:, PASSES:, :])
-        wgtw = placed([P, G, 2 * K], U8, "wgtw", 9.125)
+        wgtw = placed([P, G, 2 * K], U8, "wgtw", 0.0625)
         load_words(wgtw[:], wgt_words.rearrange("f s p c -> p (f s) c"))
         wgts = placed([P, G, K], U8, "wgts", 6.125)
         nc.gpsimd.memset(wgts[:].bitcast(I32), 0)
@@ -122,34 +119,45 @@ def tile_moe_hib_silu_kernel(tc, dy_words, dy_scales, wet_words, wet_scales, wgt
         dxs = [keep.tile([P, K // P, C1], F32, name="dxs%d" % f) for f in range(G)]
         zt_at = (34, 36, 46, 48)
 
-        def first_product(b):
-            e = b * P // C2
-            lo = 0 if e == 0 else C2
-            acc = ps1.tile([P, H], F32, name="acc", tag="bank%d" % (b % 4))
-            for s in range(PASSES):
-                nc.tensor.matmul_mx(
-                    out=acc[:],
-                    lhsT=gw[s, lo][:, b * P - lo:(b + 1) * P - lo].bitcast(FP8X4), lhsT_scale=gs[s][:, b * P:(b + 1) * P],
-                    rhs=wets[e][:, s, :].bitcast(FP4X4), rhs_scale=wsc[:, e * PASSES + s, :],
-                    start=(s == 0), stop=(s == PASSES - 1))
-            if b < PACK:
-                zt = placed([P, PACK, P], F32, "zt%d" % b, zt_at[b])[:]
-            else:
-                zt = a_t[0][:, b - PACK, :].rearrange("m (r p) -> m r p", r=PACK)
-            nc.scalar.activation(zt, acc[:].rearrange("m (p r) -> m r p", r=PACK), ACT.Copy, scale=gate_col[:, b:b + 1])
-            return zt
+        def weigh(b, acc, zt, planes):
+            nc.scalar.activation(zt[:, planes, :], acc[:].rearrange("m (p r) -> m r p", r=PACK)[:, planes, :], ACT.Copy, scale=gate_col[:, b:b + 1])
 
-        def turn(b, zt):
+        def turn(b, zt, planes, turned):
             f, u = divmod(b * P, C1)
-            turned = ps1.tile([P, PACK, P], F32, name="turned", tag="bank%d" % ((b + 2) % 4))
-            for r in range(PACK):
+            for r in range(planes.start, planes.stop):
                 nc.tensor.transpose(turned[:, r, :], zt[:, r, :], ident[:])
-            nc.scalar.activation(zs[f][:, :, u:u + P], turned[:], ACT.Copy)
+            nc.scalar.activation(zs[f][:, planes, u:u + P], turned[:, planes, :], ACT.Copy)
 
         def expert(e):
-            zts = [first_product(b) for b in (2 * e, 2 * e + 1)]
-            for b in (2 * e, 2 * e + 1):
-                turn(b, zts[b - 2 * e])
+            blocks = (2 * e, 2 * e + 1)
+            lo = 0 if e == 0 else C2
+            acc = {b: ps1.tile([P, H], F32, name="acc", tag="bank%d" % (e // 2 * 2 + b % 2)) for b in blocks}
+            for s in range(PASSES):
+                for b in blocks:
+                    nc.tensor.matmul_mx(
+                        out=acc[b][:],
+                        lhsT=gw[s, lo][:, b * P - lo:(b + 1) * P - lo].bitcast(FP8X4), lhsT_scale=gs[s][:, b * P:(b + 1) * P],
+                        rhs=wets[e][:, s, :].bitcast(FP4X4), rhs_scale=wsc[:, e * PASSES + s, :],
+                        start=(s == 0), stop=(s == PASSES - 1))
+            zt = {}
+            for b in blocks:
+                if b < PACK:
+                    zt[b] = placed([P, PACK, P], F32, "zt%d" % b, zt_at[b])[:]
+                else:
+                    zt[b] = a0[e - 2][:, b % 2, :].rearrange("m (r p) -> m r p", r=PACK)
+            whole = slice(0, PACK)
+            todo = {b: whole for b in blocks}
+            if e == 0:
+                todo[0] = slice(1, PACK)
+                lead = placed([P, 1, P], F32, "zt_lead", 36)[:]
+                weigh(0, acc[0], lead, slice(0, 1))
+                weigh(0, acc[0], zt[0], todo[0])
+                turn(0, lead, slice(0, 1), ps2.tile([P, PACK, P], F32, name="acc2"))
+            else:
+                weigh(blocks[0], acc[blocks[0]], zt[blocks[0]], whole)
+            weigh(blocks[1], acc[blocks[1]], zt[blocks[1]], whole)
+            for b in blocks:
+                turn(b, zt[b], todo[b], ps1.tile([P, PACK, P], F32, name="turned", tag="bank%d" % (2 - e // 2 * 2 + b % 2)))
 
         def one_minus(to, silu):
             nc.gpsimd.tensor_scalar(to, silu, -1.0, 1.0, ALU.mult, ALU.add)
@@ -179,41 +187,43 @@ def tile_moe_hib_silu_kernel(tc, dy_words, dy_scales, wet_words, wet_scales, wgt
             ix = offs_t[:, f * C1 // LIST:(f + 1) * C1 // LIST]
             nc.vector.tensor_copy(ow[c][:].indirect(ix), dxs[f][:, c, :])
 
-        def flat(t):
-            return t.rearrange("p r j -> p (r j)")
-
         last = PACK - 1
         halves = (slice(0, 2), slice(2, 4))
+        rest0 = [keep.tile([P, 2, C1], F32, name="rest0_first"), None]
+        nc.scalar.activation(rest0[0][:], a0[0][:], ACT.Silu, scale=-1.0)
+        one_minus(rest0[0][:], rest0[0][:])
         expert(0)
-        rest0 = placed([P, PACK, C1], F32, "rest0", 36)
-        nc.scalar.activation(flat(rest0[:, 0:2, :])[:, PIECE:], flat(a_t[0][:, 0:2, :])[:, PIECE:], ACT.Silu, scale=-1.0)
-        nc.scalar.activation(rest0[:, 2:4, :], a_t[0][:, 2:4, :], ACT.Silu, scale=-1.0)
-        one_minus(rest0[:, 0, 0:PIECE], silu_piece[:])
-        one_minus(flat(rest0[:])[:, PIECE:], flat(rest0[:])[:, PIECE:])
         expert(1)
-        ds0 = placed([P, PACK, C1], F32, "ds0", 48)
-        for h in halves:
-            nc.scalar.activation(ds0[:, h, :], a_t[0][:, h, :], ACT.Sigmoid)
-            nc.gpsimd.tensor_tensor(ds0[:, h, :], ds0[:, h, :], rest0[:, h, :], ALU.mult)
+        rest0[1] = placed([P, 2, C1], F32, "rest0_second", 45)
+        nc.scalar.activation(rest0[1][:], a0[1][:], ACT.Silu, scale=-1.0)
+        one_minus(rest0[1][:], rest0[1][:])
+        ds0 = placed([P, PACK, C1], F32, "ds0", 49)
+        for h in range(2):
+            nc.scalar.activation(ds0[:, halves[h], :], a0[h][:], ACT.Sigmoid)
+            nc.gpsimd.tensor_tensor(ds0[:, halves[h], :], ds0[:, halves[h], :], rest0[h][:], ALU.mult)
         expert(2)
         expert(3)
-        for h in halves:
-            nc.scalar.activation(a_t[0][:, h, :], a_t[1][:, h, :], ACT.Sigmoid)
+        for h in range(2):
+            nc.scalar.activation(a0[h][:], a1[:, halves[h], :], ACT.Sigmoid)
         rest1 = keep.tile([P, PACK, C1], F32, name="rest1")
-        nc.scalar.activation(rest1[:], a_t[1][:], ACT.Silu, scale=-1.0)
+        nc.scalar.activation(rest1[:], a1[:], ACT.Silu, scale=-1.0)
 
         zw0 = [keep.tile([P, T], F32, name="zw0_%d" % r) for r in range(PACK)]
-        cuts = (P, C2, C2, C2)
-        for r in range(PACK):
-            scatter_z(zw0, 0, r, 0, cuts[r])
-        for r in range(PACK):
-            scatter_z(zw0, 0, r, cuts[r], C1)
+        for r in range(last):
+            scatter_z(zw0, 0, r, 0, P)
+        scatter_z(zw0, 0, last, 0, C2)
+        scatter_z(zw0, 0, 0, P, C2)
+        scatter_z(zw0, 0, 1, P, C1)
+        scatter_z(zw0, 0, 0, C2, C1)
+        scatter_z(zw0, 0, 2, P, C1)
+        scatter_z(zw0, 0, last, C2, C1)
         grouped0 = placed([P, C1, PACK], BF16, "grouped0", 16.75)
         second_product(zw0, 0, ds0, grouped0)
 
         one_minus(rest1[:], rest1[:])
         ds1 = placed([P, PACK, C1], F32, "ds1", 11.5)
-        nc.gpsimd.tensor_tensor(ds1[:], a_t[0][:], rest1[:], ALU.mult)
+        for h in range(2):
+            nc.gpsimd.tensor_tensor(ds1[:, halves[h], :], a0[h][:], rest1[:, halves[h], :], ALU.mult)
 
         zw1 = [keep.tile([P, T], F32, name="zw1_%d" % r) for r in range(last)] + [placed([P, T], F32, "zw1_last", 20.5)]
         for r in range(last - 1):

@@ -50,14 +50,12 @@ def tile_moe_hib_silu_kernel(tc, dy_words, dy_scales, wet_words, wet_scales, wgt
         dst_t = lists.tile([P, T // LIST], U16, name="dst_t")
         offs2_t = lists.tile([P, T // LIST], U16, name="offs2_t")
         offs_t = lists.tile([P, T // LIST], U16, name="offs_t")
-        dyw0 = placed([P, T], I32, "dyw0", 8)
         nc.sync.dma_start(dst_t[:], dst)
-        load_words(dyw0[:], dy_words[0].rearrange("p t d -> p (t d)"))
         nc.sync.dma_start(offs2_t[:], offs2)
         nc.sync.dma_start(offs_t[:], offs)
 
         dys = placed([P, T + SPARE], U8, "dys", 23.5)
-        zeros = placed([P, P], F32, "zeros", 2)
+        zeros = placed([P, 576], F32, "zeros", 3.9375)
         wsc = keep.tile([P, E * PASSES, H], U8, name="wsc", align_bytes=64)
         gs = [keep.tile([P, T], U8, name="gs%d" % s, align_bytes=64) for s in range(PASSES)]
         gate_rows = placed([P, P], F32, "gate_rows", 68)
@@ -67,16 +65,16 @@ def tile_moe_hib_silu_kernel(tc, dy_words, dy_scales, wet_words, wet_scales, wgt
         nc.gpsimd.memset(dys[:].bitcast(I32), 0)
         nc.vector.memset(wsc[:].bitcast(I32), 0)
         nc.vector.memset(gs[1][:].bitcast(I32), 0)
-        nc.gpsimd.memset(zeros[:], 0.0)
-        nc.gpsimd.affine_select(out=ident[:], in_=zeros[:], compare_op=ALU.not_equal, fill=1.0, base=0, pattern=[[-1, P]], channel_multiplier=1)
+        nc.gpsimd.memset(zeros[:, 0:P], 0.0)
+        nc.gpsimd.affine_select(out=ident[:], in_=zeros[:, 0:P], compare_op=ALU.not_equal, fill=1.0, base=0, pattern=[[-1, P]], channel_multiplier=1)
         nc.gpsimd.memset(gate_rows[:], 0.0)
 
         for q in range(4):
             nc.sync.dma_start(dys[32 * q:32 * q + 8, 0:T].bitcast(I32), dy_scales[:, 4 * q:4 * q + 4, :].bitcast(I32))
-        dyw1 = placed([P, T], I32, "dyw1", 2.4375)
-        load_words(dyw1[:], dy_words[1].rearrange("p t d -> p (t d)"))
-        dyw = (dyw0, dyw1)
-        wet_first = placed([P, PASSES, 2 * H], U8, "wet_first", 0.0625)
+        dyw = [placed([P, T], I32, "dyw%d" % s, (6.125, 0)[s]) for s in range(PASSES)]
+        for s in range(PASSES):
+            load_words(dyw[s][:], dy_words[s].rearrange("p t d -> p (t d)"))
+        wet_first = placed([P, PASSES, 2 * H], U8, "wet_first", 4.0625)
         load_words(wet_first[:], wet_rows[:, 0:PASSES, :])
         nc.sync.dma_start(gate_rows[0:T // P, :], gate[0:1, :].rearrange("c (b p) -> (c b) p", p=P))
         load_scales(wsc, wet_scales.rearrange("e s b i -> (e s) b i"))
@@ -85,7 +83,7 @@ def tile_moe_hib_silu_kernel(tc, dy_words, dy_scales, wet_words, wet_scales, wgt
         nc.tensor.transpose(gate_ps[:, 0:P], gate_rows[:], ident[:])
         nc.scalar.activation(gate_col[:], gate_ps[:, 0:T // P], ACT.Copy)
 
-        a0 = [placed([P, 2, C1], F32, "a0_first", 68), placed([P, 2, C1], F32, "a0_second", 7.125)]
+        a0 = [placed([P, 2, C1], F32, "a0_first", 68), placed([P, 2, C1], F32, "a0_second", 6.0625)]
         nc.sync.dma_start(a0[0][:], a_rows[:, 0:2, 0:C1])
         gw = {}
 
@@ -93,25 +91,26 @@ def tile_moe_hib_silu_kernel(tc, dy_words, dy_scales, wet_words, wet_scales, wgt
             gw[s, lo] = tile
             nc.vector.tensor_copy(tile[:], dyw[s][:].bitcast(U32).indirect(dst_t[:, lo // LIST:hi // LIST]))
 
-        gather_words(0, 0, C2, keep.tile([P, C2], U32, name="gw0_first", align_bytes=64))
         nc.vector.tensor_copy(gs[0][:], dys[:].indirect(dst_t[:]))
         for q in range(4):
             nc.sync.dma_start(gs[1][32 * q:32 * q + 4, :].bitcast(I32), gs[0][32 * q + 4:32 * q + 8, :].bitcast(I32))
-        gather_words(1, 0, C2, keep.tile([P, C2], U32, name="gw1_first", align_bytes=64))
+        gather_words(0, 0, C2, placed([P, C2], U32, "gw0_first", 88))
+        gather_words(1, 0, C2, placed([P, C2], U32, "gw1_first", 76))
         gather_words(0, C2, T, placed([P, T - C2], U32, "gw0_rest", 20.5625))
         gather_words(1, C2, T, keep.tile([P, T - C2], U32, name="gw1_rest", align_bytes=64))
 
-        a1 = placed([P, PACK, C1], F32, "a1", 11.5)
+        a1 = [placed([P, 2, C1], F32, "a1_first", 10.0625), placed([P, 2, C1], F32, "a1_second", 76)]
         wet_second = placed([P, PASSES, 2 * H], U8, "wet_second", 24.5625)
         load_words(wet_second[:], wet_rows[:, PASSES:2 * PASSES, :])
         nc.sync.dma_start(a0[1][:], a_rows[:, 2:4, 0:C1])
-        nc.sync.dma_start(a1[:], a_rows[:, :, C1:2 * C1])
-        wet_rest = placed([P, 2 * PASSES, 2 * H], U8, "wet_rest", 2.125)
+        for h in range(2):
+            nc.sync.dma_start(a1[h][:], a_rows[:, 2 * h:2 * h + 2, C1:])
+        wet_rest = placed([P, 2 * PASSES, 2 * H], U8, "wet_rest", 0)
         load_words(wet_rest[:], wet_rows[:, 2 * PASSES:, :])
         wets = (wet_first[:], wet_second[:], wet_rest[:, 0:PASSES, :], wet_rest[:, PASSES:, :])
-        wgtw = placed([P, G, 2 * K], U8, "wgtw", 0.0625)
+        wgtw = placed([P, G, 2 * K], U8, "wgtw", 4.0625)
         load_words(wgtw[:], wgt_words.rearrange("f s p c -> p (f s) c"))
-        wgts = placed([P, G, K], U8, "wgts", 6.125)
+        wgts = placed([P, G, K], U8, "wgts", 88)
         nc.gpsimd.memset(wgts[:].bitcast(I32), 0)
         load_scales(wgts, wgt_scales.rearrange("f s b k -> (f s) b k"))
 
@@ -144,7 +143,7 @@ def tile_moe_hib_silu_kernel(tc, dy_words, dy_scales, wet_words, wet_scales, wgt
                 if b < PACK:
                     zt[b] = placed([P, PACK, P], F32, "zt%d" % b, zt_at[b])[:]
                 else:
-                    zt[b] = a0[e - 2][:, b % 2, :].rearrange("m (r p) -> m r p", r=PACK)
+                    zt[b] = a0[3 - e][:, b % 2, :].rearrange("m (r p) -> m r p", r=PACK)
             whole = slice(0, PACK)
             todo = {b: whole for b in blocks}
             if e == 0:
@@ -167,7 +166,7 @@ def tile_moe_hib_silu_kernel(tc, dy_words, dy_scales, wet_words, wet_scales, wgt
             nc.vector.tensor_copy(zw[r][:].indirect(ix), zs[f][:, r, lo:hi])
 
         def second_product(zw, f, factors, grouped):
-            planes = keep.tile([P, PACK, C1], BF16, name="planes%d" % f)
+            planes = keep.tile([P, PACK, C1], BF16, name="planes%d" % f, tag="planes%d" % f)
             for r in range(PACK):
                 nc.gpsimd.tensor_tensor(planes[:, r, :], zw[r][:, f * C1:(f + 1) * C1], factors[:, r, :], ALU.mult)
             nc.scalar.copy(grouped[:].rearrange("p (c i) r -> p c r i", i=4), planes[:].rearrange("p r (c i) -> p c r i", i=4))
@@ -183,9 +182,9 @@ def tile_moe_hib_silu_kernel(tc, dy_words, dy_scales, wet_words, wet_scales, wgt
                     start=True, stop=True)
                 nc.scalar.activation(dxs[f][:, c, :], acc2[:], ACT.Copy)
 
-        def scatter_dx(f, c):
-            ix = offs_t[:, f * C1 // LIST:(f + 1) * C1 // LIST]
-            nc.vector.tensor_copy(ow[c][:].indirect(ix), dxs[f][:, c, :])
+        def scatter_dx(f, c, lo, hi):
+            ix = offs_t[:, (f * C1 + lo) // LIST:(f * C1 + hi) // LIST]
+            nc.vector.tensor_copy(ow[c][:].indirect(ix), dxs[f][:, c, lo:hi])
 
         last = PACK - 1
         halves = (slice(0, 2), slice(2, 4))
@@ -203,10 +202,11 @@ def tile_moe_hib_silu_kernel(tc, dy_words, dy_scales, wet_words, wet_scales, wgt
             nc.gpsimd.tensor_tensor(ds0[:, halves[h], :], ds0[:, halves[h], :], rest0[h][:], ALU.mult)
         expert(2)
         expert(3)
-        for h in range(2):
-            nc.scalar.activation(a0[h][:], a1[:, halves[h], :], ACT.Sigmoid)
-        rest1 = keep.tile([P, PACK, C1], F32, name="rest1")
-        nc.scalar.activation(rest1[:], a1[:], ACT.Silu, scale=-1.0)
+        sig1 = [placed([P, 2, C1], F32, "sig1_first", 64.0625), a0[1]]
+        for h in (1, 0):
+            nc.scalar.activation(sig1[h][:], a1[h][:], ACT.Sigmoid)
+        rest1 = [placed([P, 2, C1], F32, "rest1_first", 71.9375), None]
+        nc.scalar.activation(rest1[0][:], a1[0][:], ACT.Silu, scale=-1.0)
 
         zw0 = [keep.tile([P, T], F32, name="zw0_%d" % r) for r in range(PACK)]
         for r in range(last):
@@ -217,15 +217,18 @@ def tile_moe_hib_silu_kernel(tc, dy_words, dy_scales, wet_words, wet_scales, wgt
         scatter_z(zw0, 0, 0, C2, C1)
         scatter_z(zw0, 0, 2, P, C1)
         scatter_z(zw0, 0, last, C2, C1)
-        grouped0 = placed([P, C1, PACK], BF16, "grouped0", 16.75)
+        grouped0 = placed([P, C1, PACK], BF16, "grouped0", 14)
         second_product(zw0, 0, ds0, grouped0)
 
-        one_minus(rest1[:], rest1[:])
-        ds1 = placed([P, PACK, C1], F32, "ds1", 11.5)
+        one_minus(rest1[0][:], rest1[0][:])
+        rest1[1] = keep.tile([P, 2, C1], F32, name="rest1_second", tag="planes0")
+        nc.scalar.activation(rest1[1][:], a1[1][:], ACT.Silu, scale=-1.0)
+        nc.scalar.activation(rest1[1][:], rest1[1][:], ACT.Copy, scale=-1.0, bias=1.0)
+        ds1 = placed([P, PACK, C1], F32, "ds1", 17.9375)
         for h in range(2):
-            nc.gpsimd.tensor_tensor(ds1[:, halves[h], :], a0[h][:], rest1[:, halves[h], :], ALU.mult)
+            nc.gpsimd.tensor_tensor(ds1[:, halves[h], :], sig1[h][:], rest1[h][:], ALU.mult)
 
-        zw1 = [keep.tile([P, T], F32, name="zw1_%d" % r) for r in range(last)] + [placed([P, T], F32, "zw1_last", 20.5)]
+        zw1 = [keep.tile([P, T], F32, name="zw1_%d" % r) for r in range(last)] + [placed([P, T], F32, "zw1_last", 10.0625)]
         for r in range(last - 1):
             scatter_z(zw1, 1, r, 0, C2)
         scatter_z(zw1, 1, last - 1, 0, C1)
@@ -237,7 +240,11 @@ def tile_moe_hib_silu_kernel(tc, dy_words, dy_scales, wet_words, wet_scales, wgt
 
         ow = [keep.tile([P, T], F32, name="ow%d" % c, tag="ow%d" % c if c < last else "grouped1", align_bytes=64) for c in range(K // P)]
         for c in range(K // P):
-            scatter_dx(0, c)
+            scatter_dx(0, c, 0, C1)
         for c in range(K // P):
-            scatter_dx(1, c)
-            nc.sync.dma_start(out[c * P:(c + 1) * P, :], ow[c][:])
+            scatter_dx(1, c, 0, C1)
+            if c < last:
+                nc.sync.dma_start(out[c * P:(c + 1) * P, :], ow[c][:])
+            else:
+                nc.sync.dma_start(out[c * P:(c + 1) * P, 0:C1], ow[c][:, 0:C1])
+                nc.scalar.dma_start(out[c * P:(c + 1) * P, C1:], ow[c][:, C1:])

@@ -18,11 +18,32 @@ ALU = mybir.AluOpType
 
 P = 128
 PACK = 4
+PAIR = 2
 PASSES = N // (P * PACK)
 LIST = 16
-
-
+QUADS = 4
 SPARE = 352
+RUN = 4
+
+KIB = 1024
+LAP = 64
+AT_SIG1 = 0
+AT_A0_FIRST = AT_SIG1 + 4 * KIB - LAP
+AT_GATE = AT_A0_FIRST + 4 * KIB - LAP
+AT_WORDS1 = AT_GATE + 4 * KIB
+AT_ZEROS = AT_WORDS1 + 4 * KIB - LAP
+AT_WET_FIRST = AT_ZEROS + KIB // 2 - LAP
+AT_A0_SECOND = AT_WET_FIRST + 2 * KIB
+AT_WORDS0 = AT_A0_SECOND + LAP
+AT_A1_FIRST = AT_A0_SECOND + 4 * KIB
+AT_GROUPED0 = AT_A1_FIRST + 4 * KIB - LAP
+AT_DS1 = AT_GROUPED0 + 4 * KIB - LAP
+AT_REST0 = AT_DS1 + 8 * KIB
+AT_ZT3 = AT_REST0 + 4 * KIB - LAP
+AT_DS0 = AT_ZT3 + 2 * KIB - LAP
+AT_GW0_REST = AT_DS0 + 8 * KIB
+AT_DY_SCALES = AT_GW0_REST + 3 * KIB - LAP
+AT_WET_SECOND = AT_DY_SCALES + KIB
 
 
 def tile_moe_hib_silu_kernel(tc, dy_words, dy_scales, wet_words, wet_scales, wgt_words, wgt_scales, a, gate, offs, offs2, dst, out):
@@ -30,93 +51,102 @@ def tile_moe_hib_silu_kernel(tc, dy_words, dy_scales, wet_words, wet_scales, wgt
     with ExitStack() as ctx:
         lists = ctx.enter_context(tc.tile_pool(name="lists", bufs=1))
         keep = ctx.enter_context(tc.tile_pool(name="keep", bufs=1))
-        reuse = ctx.enter_context(tc.tile_pool(name="reuse", bufs=1))
+        chain = ctx.enter_context(tc.tile_pool(name="chain", bufs=1))
         ps1 = ctx.enter_context(tc.psum_pool(name="ps1", bufs=1))
         ps2 = ctx.enter_context(tc.psum_pool(name="ps2", bufs=4))
 
-        def placed(shape, dtype, name, kib):
-            return reuse.tile(shape, dtype, name=name, offset=int(kib * 1024), align_bytes=64)
+        def placed(shape, dtype, name, at):
+            return chain.tile(shape, dtype, name=name, offset=at, align_bytes=64)
+
+        def kept(shape, dtype, name, tag=None):
+            return keep.tile(shape, dtype, name=name, tag=tag or name, align_bytes=64)
 
         def load_words(tile, words):
             nc.sync.dma_start(tile.bitcast(I32), words.bitcast(I32))
 
-        def load_scales(plane, scales):
-            for q in range(4):
-                nc.sync.dma_start(plane[32 * q:32 * q + 4].bitcast(I32), scales[:, 4 * q:4 * q + 4, :].rearrange("s b t -> b s t").bitcast(I32))
+        def load_scales(tile, scales):
+            for q in range(QUADS):
+                nc.sync.dma_start(tile[32 * q:32 * q + 4].bitcast(I32), scales[:, 4 * q:4 * q + 4, :].rearrange("s b t -> b s t").bitcast(I32))
+
+        def columns(lo, hi):
+            return slice(lo // LIST, hi // LIST)
 
         a_rows = a.rearrange("(p r) j -> p r j", r=PACK)
         wet_rows = wet_words.rearrange("e s p c -> p (e s) c")
+        pairs = [slice(PAIR * h, PAIR * (h + 1)) for h in range(PACK // PAIR)]
+        last = PACK - 1
 
         dst_t = lists.tile([P, T // LIST], U16, name="dst_t")
         offs2_t = lists.tile([P, T // LIST], U16, name="offs2_t")
         offs_t = lists.tile([P, T // LIST], U16, name="offs_t")
+        dyw = [placed([P, T], I32, "dyw%d" % s, (AT_WORDS0, AT_WORDS1)[s]) for s in range(PASSES)]
         nc.sync.dma_start(dst_t[:], dst)
+        load_words(dyw[0][:], dy_words[0].rearrange("p t d -> p (t d)"))
         nc.sync.dma_start(offs2_t[:], offs2)
         nc.sync.dma_start(offs_t[:], offs)
 
-        dys = placed([P, T + SPARE], U8, "dys", 23.5)
-        zeros = placed([P, 576], F32, "zeros", 3.9375)
-        wsc = keep.tile([P, E * PASSES, H], U8, name="wsc", align_bytes=64)
-        gs = [keep.tile([P, T], U8, name="gs%d" % s, align_bytes=64) for s in range(PASSES)]
-        gate_rows = placed([P, P], F32, "gate_rows", 68)
-        gate_col = keep.tile([P, T // P], F32, name="gate_col")
-        ident = keep.tile([P, P], F32, name="ident")
-
+        dys = placed([P, T + SPARE], U8, "dys", AT_DY_SCALES)
+        zeros = placed([P, P], F32, "zeros", AT_ZEROS)
+        ident = kept([P, P], F32, "ident")
+        gate_rows = placed([P, P], F32, "gate_rows", AT_GATE)
+        wet_sc = kept([P, E * PASSES, H], U8, "wet_sc")
+        gs = [kept([P, T], U8, "gs%d" % s) for s in range(PASSES)]
         nc.gpsimd.memset(dys[:].bitcast(I32), 0)
-        nc.vector.memset(wsc[:].bitcast(I32), 0)
+        nc.vector.memset(wet_sc[:].bitcast(I32), 0)
         nc.vector.memset(gs[1][:].bitcast(I32), 0)
-        nc.gpsimd.memset(zeros[:, 0:P], 0.0)
-        nc.gpsimd.affine_select(out=ident[:], in_=zeros[:, 0:P], compare_op=ALU.not_equal, fill=1.0, base=0, pattern=[[-1, P]], channel_multiplier=1)
+        nc.gpsimd.memset(zeros[:], 0.0)
+        nc.gpsimd.affine_select(out=ident[:], in_=zeros[:], compare_op=ALU.not_equal, fill=1.0, base=0, pattern=[[-1, P]], channel_multiplier=1)
         nc.gpsimd.memset(gate_rows[:], 0.0)
 
-        for q in range(4):
+        for q in range(QUADS):
             nc.sync.dma_start(dys[32 * q:32 * q + 8, 0:T].bitcast(I32), dy_scales[:, 4 * q:4 * q + 4, :].bitcast(I32))
-        dyw = [placed([P, T], I32, "dyw%d" % s, (6.125, 0)[s]) for s in range(PASSES)]
-        for s in range(PASSES):
-            load_words(dyw[s][:], dy_words[s].rearrange("p t d -> p (t d)"))
-        wet_first = placed([P, PASSES, 2 * H], U8, "wet_first", 4.0625)
+        load_words(dyw[1][:], dy_words[1].rearrange("p t d -> p (t d)"))
+        wet_first = placed([P, PASSES, 2 * H], U8, "wet_first", AT_WET_FIRST)
         load_words(wet_first[:], wet_rows[:, 0:PASSES, :])
         nc.sync.dma_start(gate_rows[0:T // P, :], gate[0:1, :].rearrange("c (b p) -> (c b) p", p=P))
-        load_scales(wsc, wet_scales.rearrange("e s b i -> (e s) b i"))
+        load_scales(wet_sc, wet_scales.rearrange("e s b i -> (e s) b i"))
 
+        gate_col = kept([P, T // P], F32, "gate_col")
         gate_ps = ps2.tile([P, C1], F32, name="acc2")
         nc.tensor.transpose(gate_ps[:, 0:P], gate_rows[:], ident[:])
         nc.scalar.activation(gate_col[:], gate_ps[:, 0:T // P], ACT.Copy)
 
-        a0 = [placed([P, 2, C1], F32, "a0_first", 68), placed([P, 2, C1], F32, "a0_second", 6.0625)]
-        nc.sync.dma_start(a0[0][:], a_rows[:, 0:2, 0:C1])
+        a0 = [placed([P, PAIR, C1], F32, "a0_first", AT_A0_FIRST), placed([P, PAIR, C1], F32, "a0_second", AT_A0_SECOND)]
+        nc.sync.dma_start(a0[0][:], a_rows[:, pairs[0], 0:C1])
+
         gw = {}
 
         def gather_words(s, lo, hi, tile):
             gw[s, lo] = tile
-            nc.vector.tensor_copy(tile[:], dyw[s][:].bitcast(U32).indirect(dst_t[:, lo // LIST:hi // LIST]))
+            nc.vector.tensor_copy(tile[:], dyw[s][:].bitcast(U32).indirect(dst_t[:, columns(lo, hi)]))
+
+        gather_words(0, 0, C2, kept([P, C2], U32, "gw0_first"))
 
         nc.vector.tensor_copy(gs[0][:], dys[:].indirect(dst_t[:]))
-        for q in range(4):
+        for q in range(QUADS):
             nc.sync.dma_start(gs[1][32 * q:32 * q + 4, :].bitcast(I32), gs[0][32 * q + 4:32 * q + 8, :].bitcast(I32))
-        gather_words(0, 0, C2, placed([P, C2], U32, "gw0_first", 88))
-        gather_words(1, 0, C2, placed([P, C2], U32, "gw1_first", 76))
-        gather_words(0, C2, T, placed([P, T - C2], U32, "gw0_rest", 20.5625))
-        gather_words(1, C2, T, keep.tile([P, T - C2], U32, name="gw1_rest", align_bytes=64))
 
-        a1 = [placed([P, 2, C1], F32, "a1_first", 10.0625), placed([P, 2, C1], F32, "a1_second", 76)]
-        wet_second = placed([P, PASSES, 2 * H], U8, "wet_second", 24.5625)
+        gather_words(1, 0, C2, kept([P, C2], U32, "gw1_first"))
+        gather_words(0, C2, T, placed([P, T - C2], U32, "gw0_rest", AT_GW0_REST))
+        gather_words(1, C2, T, kept([P, T - C2], U32, "gw1_rest"))
+
+        wet_second = placed([P, PASSES, 2 * H], U8, "wet_second", AT_WET_SECOND)
         load_words(wet_second[:], wet_rows[:, PASSES:2 * PASSES, :])
-        nc.sync.dma_start(a0[1][:], a_rows[:, 2:4, 0:C1])
+        nc.sync.dma_start(a0[1][:], a_rows[:, pairs[1], 0:C1])
+        a1 = [placed([P, PAIR, C1], F32, "a1_first", AT_A1_FIRST), kept([P, PAIR, C1], F32, "a1_second", "gw1_first")]
         for h in range(2):
-            nc.sync.dma_start(a1[h][:], a_rows[:, 2 * h:2 * h + 2, C1:])
-        wet_rest = placed([P, 2 * PASSES, 2 * H], U8, "wet_rest", 0)
+            nc.sync.dma_start(a1[h][:], a_rows[:, pairs[h], C1:])
+        wet_rest = placed([P, 2 * PASSES, 2 * H], U8, "wet_rest", AT_WORDS1)
         load_words(wet_rest[:], wet_rows[:, 2 * PASSES:, :])
-        wets = (wet_first[:], wet_second[:], wet_rest[:, 0:PASSES, :], wet_rest[:, PASSES:, :])
-        wgtw = placed([P, G, 2 * K], U8, "wgtw", 4.0625)
-        load_words(wgtw[:], wgt_words.rearrange("f s p c -> p (f s) c"))
-        wgts = placed([P, G, K], U8, "wgts", 88)
-        nc.gpsimd.memset(wgts[:].bitcast(I32), 0)
-        load_scales(wgts, wgt_scales.rearrange("f s b k -> (f s) b k"))
+        wet = (wet_first[:], wet_second[:], wet_rest[:, 0:PASSES, :], wet_rest[:, PASSES:, :])
+        wgt = placed([P, G, 2 * K], U8, "wgt", AT_WET_FIRST)
+        load_words(wgt[:], wgt_words.rearrange("f s p c -> p (f s) c"))
+        wgt_sc = kept([P, G, K], U8, "wgt_sc", "gw0_first")
+        nc.gpsimd.memset(wgt_sc[:].bitcast(I32), 0)
+        load_scales(wgt_sc, wgt_scales.rearrange("f s b k -> (f s) b k"))
 
-        zs = [keep.tile([P, PACK, C1], F32, name="zs%d" % f) for f in range(G)]
-        dxs = [keep.tile([P, K // P, C1], F32, name="dxs%d" % f) for f in range(G)]
-        zt_at = (34, 36, 46, 48)
+        zs = [kept([P, PACK, C1], F32, "zs%d" % f) for f in range(G)]
+        dxs = [kept([P, K // P, C1], F32, "dxs%d" % f) for f in range(G)]
 
         def weigh(b, acc, zt, planes):
             nc.scalar.activation(zt[:, planes, :], acc[:].rearrange("m (p r) -> m r p", r=PACK)[:, planes, :], ACT.Copy, scale=gate_col[:, b:b + 1])
@@ -127,88 +157,82 @@ def tile_moe_hib_silu_kernel(tc, dy_words, dy_scales, wet_words, wet_scales, wgt
                 nc.tensor.transpose(turned[:, r, :], zt[:, r, :], ident[:])
             nc.scalar.activation(zs[f][:, planes, u:u + P], turned[:, planes, :], ACT.Copy)
 
-        def expert(e):
+        def expert(e, zt, lead=None):
             blocks = (2 * e, 2 * e + 1)
+            f = e // 2
             lo = 0 if e == 0 else C2
-            acc = {b: ps1.tile([P, H], F32, name="acc", tag="bank%d" % (e // 2 * 2 + b % 2)) for b in blocks}
+            acc = [ps1.tile([P, H], F32, name="acc", tag="bank%d" % (2 * f + n)) for n in range(2)]
             for s in range(PASSES):
-                for b in blocks:
+                for n, b in enumerate(blocks):
                     nc.tensor.matmul_mx(
-                        out=acc[b][:],
+                        out=acc[n][:],
                         lhsT=gw[s, lo][:, b * P - lo:(b + 1) * P - lo].bitcast(FP8X4), lhsT_scale=gs[s][:, b * P:(b + 1) * P],
-                        rhs=wets[e][:, s, :].bitcast(FP4X4), rhs_scale=wsc[:, e * PASSES + s, :],
+                        rhs=wet[e][:, s, :].bitcast(FP4X4), rhs_scale=wet_sc[:, e * PASSES + s, :],
                         start=(s == 0), stop=(s == PASSES - 1))
-            zt = {}
-            for b in blocks:
-                if b < PACK:
-                    zt[b] = placed([P, PACK, P], F32, "zt%d" % b, zt_at[b])[:]
-                else:
-                    zt[b] = a0[3 - e][:, b % 2, :].rearrange("m (r p) -> m r p", r=PACK)
-            whole = slice(0, PACK)
-            todo = {b: whole for b in blocks}
-            if e == 0:
-                todo[0] = slice(1, PACK)
-                lead = placed([P, 1, P], F32, "zt_lead", 36)[:]
-                weigh(0, acc[0], lead, slice(0, 1))
-                weigh(0, acc[0], zt[0], todo[0])
-                turn(0, lead, slice(0, 1), ps2.tile([P, PACK, P], F32, name="acc2"))
-            else:
-                weigh(blocks[0], acc[blocks[0]], zt[blocks[0]], whole)
-            weigh(blocks[1], acc[blocks[1]], zt[blocks[1]], whole)
-            for b in blocks:
-                turn(b, zt[b], todo[b], ps1.tile([P, PACK, P], F32, name="turned", tag="bank%d" % (2 - e // 2 * 2 + b % 2)))
+            planes = [slice(0 if lead is None else 1, PACK), slice(0, PACK)]
+            if lead is not None:
+                weigh(blocks[0], acc[0], lead, slice(0, 1))
+            weigh(blocks[0], acc[0], zt[0], planes[0])
+            if lead is not None:
+                turn(blocks[0], lead, slice(0, 1), ps2.tile([P, PACK, P], F32, name="acc2"))
+            weigh(blocks[1], acc[1], zt[1], planes[1])
+            for n, b in enumerate(blocks):
+                turn(b, zt[n], planes[n], ps1.tile([P, PACK, P], F32, name="turned", tag="bank%d" % (2 * (1 - f) + n)))
 
-        def one_minus(to, silu):
-            nc.gpsimd.tensor_scalar(to, silu, -1.0, 1.0, ALU.mult, ALU.add)
+        def in_dead_a(tile):
+            return [tile[:, n, :].rearrange("m (r p) -> m r p", r=PACK) for n in range(2)]
+
+        def silu_of_minus(to, a_pair):
+            nc.scalar.activation(to[:], a_pair[:], ACT.Silu, scale=-1.0)
+
+        def one_minus(t):
+            nc.gpsimd.tensor_scalar(t[:], t[:], -1.0, 1.0, ALU.mult, ALU.add)
 
         def scatter_z(zw, f, r, lo, hi):
-            ix = offs2_t[:, (f * C1 + lo) // LIST:(f * C1 + hi) // LIST]
-            nc.vector.tensor_copy(zw[r][:].indirect(ix), zs[f][:, r, lo:hi])
+            nc.vector.tensor_copy(zw[r][:].indirect(offs2_t[:, columns(f * C1 + lo, f * C1 + hi)]), zs[f][:, r, lo:hi])
 
-        def second_product(zw, f, factors, grouped):
-            planes = keep.tile([P, PACK, C1], BF16, name="planes%d" % f, tag="planes%d" % f)
+        def second_product(zw, f, ds, grouped):
+            planes = kept([P, PACK, C1], BF16, "planes%d" % f)
             for r in range(PACK):
-                nc.gpsimd.tensor_tensor(planes[:, r, :], zw[r][:, f * C1:(f + 1) * C1], factors[:, r, :], ALU.mult)
-            nc.scalar.copy(grouped[:].rearrange("p (c i) r -> p c r i", i=4), planes[:].rearrange("p r (c i) -> p c r i", i=4))
-            codes = keep.tile([P, C1], U32, name="codes%d" % f, align_bytes=64)
-            scales = keep.tile([P, C1], U8, name="scales%d" % f, align_bytes=64)
+                nc.gpsimd.tensor_tensor(planes[:, r, :], zw[r][:, f * C1:(f + 1) * C1], ds[:, r, :], ALU.mult)
+            nc.scalar.copy(grouped[:].rearrange("p (c i) r -> p c r i", i=RUN), planes[:].rearrange("p r (c i) -> p c r i", i=RUN))
+            codes = kept([P, C1], U32, "codes%d" % f)
+            scales = kept([P, C1], U8, "scales%d" % f)
             nc.vector.quantize_mx(out=codes[:].bitcast(FP8X4), scales=scales[:], in_=grouped[:].rearrange("p j r -> p (j r)"))
             for c in range(K // P):
                 acc2 = ps2.tile([P, C1], F32, name="acc2")
                 nc.tensor.matmul_mx(
                     out=acc2[:],
-                    lhsT=wgtw[:, f, 2 * P * c:2 * P * (c + 1)].bitcast(FP4X4), lhsT_scale=wgts[:, f, P * c:P * (c + 1)],
+                    lhsT=wgt[:, f, 2 * P * c:2 * P * (c + 1)].bitcast(FP4X4), lhsT_scale=wgt_sc[:, f, P * c:P * (c + 1)],
                     rhs=codes[:].bitcast(FP8X4), rhs_scale=scales[:],
                     start=True, stop=True)
                 nc.scalar.activation(dxs[f][:, c, :], acc2[:], ACT.Copy)
 
-        def scatter_dx(f, c, lo, hi):
-            ix = offs_t[:, (f * C1 + lo) // LIST:(f * C1 + hi) // LIST]
-            nc.vector.tensor_copy(ow[c][:].indirect(ix), dxs[f][:, c, lo:hi])
+        def scatter_dx(ow, f, c):
+            nc.vector.tensor_copy(ow[c][:].indirect(offs_t[:, columns(f * C1, (f + 1) * C1)]), dxs[f][:, c, :])
 
-        last = PACK - 1
-        halves = (slice(0, 2), slice(2, 4))
-        rest0 = [keep.tile([P, 2, C1], F32, name="rest0_first"), None]
-        nc.scalar.activation(rest0[0][:], a0[0][:], ACT.Silu, scale=-1.0)
-        one_minus(rest0[0][:], rest0[0][:])
-        expert(0)
-        expert(1)
-        rest0[1] = placed([P, 2, C1], F32, "rest0_second", 45)
-        nc.scalar.activation(rest0[1][:], a0[1][:], ACT.Silu, scale=-1.0)
-        one_minus(rest0[1][:], rest0[1][:])
-        ds0 = placed([P, PACK, C1], F32, "ds0", 49)
+        rest0 = [kept([P, PAIR, C1], F32, "rest0_first")]
+        silu_of_minus(rest0[0], a0[0])
+        one_minus(rest0[0])
+        lead = kept([P, 1, P], F32, "lead", "after_lead")
+        expert(0, [kept([P, PACK, P], F32, "zt0"), kept([P, PACK, P], F32, "zt1", "after_lead")], lead)
+        expert(1, [kept([P, PACK, P], F32, "zt2"), placed([P, PACK, P], F32, "zt3", AT_ZT3)])
+        rest0.append(placed([P, PAIR, C1], F32, "rest0_second", AT_REST0))
+        silu_of_minus(rest0[1], a0[1])
+        one_minus(rest0[1])
+        ds0 = placed([P, PACK, C1], F32, "ds0", AT_DS0)
         for h in range(2):
-            nc.scalar.activation(ds0[:, halves[h], :], a0[h][:], ACT.Sigmoid)
-            nc.gpsimd.tensor_tensor(ds0[:, halves[h], :], ds0[:, halves[h], :], rest0[h][:], ALU.mult)
-        expert(2)
-        expert(3)
-        sig1 = [placed([P, 2, C1], F32, "sig1_first", 64.0625), a0[1]]
+            nc.scalar.activation(ds0[:, pairs[h], :], a0[h][:], ACT.Sigmoid)
+            nc.gpsimd.tensor_tensor(ds0[:, pairs[h], :], ds0[:, pairs[h], :], rest0[h][:], ALU.mult)
+        expert(2, in_dead_a(a0[1]))
+        expert(3, in_dead_a(a0[0]))
+        sig1 = [placed([P, PAIR, C1], F32, "sig1_first", AT_SIG1), a0[1]]
         for h in (1, 0):
             nc.scalar.activation(sig1[h][:], a1[h][:], ACT.Sigmoid)
-        rest1 = [placed([P, 2, C1], F32, "rest1_first", 71.9375), None]
-        nc.scalar.activation(rest1[0][:], a1[0][:], ACT.Silu, scale=-1.0)
+        rest1 = [placed([P, PAIR, C1], F32, "rest1_first", AT_GATE)]
+        silu_of_minus(rest1[0], a1[0])
 
-        zw0 = [keep.tile([P, T], F32, name="zw0_%d" % r) for r in range(PACK)]
+        zw0 = [kept([P, T], F32, "zw0_%d" % r) for r in range(PACK)]
         for r in range(last):
             scatter_z(zw0, 0, r, 0, P)
         scatter_z(zw0, 0, last, 0, C2)
@@ -217,34 +241,32 @@ def tile_moe_hib_silu_kernel(tc, dy_words, dy_scales, wet_words, wet_scales, wgt
         scatter_z(zw0, 0, 0, C2, C1)
         scatter_z(zw0, 0, 2, P, C1)
         scatter_z(zw0, 0, last, C2, C1)
-        grouped0 = placed([P, C1, PACK], BF16, "grouped0", 14)
+        grouped0 = placed([P, C1, PACK], BF16, "grouped0", AT_GROUPED0)
         second_product(zw0, 0, ds0, grouped0)
 
-        one_minus(rest1[0][:], rest1[0][:])
-        rest1[1] = keep.tile([P, 2, C1], F32, name="rest1_second", tag="planes0")
-        nc.scalar.activation(rest1[1][:], a1[1][:], ACT.Silu, scale=-1.0)
+        one_minus(rest1[0])
+        rest1.append(kept([P, PAIR, C1], F32, "rest1_second", "planes0"))
+        silu_of_minus(rest1[1], a1[1])
         nc.scalar.activation(rest1[1][:], rest1[1][:], ACT.Copy, scale=-1.0, bias=1.0)
-        ds1 = placed([P, PACK, C1], F32, "ds1", 17.9375)
+        ds1 = placed([P, PACK, C1], F32, "ds1", AT_DS1)
         for h in range(2):
-            nc.gpsimd.tensor_tensor(ds1[:, halves[h], :], sig1[h][:], rest1[h][:], ALU.mult)
+            nc.gpsimd.tensor_tensor(ds1[:, pairs[h], :], sig1[h][:], rest1[h][:], ALU.mult)
 
-        zw1 = [keep.tile([P, T], F32, name="zw1_%d" % r) for r in range(last)] + [placed([P, T], F32, "zw1_last", 10.0625)]
-        for r in range(last - 1):
+        zw1 = [kept([P, T], F32, "zw1_%d" % r) for r in range(last)] + [placed([P, T], F32, "zw1_last", AT_A1_FIRST)]
+        for r in range(2):
             scatter_z(zw1, 1, r, 0, C2)
-        scatter_z(zw1, 1, last - 1, 0, C1)
-        for r in range(last - 1):
+        scatter_z(zw1, 1, 2, 0, C1)
+        for r in range(2):
             scatter_z(zw1, 1, r, C2, C1)
         scatter_z(zw1, 1, last, 0, C1)
-        grouped1 = keep.tile([P, C1, PACK], BF16, name="grouped1", tag="grouped1", align_bytes=64)
-        second_product(zw1, 1, ds1, grouped1)
+        second_product(zw1, 1, ds1, kept([P, C1, PACK], BF16, "grouped1"))
 
-        ow = [keep.tile([P, T], F32, name="ow%d" % c, tag="ow%d" % c if c < last else "grouped1", align_bytes=64) for c in range(K // P)]
+        ow = [kept([P, T], F32, "ow%d" % c, "grouped1" if c == last else None) for c in range(K // P)]
         for c in range(K // P):
-            scatter_dx(0, c, 0, C1)
-        for c in range(K // P):
-            scatter_dx(1, c, 0, C1)
-            if c < last:
-                nc.sync.dma_start(out[c * P:(c + 1) * P, :], ow[c][:])
-            else:
-                nc.sync.dma_start(out[c * P:(c + 1) * P, 0:C1], ow[c][:, 0:C1])
-                nc.scalar.dma_start(out[c * P:(c + 1) * P, C1:], ow[c][:, C1:])
+            scatter_dx(ow, 0, c)
+        for c in range(last):
+            scatter_dx(ow, 1, c)
+            nc.sync.dma_start(out[c * P:(c + 1) * P, :], ow[c][:])
+        scatter_dx(ow, 1, last)
+        nc.sync.dma_start(out[last * P:, 0:T // 2], ow[last][:, 0:T // 2])
+        nc.scalar.dma_start(out[last * P:, T // 2:], ow[last][:, T // 2:])

@@ -28,22 +28,21 @@ RUN = 4
 KIB = 1024
 LAP = 64
 AT_SIG1 = 0
-AT_A0_FIRST = AT_SIG1 + 4 * KIB - LAP
+AT_A0_FIRST = AT_SIG1 + 8 * KIB - LAP
 AT_GATE = AT_A0_FIRST + 4 * KIB - LAP
-AT_WORDS1 = AT_GATE + 4 * KIB
+AT_WORDS1 = AT_GATE + 8 * KIB
 AT_ZEROS = AT_WORDS1 + 4 * KIB - LAP
-AT_WET_FIRST = AT_ZEROS + KIB // 2 - LAP
+AT_WET_FIRST = AT_WORDS1 + 4 * KIB
 AT_A0_SECOND = AT_WET_FIRST + 2 * KIB
 AT_WORDS0 = AT_A0_SECOND + LAP
-AT_A1_FIRST = AT_A0_SECOND + 4 * KIB
-AT_GROUPED0 = AT_A1_FIRST + 4 * KIB - LAP
+ZEROS_BYTES = AT_WORDS0 + LAP - AT_ZEROS
+AT_A1 = AT_A0_SECOND + 4 * KIB
+AT_GROUPED0 = AT_A1 + 4 * KIB - LAP
 AT_DS1 = AT_GROUPED0 + 4 * KIB - LAP
 AT_REST0 = AT_DS1 + 8 * KIB
-AT_ZT3 = AT_REST0 + 4 * KIB - LAP
+AT_ZT1 = AT_REST0 + 4 * KIB - LAP
+AT_ZT3 = AT_ZT1 + 2 * KIB
 AT_DS0 = AT_ZT3 + 2 * KIB - LAP
-AT_GW0_REST = AT_DS0 + 8 * KIB
-AT_DY_SCALES = AT_GW0_REST + 3 * KIB - LAP
-AT_WET_SECOND = AT_DY_SCALES + KIB
 
 
 def tile_moe_hib_silu_kernel(tc, dy_words, dy_scales, wet_words, wet_scales, wgt_words, wgt_scales, a, gate, offs, offs2, dst, out):
@@ -79,14 +78,12 @@ def tile_moe_hib_silu_kernel(tc, dy_words, dy_scales, wet_words, wet_scales, wgt
         dst_t = lists.tile([P, T // LIST], U16, name="dst_t")
         offs2_t = lists.tile([P, T // LIST], U16, name="offs2_t")
         offs_t = lists.tile([P, T // LIST], U16, name="offs_t")
-        dyw = [placed([P, T], I32, "dyw%d" % s, (AT_WORDS0, AT_WORDS1)[s]) for s in range(PASSES)]
         nc.sync.dma_start(dst_t[:], dst)
-        load_words(dyw[0][:], dy_words[0].rearrange("p t d -> p (t d)"))
         nc.sync.dma_start(offs2_t[:], offs2)
         nc.sync.dma_start(offs_t[:], offs)
 
-        dys = placed([P, T + SPARE], U8, "dys", AT_DY_SCALES)
-        zeros = placed([P, P], F32, "zeros", AT_ZEROS)
+        dys = kept([P, T + SPARE], U8, "dys", "after_scale_gather")
+        zeros = placed([P, ZEROS_BYTES // 4], F32, "zeros", AT_ZEROS)
         ident = kept([P, P], F32, "ident")
         gate_rows = placed([P, P], F32, "gate_rows", AT_GATE)
         wet_sc = kept([P, E * PASSES, H], U8, "wet_sc")
@@ -94,13 +91,15 @@ def tile_moe_hib_silu_kernel(tc, dy_words, dy_scales, wet_words, wet_scales, wgt
         nc.gpsimd.memset(dys[:].bitcast(I32), 0)
         nc.vector.memset(wet_sc[:].bitcast(I32), 0)
         nc.vector.memset(gs[1][:].bitcast(I32), 0)
-        nc.gpsimd.memset(zeros[:], 0.0)
-        nc.gpsimd.affine_select(out=ident[:], in_=zeros[:], compare_op=ALU.not_equal, fill=1.0, base=0, pattern=[[-1, P]], channel_multiplier=1)
+        nc.gpsimd.memset(zeros[:, 0:P], 0.0)
+        nc.gpsimd.affine_select(out=ident[:], in_=zeros[:, 0:P], compare_op=ALU.not_equal, fill=1.0, base=0, pattern=[[-1, P]], channel_multiplier=1)
         nc.gpsimd.memset(gate_rows[:], 0.0)
 
         for q in range(QUADS):
             nc.sync.dma_start(dys[32 * q:32 * q + 8, 0:T].bitcast(I32), dy_scales[:, 4 * q:4 * q + 4, :].bitcast(I32))
-        load_words(dyw[1][:], dy_words[1].rearrange("p t d -> p (t d)"))
+        dyw = [placed([P, T], I32, "dyw%d" % s, (AT_WORDS0, AT_WORDS1)[s]) for s in range(PASSES)]
+        for s in range(PASSES):
+            load_words(dyw[s][:], dy_words[s].rearrange("p t d -> p (t d)"))
         wet_first = placed([P, PASSES, 2 * H], U8, "wet_first", AT_WET_FIRST)
         load_words(wet_first[:], wet_rows[:, 0:PASSES, :])
         nc.sync.dma_start(gate_rows[0:T // P, :], gate[0:1, :].rearrange("c (b p) -> (c b) p", p=P))
@@ -114,34 +113,28 @@ def tile_moe_hib_silu_kernel(tc, dy_words, dy_scales, wet_words, wet_scales, wgt
         a0 = [placed([P, PAIR, C1], F32, "a0_first", AT_A0_FIRST), placed([P, PAIR, C1], F32, "a0_second", AT_A0_SECOND)]
         nc.sync.dma_start(a0[0][:], a_rows[:, pairs[0], 0:C1])
 
-        gw = {}
-
-        def gather_words(s, lo, hi, tile):
-            gw[s, lo] = tile
-            nc.vector.tensor_copy(tile[:], dyw[s][:].bitcast(U32).indirect(dst_t[:, columns(lo, hi)]))
-
-        gather_words(0, 0, C2, kept([P, C2], U32, "gw0_first"))
-
         nc.vector.tensor_copy(gs[0][:], dys[:].indirect(dst_t[:]))
         for q in range(QUADS):
             nc.sync.dma_start(gs[1][32 * q:32 * q + 4, :].bitcast(I32), gs[0][32 * q + 4:32 * q + 8, :].bitcast(I32))
 
-        gather_words(1, 0, C2, kept([P, C2], U32, "gw1_first"))
-        gather_words(0, C2, T, placed([P, T - C2], U32, "gw0_rest", AT_GW0_REST))
-        gather_words(1, C2, T, kept([P, T - C2], U32, "gw1_rest"))
 
-        wet_second = placed([P, PASSES, 2 * H], U8, "wet_second", AT_WET_SECOND)
+        gw = {}
+        for lo, hi in ((0, C2), (C2, T)):
+            for s in range(PASSES):
+                gw[s, lo] = kept([P, hi - lo], U32, "gw%d_%d" % (s, lo))
+                nc.vector.tensor_copy(gw[s, lo][:], dyw[s][:].bitcast(U32).indirect(dst_t[:, columns(lo, hi)]))
+
+        wet_second = kept([P, PASSES, 2 * H], U8, "wet_second", "after_scale_gather")
         load_words(wet_second[:], wet_rows[:, PASSES:2 * PASSES, :])
         nc.sync.dma_start(a0[1][:], a_rows[:, pairs[1], 0:C1])
-        a1 = [placed([P, PAIR, C1], F32, "a1_first", AT_A1_FIRST), kept([P, PAIR, C1], F32, "a1_second", "gw1_first")]
-        for h in range(2):
-            nc.sync.dma_start(a1[h][:], a_rows[:, pairs[h], C1:])
+        a1 = placed([P, PACK, C1], F32, "a1", AT_A1)
+        nc.sync.dma_start(a1[:], a_rows[:, :, C1:])
         wet_rest = placed([P, 2 * PASSES, 2 * H], U8, "wet_rest", AT_WORDS1)
         load_words(wet_rest[:], wet_rows[:, 2 * PASSES:, :])
         wet = (wet_first[:], wet_second[:], wet_rest[:, 0:PASSES, :], wet_rest[:, PASSES:, :])
         wgt = placed([P, G, 2 * K], U8, "wgt", AT_WET_FIRST)
         load_words(wgt[:], wgt_words.rearrange("f s p c -> p (f s) c"))
-        wgt_sc = kept([P, G, K], U8, "wgt_sc", "gw0_first")
+        wgt_sc = kept([P, G, K], U8, "wgt_sc", "gw0_0")
         nc.gpsimd.memset(wgt_sc[:].bitcast(I32), 0)
         load_scales(wgt_sc, wgt_scales.rearrange("f s b k -> (f s) b k"))
 
@@ -182,11 +175,10 @@ def tile_moe_hib_silu_kernel(tc, dy_words, dy_scales, wet_words, wet_scales, wgt
         def in_dead_a(tile):
             return [tile[:, n, :].rearrange("m (r p) -> m r p", r=PACK) for n in range(2)]
 
-        def silu_of_minus(to, a_pair):
-            nc.scalar.activation(to[:], a_pair[:], ACT.Silu, scale=-1.0)
-
-        def one_minus(t):
-            nc.gpsimd.tensor_scalar(t[:], t[:], -1.0, 1.0, ALU.mult, ALU.add)
+        def rest_by_sigmoid(to, a_pair):
+            nc.scalar.activation(to[:], a_pair[:], ACT.Sigmoid, scale=-1.0)
+            nc.gpsimd.tensor_tensor(to[:], to[:], a_pair[:], ALU.mult)
+            nc.gpsimd.tensor_scalar(to[:], to[:], 1.0, 1.0, ALU.mult, ALU.add)
 
         def scatter_z(zw, f, r, lo, hi):
             nc.vector.tensor_copy(zw[r][:].indirect(offs2_t[:, columns(f * C1 + lo, f * C1 + hi)]), zs[f][:, r, lo:hi])
@@ -212,61 +204,50 @@ def tile_moe_hib_silu_kernel(tc, dy_words, dy_scales, wet_words, wet_scales, wgt
             nc.vector.tensor_copy(ow[c][:].indirect(offs_t[:, columns(f * C1, (f + 1) * C1)]), dxs[f][:, c, :])
 
         rest0 = [kept([P, PAIR, C1], F32, "rest0_first")]
-        silu_of_minus(rest0[0], a0[0])
-        one_minus(rest0[0])
-        lead = kept([P, 1, P], F32, "lead", "after_lead")
-        expert(0, [kept([P, PACK, P], F32, "zt0"), kept([P, PACK, P], F32, "zt1", "after_lead")], lead)
-        expert(1, [kept([P, PACK, P], F32, "zt2"), placed([P, PACK, P], F32, "zt3", AT_ZT3)])
+        rest_by_sigmoid(rest0[0], a0[0])
+        lead = placed([P, 1, P], F32, "lead", AT_ZT1)
+        expert(0, [kept([P, PACK, P], F32, "zt0"), placed([P, PACK, P], F32, "zt1", AT_ZT1)], lead)
         rest0.append(placed([P, PAIR, C1], F32, "rest0_second", AT_REST0))
-        silu_of_minus(rest0[1], a0[1])
-        one_minus(rest0[1])
+        rest_by_sigmoid(rest0[1], a0[1])
+        expert(1, [kept([P, PACK, P], F32, "zt2"), placed([P, PACK, P], F32, "zt3", AT_ZT3)])
         ds0 = placed([P, PACK, C1], F32, "ds0", AT_DS0)
         for h in range(2):
             nc.scalar.activation(ds0[:, pairs[h], :], a0[h][:], ACT.Sigmoid)
             nc.gpsimd.tensor_tensor(ds0[:, pairs[h], :], ds0[:, pairs[h], :], rest0[h][:], ALU.mult)
         expert(2, in_dead_a(a0[1]))
         expert(3, in_dead_a(a0[0]))
-        sig1 = [placed([P, PAIR, C1], F32, "sig1_first", AT_SIG1), a0[1]]
-        for h in (1, 0):
-            nc.scalar.activation(sig1[h][:], a1[h][:], ACT.Sigmoid)
-        rest1 = [placed([P, PAIR, C1], F32, "rest1_first", AT_GATE)]
-        silu_of_minus(rest1[0], a1[0])
+        sig1 = placed([P, PACK, C1], F32, "sig1", AT_SIG1)
+        nc.scalar.activation(sig1[:], a1[:], ACT.Sigmoid)
+        rest1 = placed([P, PACK, C1], F32, "rest1", AT_GATE)
+        nc.scalar.activation(rest1[:], a1[:], ACT.Silu, scale=-1.0)
 
         zw0 = [kept([P, T], F32, "zw0_%d" % r) for r in range(PACK)]
         for r in range(last):
             scatter_z(zw0, 0, r, 0, P)
         scatter_z(zw0, 0, last, 0, C2)
-        scatter_z(zw0, 0, 0, P, C2)
-        scatter_z(zw0, 0, 1, P, C1)
-        scatter_z(zw0, 0, 0, C2, C1)
+        for r in range(2):
+            scatter_z(zw0, 0, r, P, C2)
         scatter_z(zw0, 0, 2, P, C1)
-        scatter_z(zw0, 0, last, C2, C1)
+        for r in (0, 1, last):
+            scatter_z(zw0, 0, r, C2, C1)
         grouped0 = placed([P, C1, PACK], BF16, "grouped0", AT_GROUPED0)
         second_product(zw0, 0, ds0, grouped0)
 
-        one_minus(rest1[0])
-        rest1.append(kept([P, PAIR, C1], F32, "rest1_second", "planes0"))
-        silu_of_minus(rest1[1], a1[1])
-        nc.scalar.activation(rest1[1][:], rest1[1][:], ACT.Copy, scale=-1.0, bias=1.0)
+        nc.gpsimd.tensor_scalar(rest1[:], rest1[:], -1.0, 1.0, ALU.mult, ALU.add)
         ds1 = placed([P, PACK, C1], F32, "ds1", AT_DS1)
-        for h in range(2):
-            nc.gpsimd.tensor_tensor(ds1[:, pairs[h], :], sig1[h][:], rest1[h][:], ALU.mult)
+        nc.gpsimd.tensor_tensor(ds1[:], sig1[:], rest1[:], ALU.mult)
 
-        zw1 = [kept([P, T], F32, "zw1_%d" % r) for r in range(last)] + [placed([P, T], F32, "zw1_last", AT_A1_FIRST)]
-        for r in range(2):
-            scatter_z(zw1, 1, r, 0, C2)
-        scatter_z(zw1, 1, 2, 0, C1)
-        for r in range(2):
-            scatter_z(zw1, 1, r, C2, C1)
+        zw1 = [kept([P, T], F32, "zw1_%d" % r) for r in range(last)] + [placed([P, T], F32, "zw1_last", AT_A1)]
+        scatter_z(zw1, 1, 0, 0, C2)
+        for r in (1, 2):
+            scatter_z(zw1, 1, r, 0, C1)
+        scatter_z(zw1, 1, 0, C2, C1)
         scatter_z(zw1, 1, last, 0, C1)
         second_product(zw1, 1, ds1, kept([P, C1, PACK], BF16, "grouped1"))
 
         ow = [kept([P, T], F32, "ow%d" % c, "grouped1" if c == last else None) for c in range(K // P)]
         for c in range(K // P):
             scatter_dx(ow, 0, c)
-        for c in range(last):
+        for c in range(K // P):
             scatter_dx(ow, 1, c)
             nc.sync.dma_start(out[c * P:(c + 1) * P, :], ow[c][:])
-        scatter_dx(ow, 1, last)
-        nc.sync.dma_start(out[last * P:, 0:T // 2], ow[last][:, 0:T // 2])
-        nc.scalar.dma_start(out[last * P:, T // 2:], ow[last][:, T // 2:])

@@ -23,7 +23,6 @@ PASSES = N // (P * PACK)
 LIST = 16
 QUADS = 4
 SPARE = 352
-RUN = 4
 
 KIB = 1024
 LAP = 64
@@ -37,12 +36,13 @@ AT_A0_SECOND = AT_WET_FIRST + 2 * KIB
 AT_WORDS0 = AT_A0_SECOND + LAP
 ZEROS_BYTES = AT_WORDS0 + LAP - AT_ZEROS
 AT_A1 = AT_A0_SECOND + 4 * KIB
-AT_GROUPED0 = AT_A1 + 4 * KIB - LAP
+AT_GROUPED0 = AT_A1 + 8 * KIB
 AT_DS1 = AT_GROUPED0 + 4 * KIB - LAP
 AT_REST0 = AT_DS1 + 8 * KIB
 AT_ZT1 = AT_REST0 + 4 * KIB - LAP
 AT_ZT3 = AT_ZT1 + 2 * KIB
 AT_DS0 = AT_ZT3 + 2 * KIB - LAP
+AT_ZW1_LAST = AT_DS0
 
 
 def tile_moe_hib_silu_kernel(tc, dy_words, dy_scales, wet_words, wet_scales, wgt_words, wgt_scales, a, gate, offs, offs2, dst, out):
@@ -138,8 +138,9 @@ def tile_moe_hib_silu_kernel(tc, dy_words, dy_scales, wet_words, wet_scales, wgt
         nc.gpsimd.memset(wgt_sc[:].bitcast(I32), 0)
         load_scales(wgt_sc, wgt_scales.rearrange("f s b k -> (f s) b k"))
 
-        zs = [kept([P, PACK, C1], F32, "zs%d" % f) for f in range(G)]
-        dxs = [kept([P, K // P, C1], F32, "dxs%d" % f) for f in range(G)]
+        zs0 = kept([P, PACK, C1], F32, "zs0")
+        zs1 = [kept([P, PAIR, C1], F32, "zs1_first", "before_quantize0"), kept([P, PAIR, C1], F32, "zs1_second")]
+        dxs = [placed([P, K // P, C1], F32, "dxs0", AT_GATE), kept([P, K // P, C1], F32, "dxs1")]
 
         def weigh(b, acc, zt, planes):
             nc.scalar.activation(zt[:, planes, :], acc[:].rearrange("m (p r) -> m r p", r=PACK)[:, planes, :], ACT.Copy, scale=gate_col[:, b:b + 1])
@@ -148,7 +149,11 @@ def tile_moe_hib_silu_kernel(tc, dy_words, dy_scales, wet_words, wet_scales, wgt
             f, u = divmod(b * P, C1)
             for r in range(planes.start, planes.stop):
                 nc.tensor.transpose(turned[:, r, :], zt[:, r, :], ident[:])
-            nc.scalar.activation(zs[f][:, planes, u:u + P], turned[:, planes, :], ACT.Copy)
+            if f == 0:
+                nc.scalar.activation(zs0[:, planes, u:u + P], turned[:, planes, :], ACT.Copy)
+            else:
+                for h in range(2):
+                    nc.scalar.activation(zs1[h][:, :, u:u + P], turned[:, pairs[h], :], ACT.Copy)
 
         def expert(e, zt, lead=None):
             blocks = (2 * e, 2 * e + 1)
@@ -181,14 +186,13 @@ def tile_moe_hib_silu_kernel(tc, dy_words, dy_scales, wet_words, wet_scales, wgt
             nc.gpsimd.tensor_scalar(to[:], to[:], 1.0, 1.0, ALU.mult, ALU.add)
 
         def scatter_z(zw, f, r, lo, hi):
-            nc.vector.tensor_copy(zw[r][:].indirect(offs2_t[:, columns(f * C1 + lo, f * C1 + hi)]), zs[f][:, r, lo:hi])
+            sums = zs0[:, r, lo:hi] if f == 0 else zs1[r // PAIR][:, r % PAIR, lo:hi]
+            nc.vector.tensor_copy(zw[r][:].indirect(offs2_t[:, columns(f * C1 + lo, f * C1 + hi)]), sums)
 
-        def second_product(zw, f, ds, grouped):
-            planes = kept([P, PACK, C1], BF16, "planes%d" % f)
-            for r in range(PACK):
-                nc.gpsimd.tensor_tensor(planes[:, r, :], zw[r][:, f * C1:(f + 1) * C1], ds[:, r, :], ALU.mult)
-            nc.scalar.copy(grouped[:].rearrange("p (c i) r -> p c r i", i=RUN), planes[:].rearrange("p r (c i) -> p c r i", i=RUN))
-            codes = kept([P, C1], U32, "codes%d" % f)
+        def gradient(zw, f, ds, grouped, r):
+            nc.gpsimd.tensor_tensor(grouped[:, :, r], zw[r][:, f * C1:(f + 1) * C1], ds[:, r, :], ALU.mult)
+
+        def second_product(f, grouped, codes):
             scales = kept([P, C1], U8, "scales%d" % f)
             nc.vector.quantize_mx(out=codes[:].bitcast(FP8X4), scales=scales[:], in_=grouped[:].rearrange("p j r -> p (j r)"))
             for c in range(K // P):
@@ -218,8 +222,10 @@ def tile_moe_hib_silu_kernel(tc, dy_words, dy_scales, wet_words, wet_scales, wgt
         expert(3, in_dead_a(a0[0]))
         sig1 = placed([P, PACK, C1], F32, "sig1", AT_SIG1)
         nc.scalar.activation(sig1[:], a1[:], ACT.Sigmoid)
-        rest1 = placed([P, PACK, C1], F32, "rest1", AT_GATE)
-        nc.scalar.activation(rest1[:], a1[:], ACT.Silu, scale=-1.0)
+        silu1 = placed([P, PACK, C1], F32, "silu1", AT_GATE)
+        nc.scalar.activation(silu1[:], a1[:], ACT.Silu, scale=-1.0)
+        rest1 = kept([P, PACK, C1], F32, "rest1")
+        nc.scalar.activation(rest1[:], silu1[:], ACT.Copy, scale=-1.0, bias=1.0)
 
         zw0 = [kept([P, T], F32, "zw0_%d" % r) for r in range(PACK)]
         for r in range(last):
@@ -231,23 +237,27 @@ def tile_moe_hib_silu_kernel(tc, dy_words, dy_scales, wet_words, wet_scales, wgt
         for r in (0, 1, last):
             scatter_z(zw0, 0, r, C2, C1)
         grouped0 = placed([P, C1, PACK], BF16, "grouped0", AT_GROUPED0)
-        second_product(zw0, 0, ds0, grouped0)
+        for r in (2, 0, 1, last):
+            gradient(zw0, 0, ds0, grouped0, r)
 
-        nc.gpsimd.tensor_scalar(rest1[:], rest1[:], -1.0, 1.0, ALU.mult, ALU.add)
+        zw1 = [kept([P, T], F32, "zw1_%d" % r) for r in range(last)] + [placed([P, T], F32, "zw1_last", AT_ZW1_LAST)]
+        scatter_z(zw1, 1, 0, 0, C2)
+        scatter_z(zw1, 1, 1, 0, C1)
+        scatter_z(zw1, 1, 0, C2, C1)
+        scatter_z(zw1, 1, 2, 0, C1)
+        second_product(0, grouped0, kept([P, C1], U32, "codes0", "before_quantize0"))
+        scatter_z(zw1, 1, last, 0, C1)
         ds1 = placed([P, PACK, C1], F32, "ds1", AT_DS1)
         nc.gpsimd.tensor_tensor(ds1[:], sig1[:], rest1[:], ALU.mult)
+        grouped1 = kept([P, C1, PACK], BF16, "grouped1")
+        for r in (1, 0, 2, last):
+            gradient(zw1, 1, ds1, grouped1, r)
 
-        zw1 = [kept([P, T], F32, "zw1_%d" % r) for r in range(last)] + [placed([P, T], F32, "zw1_last", AT_A1)]
-        scatter_z(zw1, 1, 0, 0, C2)
-        for r in (1, 2):
-            scatter_z(zw1, 1, r, 0, C1)
-        scatter_z(zw1, 1, 0, C2, C1)
-        scatter_z(zw1, 1, last, 0, C1)
-        second_product(zw1, 1, ds1, kept([P, C1, PACK], BF16, "grouped1"))
-
-        ow = [kept([P, T], F32, "ow%d" % c, "grouped1" if c == last else None) for c in range(K // P)]
-        for c in range(K // P):
+        ow = [kept([P, T], F32, "ow%d" % c) for c in range(last)] + [placed([P, T], F32, "ow_last", AT_DS1 + 4 * KIB)]
+        for c in range(last):
             scatter_dx(ow, 0, c)
+        second_product(1, grouped1, kept([P, C1], U32, "codes1"))
+        scatter_dx(ow, 0, last)
         for c in range(K // P):
             scatter_dx(ow, 1, c)
             nc.sync.dma_start(out[c * P:(c + 1) * P, :], ow[c][:])

@@ -26,16 +26,22 @@ SPARE = 352
 
 KIB = 1024
 LAP = 64
-AT_SIG1 = 0
-AT_A0_FIRST = AT_SIG1 + 8 * KIB - LAP
-AT_GATE = AT_A0_FIRST + 4 * KIB - LAP
-AT_WORDS1 = AT_GATE + 8 * KIB
-AT_ZEROS = AT_WORDS1 + 4 * KIB - LAP
-AT_WET_FIRST = AT_WORDS1 + 4 * KIB
-AT_A0_SECOND = AT_WET_FIRST + 2 * KIB
-AT_WORDS0 = AT_A0_SECOND + LAP
-ZEROS_BYTES = AT_WORDS0 + LAP - AT_ZEROS
-AT_A1 = AT_A0_SECOND + 4 * KIB
+AT_WORDS = 0
+AT_WET_REST = AT_WORDS + 4 * KIB + LAP
+AT_ZEROS = AT_WORDS + 8 * KIB - LAP
+AT_WET_FIRST = AT_WORDS + 8 * KIB
+AT_LATE_SC = AT_WET_FIRST + 2 * KIB
+AT_A0_SECOND = AT_LATE_SC + 3 * KIB
+AT_GATE = AT_A0_SECOND - KIB // 4
+AT_A0_FIRST = AT_A0_SECOND + 4 * KIB
+AT_SIG1 = AT_A0_FIRST + LAP - 8 * KIB
+AT_GS1 = AT_A0_FIRST + 4 * KIB
+AT_SILU1 = AT_GS1 - LAP
+AT_FIRST_SC = AT_GS1 + KIB
+AT_WET_SECOND = AT_FIRST_SC + KIB - LAP
+ZEROS_BYTES = AT_FIRST_SC + LAP - AT_ZEROS
+AT_A1 = AT_SILU1 + 8 * KIB
+AT_ZT0 = AT_A1
 AT_GROUPED0 = AT_A1 + 8 * KIB
 AT_DS1 = AT_GROUPED0 + 4 * KIB - LAP
 AT_REST0 = AT_DS1 + 8 * KIB
@@ -82,28 +88,28 @@ def tile_moe_hib_silu_kernel(tc, dy_words, dy_scales, wet_words, wet_scales, wgt
         nc.sync.dma_start(offs2_t[:], offs2)
         nc.sync.dma_start(offs_t[:], offs)
 
-        dys = kept([P, T + SPARE], U8, "dys", "after_scale_gather")
+        dys = kept([P, T + SPARE], U8, "dys")
         zeros = placed([P, ZEROS_BYTES // 4], F32, "zeros", AT_ZEROS)
         ident = kept([P, P], F32, "ident")
         gate_rows = placed([P, P], F32, "gate_rows", AT_GATE)
-        wet_sc = kept([P, E * PASSES, H], U8, "wet_sc")
-        gs = [kept([P, T], U8, "gs%d" % s) for s in range(PASSES)]
+        first_sc = placed([P, PASSES, H], U8, "first_sc", AT_FIRST_SC)
+        gs = [kept([P, T], U8, "gs0"), placed([P, T], U8, "gs1", AT_GS1)]
         nc.gpsimd.memset(dys[:].bitcast(I32), 0)
-        nc.vector.memset(wet_sc[:].bitcast(I32), 0)
-        nc.vector.memset(gs[1][:].bitcast(I32), 0)
         nc.gpsimd.memset(zeros[:, 0:P], 0.0)
         nc.gpsimd.affine_select(out=ident[:], in_=zeros[:, 0:P], compare_op=ALU.not_equal, fill=1.0, base=0, pattern=[[-1, P]], channel_multiplier=1)
+        nc.gpsimd.memset(first_sc[:].bitcast(I32), 0)
         nc.gpsimd.memset(gate_rows[:], 0.0)
+        nc.gpsimd.memset(gs[1][:].bitcast(I32), 0)
 
         for q in range(QUADS):
             nc.sync.dma_start(dys[32 * q:32 * q + 8, 0:T].bitcast(I32), dy_scales[:, 4 * q:4 * q + 4, :].bitcast(I32))
-        dyw = [placed([P, T], I32, "dyw%d" % s, (AT_WORDS0, AT_WORDS1)[s]) for s in range(PASSES)]
-        for s in range(PASSES):
-            load_words(dyw[s][:], dy_words[s].rearrange("p t d -> p (t d)"))
+        dyw = placed([P, PASSES, T], I32, "dyw", AT_WORDS)
+        load_words(dyw[:], dy_words.rearrange("s p t d -> p s (t d)"))
         wet_first = placed([P, PASSES, 2 * H], U8, "wet_first", AT_WET_FIRST)
         load_words(wet_first[:], wet_rows[:, 0:PASSES, :])
         nc.sync.dma_start(gate_rows[0:T // P, :], gate[0:1, :].rearrange("c (b p) -> (c b) p", p=P))
-        load_scales(wet_sc, wet_scales.rearrange("e s b i -> (e s) b i"))
+        wet_sc_rows = wet_scales.rearrange("e s b i -> (e s) b i")
+        load_scales(first_sc, wet_sc_rows[0:PASSES])
 
         gate_col = kept([P, T // P], F32, "gate_col")
         gate_ps = ps2.tile([P, C1], F32, name="acc2")
@@ -122,25 +128,20 @@ def tile_moe_hib_silu_kernel(tc, dy_words, dy_scales, wet_words, wet_scales, wgt
         for lo, hi in ((0, C2), (C2, T)):
             for s in range(PASSES):
                 gw[s, lo] = kept([P, hi - lo], U32, "gw%d_%d" % (s, lo))
-                nc.vector.tensor_copy(gw[s, lo][:], dyw[s][:].bitcast(U32).indirect(dst_t[:, columns(lo, hi)]))
+                nc.vector.tensor_copy(gw[s, lo][:], dyw[:, s, :].bitcast(U32).indirect(dst_t[:, columns(lo, hi)]))
 
-        wet_second = kept([P, PASSES, 2 * H], U8, "wet_second", "after_scale_gather")
-        load_words(wet_second[:], wet_rows[:, PASSES:2 * PASSES, :])
+        wet_second = placed([P, PASSES, 2 * H], U8, "wet_second", AT_WET_SECOND)
         nc.sync.dma_start(a0[1][:], a_rows[:, pairs[1], 0:C1])
-        a1 = placed([P, PACK, C1], F32, "a1", AT_A1)
-        nc.sync.dma_start(a1[:], a_rows[:, :, C1:])
-        wet_rest = placed([P, 2 * PASSES, 2 * H], U8, "wet_rest", AT_WORDS1)
-        load_words(wet_rest[:], wet_rows[:, 2 * PASSES:, :])
+        late_sc = placed([P, (E - 1) * PASSES, H], U8, "late_sc", AT_LATE_SC)
+        nc.gpsimd.memset(late_sc[:].bitcast(I32), 0)
+        load_scales(late_sc, wet_sc_rows[PASSES:])
+        wet_sc = [first_sc[:]] + [late_sc[:, PASSES * e:PASSES * (e + 1), :] for e in range(E - 1)]
+        wet_rest = placed([P, 2 * PASSES, 2 * H], U8, "wet_rest", AT_WET_REST)
         wet = (wet_first[:], wet_second[:], wet_rest[:, 0:PASSES, :], wet_rest[:, PASSES:, :])
-        wgt = placed([P, G, 2 * K], U8, "wgt", AT_WET_FIRST)
-        load_words(wgt[:], wgt_words.rearrange("f s p c -> p (f s) c"))
-        wgt_sc = kept([P, G, K], U8, "wgt_sc", "gw0_0")
-        nc.gpsimd.memset(wgt_sc[:].bitcast(I32), 0)
-        load_scales(wgt_sc, wgt_scales.rearrange("f s b k -> (f s) b k"))
 
         zs0 = kept([P, PACK, C1], F32, "zs0")
         zs1 = [kept([P, PAIR, C1], F32, "zs1_first", "before_quantize0"), kept([P, PAIR, C1], F32, "zs1_second")]
-        dxs = [placed([P, K // P, C1], F32, "dxs0", AT_GATE), kept([P, K // P, C1], F32, "dxs1")]
+        dxs = [placed([P, K // P, C1], F32, "dxs0", AT_SILU1), kept([P, K // P, C1], F32, "dxs1")]
 
         def weigh(b, acc, zt, planes):
             nc.scalar.activation(zt[:, planes, :], acc[:].rearrange("m (p r) -> m r p", r=PACK)[:, planes, :], ACT.Copy, scale=gate_col[:, b:b + 1])
@@ -165,7 +166,7 @@ def tile_moe_hib_silu_kernel(tc, dy_words, dy_scales, wet_words, wet_scales, wgt
                     nc.tensor.matmul_mx(
                         out=acc[n][:],
                         lhsT=gw[s, lo][:, b * P - lo:(b + 1) * P - lo].bitcast(FP8X4), lhsT_scale=gs[s][:, b * P:(b + 1) * P],
-                        rhs=wet[e][:, s, :].bitcast(FP4X4), rhs_scale=wet_sc[:, e * PASSES + s, :],
+                        rhs=wet[e][:, s, :].bitcast(FP4X4), rhs_scale=wet_sc[e][:, s, :],
                         start=(s == 0), stop=(s == PASSES - 1))
             planes = [slice(0 if lead is None else 1, PACK), slice(0, PACK)]
             if lead is not None:
@@ -210,7 +211,16 @@ def tile_moe_hib_silu_kernel(tc, dy_words, dy_scales, wet_words, wet_scales, wgt
         rest0 = [kept([P, PAIR, C1], F32, "rest0_first")]
         rest_by_sigmoid(rest0[0], a0[0])
         lead = placed([P, 1, P], F32, "lead", AT_ZT1)
-        expert(0, [kept([P, PACK, P], F32, "zt0"), placed([P, PACK, P], F32, "zt1", AT_ZT1)], lead)
+        expert(0, [placed([P, PACK, P], F32, "zt0", AT_ZT0), placed([P, PACK, P], F32, "zt1", AT_ZT1)], lead)
+        load_words(wet_second[:], wet_rows[:, PASSES:2 * PASSES, :])
+        load_words(wet_rest[:], wet_rows[:, 2 * PASSES:, :])
+        a1 = placed([P, PACK, C1], F32, "a1", AT_A1)
+        nc.sync.dma_start(a1[:], a_rows[:, :, C1:])
+        wgt = kept([P, G, 2 * K], U8, "wgt", "gw1_0")
+        load_words(wgt[:], wgt_words.rearrange("f s p c -> p (f s) c"))
+        wgt_sc = kept([P, G, K], U8, "wgt_sc", "gw0_0")
+        nc.gpsimd.memset(wgt_sc[:].bitcast(I32), 0)
+        load_scales(wgt_sc, wgt_scales.rearrange("f s b k -> (f s) b k"))
         rest0.append(placed([P, PAIR, C1], F32, "rest0_second", AT_REST0))
         rest_by_sigmoid(rest0[1], a0[1])
         expert(1, [kept([P, PACK, P], F32, "zt2"), placed([P, PACK, P], F32, "zt3", AT_ZT3)])
@@ -222,7 +232,7 @@ def tile_moe_hib_silu_kernel(tc, dy_words, dy_scales, wet_words, wet_scales, wgt
         expert(3, in_dead_a(a0[0]))
         sig1 = placed([P, PACK, C1], F32, "sig1", AT_SIG1)
         nc.scalar.activation(sig1[:], a1[:], ACT.Sigmoid)
-        silu1 = placed([P, PACK, C1], F32, "silu1", AT_GATE)
+        silu1 = placed([P, PACK, C1], F32, "silu1", AT_SILU1)
         nc.scalar.activation(silu1[:], a1[:], ACT.Silu, scale=-1.0)
         rest1 = kept([P, PACK, C1], F32, "rest1")
         nc.scalar.activation(rest1[:], silu1[:], ACT.Copy, scale=-1.0, bias=1.0)

@@ -79,6 +79,7 @@ def tile_moe_hib_silu_kernel(tc, dy_words, dy_scales, wet_words, wet_scales, wgt
         a_rows = a.rearrange("(p r) j -> p r j", r=PACK)
         wet_rows = wet_words.rearrange("e s p c -> p (e s) c")
         pairs = [slice(PAIR * h, PAIR * (h + 1)) for h in range(PACK // PAIR)]
+        pairs1 = [slice(0, PACK, 2), slice(1, PACK, 2)]
         last = PACK - 1
 
         dst_t = lists.tile([P, T // LIST], U16, name="dst_t")
@@ -140,7 +141,7 @@ def tile_moe_hib_silu_kernel(tc, dy_words, dy_scales, wet_words, wet_scales, wgt
         wet = (wet_first[:], wet_second[:], wet_rest[:, 0:PASSES, :], wet_rest[:, PASSES:, :])
 
         zs0 = kept([P, PACK, C1], F32, "zs0")
-        zs1 = [kept([P, PAIR, C1], F32, "zs1_first", "before_quantize0"), kept([P, PAIR, C1], F32, "zs1_second")]
+        zs1 = [kept([P, 1, C1], F32, "zs1_first", "before_quantize0"), kept([P, last, C1], F32, "zs1_rest")]
         dxs = [placed([P, K // P, C1], F32, "dxs0", AT_SILU1), kept([P, K // P, C1], F32, "dxs1")]
 
         def weigh(b, acc, zt, planes):
@@ -153,8 +154,8 @@ def tile_moe_hib_silu_kernel(tc, dy_words, dy_scales, wet_words, wet_scales, wgt
             if f == 0:
                 nc.scalar.activation(zs0[:, planes, u:u + P], turned[:, planes, :], ACT.Copy)
             else:
-                for h in range(2):
-                    nc.scalar.activation(zs1[h][:, :, u:u + P], turned[:, pairs[h], :], ACT.Copy)
+                nc.scalar.activation(zs1[0][:, :, u:u + P], turned[:, 0:1, :], ACT.Copy)
+                nc.scalar.activation(zs1[1][:, :, u:u + P], turned[:, 1:PACK, :], ACT.Copy)
 
         def expert(e, zt, lead=None):
             blocks = (2 * e, 2 * e + 1)
@@ -187,7 +188,7 @@ def tile_moe_hib_silu_kernel(tc, dy_words, dy_scales, wet_words, wet_scales, wgt
             nc.gpsimd.tensor_scalar(to[:], to[:], 1.0, 1.0, ALU.mult, ALU.add)
 
         def scatter_z(zw, f, r, lo, hi):
-            sums = zs0[:, r, lo:hi] if f == 0 else zs1[r // PAIR][:, r % PAIR, lo:hi]
+            sums = zs0[:, r, lo:hi] if f == 0 else zs1[min(r, 1)][:, max(r - 1, 0), lo:hi]
             nc.vector.tensor_copy(zw[r][:].indirect(offs2_t[:, columns(f * C1 + lo, f * C1 + hi)]), sums)
 
         def gradient(zw, f, ds, grouped, r):
@@ -233,9 +234,10 @@ def tile_moe_hib_silu_kernel(tc, dy_words, dy_scales, wet_words, wet_scales, wgt
         sig1 = placed([P, PACK, C1], F32, "sig1", AT_SIG1)
         nc.scalar.activation(sig1[:], a1[:], ACT.Sigmoid)
         silu1 = placed([P, PACK, C1], F32, "silu1", AT_SILU1)
-        nc.scalar.activation(silu1[:], a1[:], ACT.Silu, scale=-1.0)
         rest1 = kept([P, PACK, C1], F32, "rest1")
-        nc.scalar.activation(rest1[:], silu1[:], ACT.Copy, scale=-1.0, bias=1.0)
+        for pair in pairs1:
+            nc.scalar.activation(silu1[:, pair, :], a1[:, pair, :], ACT.Silu, scale=-1.0)
+            nc.scalar.activation(rest1[:, pair, :], silu1[:, pair, :], ACT.Copy, scale=-1.0, bias=1.0)
 
         zw0 = [kept([P, T], F32, "zw0_%d" % r) for r in range(PACK)]
         for r in range(last):
@@ -251,16 +253,17 @@ def tile_moe_hib_silu_kernel(tc, dy_words, dy_scales, wet_words, wet_scales, wgt
             gradient(zw0, 0, ds0, grouped0, r)
 
         zw1 = [kept([P, T], F32, "zw1_%d" % r) for r in range(last)] + [placed([P, T], F32, "zw1_last", AT_ZW1_LAST)]
-        scatter_z(zw1, 1, 0, 0, C2)
-        scatter_z(zw1, 1, 1, 0, C1)
-        scatter_z(zw1, 1, 0, C2, C1)
+        scatter_z(zw1, 1, 1, 0, C2)
+        scatter_z(zw1, 1, 0, 0, C1)
         scatter_z(zw1, 1, 2, 0, C1)
         second_product(0, grouped0, kept([P, C1], U32, "codes0", "before_quantize0"))
+        scatter_z(zw1, 1, 1, C2, C1)
         scatter_z(zw1, 1, last, 0, C1)
         ds1 = placed([P, PACK, C1], F32, "ds1", AT_DS1)
-        nc.gpsimd.tensor_tensor(ds1[:], sig1[:], rest1[:], ALU.mult)
         grouped1 = kept([P, C1, PACK], BF16, "grouped1")
-        for r in (1, 0, 2, last):
+        for pair in pairs1:
+            nc.gpsimd.tensor_tensor(ds1[:, pair, :], sig1[:, pair, :], rest1[:, pair, :], ALU.mult)
+        for r in (0, 2, 1, last):
             gradient(zw1, 1, ds1, grouped1, r)
 
         ow = [kept([P, T], F32, "ow%d" % c) for c in range(last)] + [placed([P, T], F32, "ow_last", AT_DS1 + 4 * KIB)]

@@ -98,6 +98,8 @@ def tile_moe_hib_silu_kernel(tc, dy_words, dy_scales, wet_words, wet_scales, wgt
         nc.gpsimd.memset(dys[:].bitcast(I32), 0)
         nc.gpsimd.memset(zeros[:, 0:P], 0.0)
         nc.gpsimd.affine_select(out=ident[:], in_=zeros[:, 0:P], compare_op=ALU.not_equal, fill=1.0, base=0, pattern=[[-1, P]], channel_multiplier=1)
+        unread = kept([P, 1], F32, "unread")
+        nc.scalar.activation(unread[:], ident[:, 0:1], ACT.Sigmoid)
         nc.gpsimd.memset(first_sc[:].bitcast(I32), 0)
         nc.gpsimd.memset(gate_rows[:], 0.0)
         nc.gpsimd.memset(gs[1][:].bitcast(I32), 0)

@@ -41,11 +41,12 @@ AT_FIRST_SC = AT_GS1 + KIB
 AT_WET_SECOND = AT_FIRST_SC + KIB - LAP
 ZEROS_BYTES = AT_FIRST_SC + LAP - AT_ZEROS
 AT_A1 = AT_SILU1 + 8 * KIB
-AT_ZT0 = AT_A1
+AT_LEAD = AT_A1
 AT_GROUPED0 = AT_A1 + 8 * KIB
 AT_DS1 = AT_GROUPED0 + 4 * KIB - LAP
 AT_REST0 = AT_DS1 + 8 * KIB
 AT_ZT1 = AT_REST0 + 4 * KIB - LAP
+AT_ZT0 = AT_ZT1 + KIB
 AT_ZT3 = AT_ZT1 + 2 * KIB
 AT_DS0 = AT_ZT3 + 2 * KIB - LAP
 AT_ZW1_LAST = AT_DS0
@@ -177,9 +178,13 @@ def tile_moe_hib_silu_kernel(tc, dy_words, dy_scales, wet_words, wet_scales, wgt
             weigh(blocks[0], acc[0], zt[0], planes[0])
             if lead is not None:
                 turn(blocks[0], lead, slice(0, 1), ps2.tile([P, PACK, P], F32, name="acc2"))
+            turned = [ps1.tile([P, PACK, P], F32, name="turned", tag="bank%d" % (2 * (1 - f) + n)) for n in range(2)]
+            if lead is not None:
+                turn(blocks[0], zt[0], planes[0], turned[0])
             weigh(blocks[1], acc[1], zt[1], planes[1])
-            for n, b in enumerate(blocks):
-                turn(b, zt[n], planes[n], ps1.tile([P, PACK, P], F32, name="turned", tag="bank%d" % (2 * (1 - f) + n)))
+            if lead is None:
+                turn(blocks[0], zt[0], planes[0], turned[0])
+            turn(blocks[1], zt[1], planes[1], turned[1])
 
         def in_dead_a(tile):
             return [tile[:, n, :].rearrange("m (r p) -> m r p", r=PACK) for n in range(2)]
@@ -213,7 +218,7 @@ def tile_moe_hib_silu_kernel(tc, dy_words, dy_scales, wet_words, wet_scales, wgt
 
         rest0 = [kept([P, PAIR, C1], F32, "rest0_first")]
         rest_by_sigmoid(rest0[0], a0[0])
-        lead = placed([P, 1, P], F32, "lead", AT_ZT1)
+        lead = placed([P, 1, P], F32, "lead", AT_LEAD)
         expert(0, [placed([P, PACK, P], F32, "zt0", AT_ZT0), placed([P, PACK, P], F32, "zt1", AT_ZT1)], lead)
         load_words(wet_second[:], wet_rows[:, PASSES:2 * PASSES, :])
         load_words(wet_rest[:], wet_rows[:, 2 * PASSES:, :])
@@ -242,22 +247,18 @@ def tile_moe_hib_silu_kernel(tc, dy_words, dy_scales, wet_words, wet_scales, wgt
             nc.scalar.activation(rest1[:, pair, :], silu1[:, pair, :], ACT.Copy, scale=-1.0, bias=1.0)
 
         zw0 = [kept([P, T], F32, "zw0_%d" % r) for r in range(PACK)]
-        for r in range(last):
-            scatter_z(zw0, 0, r, 0, P)
-        scatter_z(zw0, 0, last, 0, C2)
-        for r in range(2):
-            scatter_z(zw0, 0, r, P, C2)
-        scatter_z(zw0, 0, 2, P, C1)
-        for r in (0, 1, last):
-            scatter_z(zw0, 0, r, C2, C1)
+        for lo, hi in ((0, P), (P, C2), (C2, C1)):
+            for r in range(PACK):
+                scatter_z(zw0, 0, r, lo, hi)
         grouped0 = placed([P, C1, PACK], BF16, "grouped0", AT_GROUPED0)
-        for r in (2, 0, 1, last):
+        for r in range(PACK):
             gradient(zw0, 0, ds0, grouped0, r)
 
         zw1 = [kept([P, T], F32, "zw1_%d" % r) for r in range(last)] + [placed([P, T], F32, "zw1_last", AT_ZW1_LAST)]
-        scatter_z(zw1, 1, 1, 0, C2)
+        for r in (1, 2):
+            scatter_z(zw1, 1, r, 0, C2)
         scatter_z(zw1, 1, 0, 0, C1)
-        scatter_z(zw1, 1, 2, 0, C1)
+        scatter_z(zw1, 1, 2, C2, C1)
         second_product(0, grouped0, kept([P, C1], U32, "codes0", "before_quantize0"))
         scatter_z(zw1, 1, 1, C2, C1)
         scatter_z(zw1, 1, last, 0, C1)

@@ -97,7 +97,7 @@ def tile_moe_hib_silu_kernel(tc, dy_words, dy_scales, wet_words, wet_scales, wgt
         first_sc = placed([P, PASSES, H], U8, "first_sc", AT_FIRST_SC)
         gs = [kept([P, T], U8, "gs0"), placed([P, T], U8, "gs1", AT_GS1)]
         nc.gpsimd.memset(dys[:].bitcast(I32), 0)
-        nc.gpsimd.memset(zeros[:, 0:P], 0.0)
+        nc.vector.memset(zeros[:, 0:P], 0.0)
         nc.gpsimd.affine_select(out=ident[:], in_=zeros[:, 0:P], compare_op=ALU.not_equal, fill=1.0, base=0, pattern=[[-1, P]], channel_multiplier=1)
         unread = kept([P, 1], F32, "unread")
         nc.scalar.activation(unread[:], ident[:, 0:1], ACT.Sigmoid)
@@ -211,6 +211,9 @@ def tile_moe_hib_silu_kernel(tc, dy_words, dy_scales, wet_words, wet_scales, wgt
                     lhsT=wgt[:, f, 2 * P * c:2 * P * (c + 1)].bitcast(FP4X4), lhsT_scale=wgt_sc[:, f, P * c:P * (c + 1)],
                     rhs=codes[:].bitcast(FP8X4), rhs_scale=scales[:],
                     start=True, stop=True)
+                if (f, c) == (0, last):
+                    nc.scalar.activation(dxs[f][:, c, 0:P], acc2[:, 0:P], ACT.Copy)
+                    return acc2
                 nc.scalar.activation(dxs[f][:, c, :], acc2[:], ACT.Copy)
 
         def scatter_dx(ow, f, c):
@@ -259,8 +262,9 @@ def tile_moe_hib_silu_kernel(tc, dy_words, dy_scales, wet_words, wet_scales, wgt
             scatter_z(zw1, 1, r, 0, C2)
         scatter_z(zw1, 1, 0, 0, C1)
         scatter_z(zw1, 1, 2, C2, C1)
-        second_product(0, grouped0, kept([P, C1], U32, "codes0", "before_quantize0"))
-        scatter_z(zw1, 1, 1, C2, C1)
+        scatter_z(zw1, 1, 1, C2, C2 + P)
+        held = second_product(0, grouped0, kept([P, C1], U32, "codes0", "before_quantize0"))
+        scatter_z(zw1, 1, 1, C2 + P, C1)
         scatter_z(zw1, 1, last, 0, C1)
         ds1 = placed([P, PACK, C1], F32, "ds1", AT_DS1)
         grouped1 = kept([P, C1, PACK], BF16, "grouped1")
@@ -269,11 +273,14 @@ def tile_moe_hib_silu_kernel(tc, dy_words, dy_scales, wet_words, wet_scales, wgt
         for r in (0, 2, 1, last):
             gradient(zw1, 1, ds1, grouped1, r)
 
-        ow = [kept([P, T], F32, "ow%d" % c) for c in range(last)] + [placed([P, T], F32, "ow_last", AT_DS1 + 4 * KIB)]
+        dx_late = placed([P, C1 - P], F32, "dx_late", AT_DS1 + 4 * KIB)
+        nc.scalar.activation(dx_late[:], held[:, P:], ACT.Copy)
+        ow = [kept([P, T], F32, "ow%d" % c) for c in range(PACK)]
         for c in range(last):
             scatter_dx(ow, 0, c)
+        nc.vector.tensor_copy(ow[last][:].indirect(offs_t[:, columns(0, P)]), dxs[0][:, last, 0:P])
         second_product(1, grouped1, kept([P, C1], U32, "codes1"))
-        scatter_dx(ow, 0, last)
+        nc.vector.tensor_copy(ow[last][:].indirect(offs_t[:, columns(P, C1)]), dx_late[:])
         for c in range(K // P):
             scatter_dx(ow, 1, c)
             nc.sync.dma_start(out[c * P:(c + 1) * P, :], ow[c][:])

@@ -1,6 +1,7 @@
 from contextlib import ExitStack
 
 import concourse.mybir as mybir
+from concourse.masks import make_identity
 
 K, T, G, C1, E, C2, H, N = 512, 1024, 2, 512, 4, 256, 512, 1024
 FLOPS = 2 * T * N * H + 2 * T * H * K
@@ -22,34 +23,7 @@ PAIR = 2
 PASSES = N // (P * PACK)
 LIST = 16
 QUADS = 4
-SPARE = 352
-
-KIB = 1024
-LAP = 64
-AT_WORDS = 0
-AT_WET_REST = AT_WORDS + 4 * KIB + LAP
-AT_ZEROS = AT_WORDS + 8 * KIB - LAP
-AT_WET_FIRST = AT_WORDS + 8 * KIB
-AT_LATE_SC = AT_WET_FIRST + 2 * KIB
-AT_A0_SECOND = AT_LATE_SC + 3 * KIB
-AT_GATE = AT_A0_SECOND - KIB // 4
-AT_A0_FIRST = AT_A0_SECOND + 4 * KIB
-AT_SIG1 = AT_A0_FIRST + LAP - 8 * KIB
-AT_GS1 = AT_A0_FIRST + 4 * KIB
-AT_SILU1 = AT_GS1 - LAP
-AT_FIRST_SC = AT_GS1 + KIB
-AT_WET_SECOND = AT_FIRST_SC + KIB - LAP
-ZEROS_BYTES = AT_FIRST_SC + LAP - AT_ZEROS
-AT_A1 = AT_SILU1 + 8 * KIB
-AT_LEAD = AT_A1
-AT_GROUPED0 = AT_A1 + 8 * KIB
-AT_DS1 = AT_GROUPED0 + 4 * KIB - LAP
-AT_REST0 = AT_DS1 + 8 * KIB
-AT_ZT1 = AT_REST0 + 4 * KIB - LAP
-AT_ZT0 = AT_ZT1 + KIB
-AT_ZT3 = AT_ZT1 + 2 * KIB
-AT_DS0 = AT_ZT3 + 2 * KIB - LAP
-AT_ZW1_LAST = AT_DS0
+BLOCKS = T // P
 
 
 def tile_moe_hib_silu_kernel(tc, dy_words, dy_scales, wet_words, wet_scales, wgt_words, wgt_scales, a, gate, offs, offs2, dst, out):
@@ -57,15 +31,13 @@ def tile_moe_hib_silu_kernel(tc, dy_words, dy_scales, wet_words, wet_scales, wgt
     with ExitStack() as ctx:
         lists = ctx.enter_context(tc.tile_pool(name="lists", bufs=1))
         keep = ctx.enter_context(tc.tile_pool(name="keep", bufs=1))
-        chain = ctx.enter_context(tc.tile_pool(name="chain", bufs=1))
-        ps1 = ctx.enter_context(tc.psum_pool(name="ps1", bufs=1))
-        ps2 = ctx.enter_context(tc.psum_pool(name="ps2", bufs=4))
-
-        def placed(shape, dtype, name, at):
-            return chain.tile(shape, dtype, name=name, offset=at, align_bytes=64)
+        ps = ctx.enter_context(tc.psum_pool(name="ps", bufs=1))
 
         def kept(shape, dtype, name, tag=None):
             return keep.tile(shape, dtype, name=name, tag=tag or name, align_bytes=64)
+
+        def bank(shape, name, n):
+            return ps.tile(shape, F32, name=name, tag="bank%d" % n)
 
         def load_words(tile, words):
             nc.sync.dma_start(tile.bitcast(I32), words.bitcast(I32))
@@ -79,208 +51,201 @@ def tile_moe_hib_silu_kernel(tc, dy_words, dy_scales, wet_words, wet_scales, wgt
 
         a_rows = a.rearrange("(p r) j -> p r j", r=PACK)
         wet_rows = wet_words.rearrange("e s p c -> p (e s) c")
-        pairs = [slice(PAIR * h, PAIR * (h + 1)) for h in range(PACK // PAIR)]
-        pairs1 = [slice(0, PACK, 2), slice(1, PACK, 2)]
-        last = PACK - 1
+        wet_sc_rows = wet_scales.rearrange("e s b i -> (e s) b i")
+        dy_rows = dy_words.rearrange("s p t d -> p s (t d)")
+
+        first_sc = kept([P, PASSES, H], U8, "first_sc")
+        late_sc = kept([P, (E - 1) * PASSES, H], U8, "late_sc")
+        wgt_sc = kept([P, G, K], U8, "wgt_sc")
+        dys = kept([P, T], U8, "dys")
+        gs = [kept([P, PASSES, C1], U8, "gs%d" % f) for f in range(G)]
+        ident = kept([P, P], F32, "ident")
+        nc.gpsimd.memset(first_sc[:].bitcast(I32), 0)
+        nc.gpsimd.memset(dys[32:64, :].bitcast(I32), 0)
+        nc.gpsimd.memset(dys[64:P, :].bitcast(I32), 0)
+        nc.gpsimd.memset(gs[0][:].bitcast(I32), 0)
+        make_identity(nc, ident[:])
+        nc.gpsimd.memset(late_sc[:].bitcast(I32), 0)
+        nc.gpsimd.memset(gs[1][:].bitcast(I32), 0)
+        nc.gpsimd.memset(wgt_sc[:].bitcast(I32), 0)
 
         dst_t = lists.tile([P, T // LIST], U16, name="dst_t")
         offs2_t = lists.tile([P, T // LIST], U16, name="offs2_t")
         offs_t = lists.tile([P, T // LIST], U16, name="offs_t")
         nc.sync.dma_start(dst_t[:], dst)
-        nc.sync.dma_start(offs2_t[:], offs2)
-        nc.sync.dma_start(offs_t[:], offs)
+        nc.sync.dma_start(dys[0:32, :].bitcast(I32), dy_scales.rearrange("s r t -> r s t").bitcast(I32))
 
-        dys = kept([P, T + SPARE], U8, "dys")
-        zeros = placed([P, ZEROS_BYTES // 4], F32, "zeros", AT_ZEROS)
-        ident = kept([P, P], F32, "ident")
-        gate_rows = placed([P, P], F32, "gate_rows", AT_GATE)
-        first_sc = placed([P, PASSES, H], U8, "first_sc", AT_FIRST_SC)
-        gs = [kept([P, T], U8, "gs0"), placed([P, T], U8, "gs1", AT_GS1)]
-        nc.gpsimd.memset(dys[:].bitcast(I32), 0)
-        nc.vector.memset(zeros[:, 0:P], 0.0)
-        nc.gpsimd.affine_select(out=ident[:], in_=zeros[:, 0:P], compare_op=ALU.not_equal, fill=1.0, base=0, pattern=[[-1, P]], channel_multiplier=1)
-        unread = kept([P, 1], F32, "unread")
-        nc.scalar.activation(unread[:], ident[:, 0:1], ACT.Sigmoid)
-        nc.gpsimd.memset(first_sc[:].bitcast(I32), 0)
-        nc.gpsimd.memset(gate_rows[:], 0.0)
-        nc.gpsimd.memset(gs[1][:].bitcast(I32), 0)
+        av = [[kept([P, PAIR, C1], F32, "a%d_%d" % (f, h)) for h in range(2)] for f in range(G)]
+        sg = [[kept([P, PAIR, C1], F32, "sg%d_%d" % (f, h)) for h in range(2)] for f in range(G)]
 
-        for q in range(QUADS):
-            nc.sync.dma_start(dys[32 * q:32 * q + 8, 0:T].bitcast(I32), dy_scales[:, 4 * q:4 * q + 4, :].bitcast(I32))
-        dyw = placed([P, PASSES, T], I32, "dyw", AT_WORDS)
-        load_words(dyw[:], dy_words.rearrange("s p t d -> p s (t d)"))
-        wet_first = placed([P, PASSES, 2 * H], U8, "wet_first", AT_WET_FIRST)
-        load_words(wet_first[:], wet_rows[:, 0:PASSES, :])
-        nc.sync.dma_start(gate_rows[0:T // P, :], gate[0:1, :].rearrange("c (b p) -> (c b) p", p=P))
-        wet_sc_rows = wet_scales.rearrange("e s b i -> (e s) b i")
+        def load_a(f, h):
+            nc.sync.dma_start(av[f][h][:], a_rows[:, PAIR * h:PAIR * (h + 1), f * C1:(f + 1) * C1])
+
+        def sigmoid(f, h):
+            nc.scalar.activation(sg[f][h][:], av[f][h][:], ACT.Sigmoid)
+
+        load_a(0, 0)
+        dyw = [kept([P, T], I32, "dyw%d" % s) for s in range(PASSES)]
+        for s in range(PASSES):
+            load_words(dyw[s][:], dy_rows[:, s, :])
+        wet_t = [kept([P, PASSES, 2 * H], U8, "wet0"), kept([P, PASSES, 2 * H], U8, "wet1"), kept([P, 2 * PASSES, 2 * H], U8, "wet23")]
+        wet = (wet_t[0][:], wet_t[1][:], wet_t[2][:, 0:PASSES, :], wet_t[2][:, PASSES:, :])
+        wet_sc = [first_sc[:]] + [late_sc[:, PASSES * e:PASSES * (e + 1), :] for e in range(E - 1)]
+        load_words(wet_t[0][:], wet_rows[:, 0:PASSES, :])
         load_scales(first_sc, wet_sc_rows[0:PASSES])
+        gate_rows = kept([P, P], F32, "gate_rows")
+        nc.sync.dma_start(gate_rows[:], gate[0:P // BLOCKS, :].rearrange("x (b c) -> (x b) c", c=P))
 
-        gate_col = kept([P, T // P], F32, "gate_col")
-        gate_ps = ps2.tile([P, C1], F32, name="acc2")
-        nc.tensor.transpose(gate_ps[:, 0:P], gate_rows[:], ident[:])
-        nc.scalar.activation(gate_col[:], gate_ps[:, 0:T // P], ACT.Copy)
+        picked = [kept([P, C1], U8, "picked%d" % f) for f in range(G)]
 
-        a0 = [placed([P, PAIR, C1], F32, "a0_first", AT_A0_FIRST), placed([P, PAIR, C1], F32, "a0_second", AT_A0_SECOND)]
-        nc.sync.dma_start(a0[0][:], a_rows[:, pairs[0], 0:C1])
+        def gather_scales(f):
+            nc.vector.tensor_copy(picked[f][:], dys[:].indirect(dst_t[:, columns(f * C1, (f + 1) * C1)]))
 
-        nc.vector.tensor_copy(gs[0][:], dys[:].indirect(dst_t[:]))
-        for q in range(QUADS):
-            nc.sync.dma_start(gs[1][32 * q:32 * q + 4, :].bitcast(I32), gs[0][32 * q + 4:32 * q + 8, :].bitcast(I32))
-
+        def move_scales(f):
+            for q in range(QUADS):
+                nc.sync.dma_start(gs[f][32 * q:32 * q + 4].bitcast(I32), picked[f][8 * q:8 * q + 8, :].bitcast(I32))
 
         gw = {}
-        for lo, hi in ((0, C2), (C2, T)):
-            for s in range(PASSES):
-                gw[s, lo] = kept([P, hi - lo], U32, "gw%d_%d" % (s, lo))
-                nc.vector.tensor_copy(gw[s, lo][:], dyw[:, s, :].bitcast(U32).indirect(dst_t[:, columns(lo, hi)]))
 
-        wet_second = placed([P, PASSES, 2 * H], U8, "wet_second", AT_WET_SECOND)
-        nc.sync.dma_start(a0[1][:], a_rows[:, pairs[1], 0:C1])
-        late_sc = placed([P, (E - 1) * PASSES, H], U8, "late_sc", AT_LATE_SC)
-        nc.gpsimd.memset(late_sc[:].bitcast(I32), 0)
+        def gather_words(s, lo, hi):
+            tile = kept([P, hi - lo], U32, "gw%d_%d" % (s, lo))
+            nc.vector.tensor_copy(tile[:], dyw[s][:].bitcast(U32).indirect(dst_t[:, columns(lo, hi)]))
+            for b in range(lo // P, hi // P):
+                gw[s, b] = tile[:, b * P - lo:(b + 1) * P - lo]
+
+        gather_scales(0)
+        move_scales(0)
+        gather_scales(1)
+        gather_words(0, 0, C1)
+        gather_words(1, 0, C2)
+        gather_words(1, C2, C1)
+        gather_words(0, C1, T)
+        gather_words(1, C1, T)
+
+        load_a(0, 1)
+        load_words(wet_t[1][:], wet_rows[:, PASSES:2 * PASSES, :])
         load_scales(late_sc, wet_sc_rows[PASSES:])
-        wet_sc = [first_sc[:]] + [late_sc[:, PASSES * e:PASSES * (e + 1), :] for e in range(E - 1)]
-        wet_rest = placed([P, 2 * PASSES, 2 * H], U8, "wet_rest", AT_WET_REST)
-        wet = (wet_first[:], wet_second[:], wet_rest[:, 0:PASSES, :], wet_rest[:, PASSES:, :])
+        move_scales(1)
+        load_a(1, 0)
+        load_a(1, 1)
+        load_words(wet_t[2][:], wet_rows[:, 2 * PASSES:, :])
+        nc.sync.dma_start(offs2_t[:], offs2)
+        nc.sync.dma_start(offs_t[:], offs)
+        wgt = kept([P, G, 2 * K], U8, "wgt")
+        load_words(wgt[:], wgt_words.rearrange("f s p c -> p (f s) c"))
+        load_scales(wgt_sc, wgt_scales.rearrange("f s b k -> (f s) b k"))
 
-        zs0 = kept([P, PACK, C1], F32, "zs0")
-        zs1 = [kept([P, 1, C1], F32, "zs1_first", "before_quantize0"), kept([P, last, C1], F32, "zs1_rest")]
-        dxs = [placed([P, K // P, C1], F32, "dxs0", AT_SILU1), kept([P, K // P, C1], F32, "dxs1")]
+        sigmoid(0, 0)
+        gate_col = kept([P, BLOCKS], F32, "gate_col")
+        gate_ps = bank([P, P], "gate_ps", 7)
+        nc.tensor.transpose(gate_ps[:], gate_rows[:], ident[:])
+        nc.scalar.activation(gate_col[:], gate_ps[:, 0:BLOCKS], ACT.Copy, scale=-1.0)
 
-        def weigh(b, acc, zt, planes):
-            nc.scalar.activation(zt[:, planes, :], acc[:].rearrange("m (p r) -> m r p", r=PACK)[:, planes, :], ACT.Copy, scale=gate_col[:, b:b + 1])
+        zs = [kept([P, PACK, C1], F32, "zs%d" % f) for f in range(G)]
 
-        def turn(b, zt, planes, turned):
-            f, u = divmod(b * P, C1)
-            for r in range(planes.start, planes.stop):
-                nc.tensor.transpose(turned[:, r, :], zt[:, r, :], ident[:])
-            if f == 0:
-                nc.scalar.activation(zs0[:, planes, u:u + P], turned[:, planes, :], ACT.Copy)
-            else:
-                nc.scalar.activation(zs1[0][:, :, u:u + P], turned[:, 0:1, :], ACT.Copy)
-                nc.scalar.activation(zs1[1][:, :, u:u + P], turned[:, 1:PACK, :], ACT.Copy)
-
-        def expert(e, zt, lead=None):
+        def expert(e):
             blocks = (2 * e, 2 * e + 1)
             f = e // 2
-            lo = 0 if e == 0 else C2
-            acc = [ps1.tile([P, H], F32, name="acc", tag="bank%d" % (2 * f + n)) for n in range(2)]
+            acc = {b: bank([P, H], "acc", b % 4) for b in blocks}
             for s in range(PASSES):
-                for n, b in enumerate(blocks):
+                for b in blocks:
+                    u = b * P - f * C1
                     nc.tensor.matmul_mx(
-                        out=acc[n][:],
-                        lhsT=gw[s, lo][:, b * P - lo:(b + 1) * P - lo].bitcast(FP8X4), lhsT_scale=gs[s][:, b * P:(b + 1) * P],
+                        out=acc[b][:],
+                        lhsT=gw[s, b].bitcast(FP8X4), lhsT_scale=gs[f][:, s, u:u + P],
                         rhs=wet[e][:, s, :].bitcast(FP4X4), rhs_scale=wet_sc[e][:, s, :],
                         start=(s == 0), stop=(s == PASSES - 1))
-            planes = [slice(0 if lead is None else 1, PACK), slice(0, PACK)]
-            if lead is not None:
-                weigh(blocks[0], acc[0], lead, slice(0, 1))
-            weigh(blocks[0], acc[0], zt[0], planes[0])
-            if lead is not None:
-                turn(blocks[0], lead, slice(0, 1), ps2.tile([P, PACK, P], F32, name="acc2"))
-            turned = [ps1.tile([P, PACK, P], F32, name="turned", tag="bank%d" % (2 * (1 - f) + n)) for n in range(2)]
-            if lead is not None:
-                turn(blocks[0], zt[0], planes[0], turned[0])
-            weigh(blocks[1], acc[1], zt[1], planes[1])
-            if lead is None:
-                turn(blocks[0], zt[0], planes[0], turned[0])
-            turn(blocks[1], zt[1], planes[1], turned[1])
+            zt = {b: kept([P, PACK, P], F32, "zt", "zt%d" % (b % 4)) for b in blocks}
+            for b in blocks:
+                nc.scalar.activation(zt[b][:], acc[b][:].rearrange("m (p r) -> m r p", r=PACK), ACT.Copy, scale=gate_col[:, b:b + 1])
+            for b in blocks:
+                u = b * P - f * C1
+                turned = bank([P, PACK, P], "turned", 4 + b % 4)
+                for r in range(PACK):
+                    nc.tensor.transpose(turned[:, r, :], zt[b][:, r, :], ident[:])
+                nc.scalar.activation(zs[f][:, :, u:u + P], turned[:], ACT.Copy)
 
-        def in_dead_a(tile):
-            return [tile[:, n, :].rearrange("m (r p) -> m r p", r=PACK) for n in range(2)]
+        def derivative(f):
+            for h in range(2):
+                nc.vector.scalar_tensor_tensor(av[f][h][:], sg[f][h][:], 1.0, av[f][h][:], ALU.subtract, ALU.mult)
+            for h in range(2):
+                nc.vector.scalar_tensor_tensor(sg[f][h][:], av[f][h][:], 1.0, sg[f][h][:], ALU.subtract, ALU.mult)
 
-        def rest_by_sigmoid(to, a_pair):
-            nc.scalar.activation(to[:], a_pair[:], ACT.Sigmoid, scale=-1.0)
-            nc.gpsimd.tensor_tensor(to[:], to[:], a_pair[:], ALU.mult)
-            nc.gpsimd.tensor_scalar(to[:], to[:], 1.0, 1.0, ALU.mult, ALU.add)
+        expert(0)
+        sigmoid(0, 1)
+        expert(1)
+        sigmoid(1, 0)
+        sigmoid(1, 1)
+        expert(2)
+        expert(3)
+        derivative(0)
+        derivative(1)
 
-        def scatter_z(zw, f, r, lo, hi):
-            sums = zs0[:, r, lo:hi] if f == 0 else zs1[min(r, 1)][:, max(r - 1, 0), lo:hi]
-            nc.vector.tensor_copy(zw[r][:].indirect(offs2_t[:, columns(f * C1 + lo, f * C1 + hi)]), sums)
+        def by_vector(window, offsets, lo, hi, values):
+            nc.vector.tensor_copy(window[:].indirect(offsets[:, columns(lo, hi)]), values)
 
-        def gradient(zw, f, ds, grouped, r):
-            nc.gpsimd.tensor_tensor(grouped[:, :, r], zw[r][:, f * C1:(f + 1) * C1], ds[:, r, :], ALU.mult)
+        def by_scalar(window, offsets, lo, hi, values):
+            nc.scalar.activation(window[:].indirect(offsets[:, columns(lo, hi)]), values, ACT.Copy)
 
-        def second_product(f, grouped, codes):
+        def gradient(f, zw, grouped):
+            for r in (0, 2, 3, 1):
+                nc.gpsimd.tensor_tensor(grouped[:, :, r], zw[r][:, f * C1:(f + 1) * C1], sg[f][r // PAIR][:, r % PAIR, :], ALU.mult)
+
+        def second_product(f, grouped):
+            codes = kept([P, C1], U32, "codes%d" % f)
             scales = kept([P, C1], U8, "scales%d" % f)
             nc.vector.quantize_mx(out=codes[:].bitcast(FP8X4), scales=scales[:], in_=grouped[:].rearrange("p j r -> p (j r)"))
-            for c in range(K // P):
-                acc2 = ps2.tile([P, C1], F32, name="acc2")
+            acc2 = [bank([P, C1], "acc2", 4 * f + c) for c in range(K // P)]
+            for c in (2, 0, 3, 1):
                 nc.tensor.matmul_mx(
-                    out=acc2[:],
+                    out=acc2[c][:],
                     lhsT=wgt[:, f, 2 * P * c:2 * P * (c + 1)].bitcast(FP4X4), lhsT_scale=wgt_sc[:, f, P * c:P * (c + 1)],
                     rhs=codes[:].bitcast(FP8X4), rhs_scale=scales[:],
                     start=True, stop=True)
-                if (f, c) == (0, last):
-                    nc.scalar.activation(dxs[f][:, c, 0:P], acc2[:, 0:P], ACT.Copy)
-                    return acc2
-                nc.scalar.activation(dxs[f][:, c, :], acc2[:], ACT.Copy)
+            return acc2
 
-        def scatter_dx(ow, f, c):
-            nc.vector.tensor_copy(ow[c][:].indirect(offs_t[:, columns(f * C1, (f + 1) * C1)]), dxs[f][:, c, :])
+        zw0 = [kept([P, T], F32, "zw0_0", "a1_0"), kept([P, T], F32, "zw0_1", "a1_1"), kept([P, C1], F32, "zw0_2", "zt2"), kept([P, C1], F32, "zw0_3", "zt3")]
+        for r in (0, 1):
+            by_vector(zw0[r], offs2_t, 0, C1, zs[0][:, r, :])
+        for lo in (0, C2):
+            for r in (2, 3):
+                by_scalar(zw0[r], offs2_t, lo, lo + C2, zs[0][:, r, lo:lo + C2])
+        grouped0 = kept([P, C1, PACK], BF16, "grouped0", "grouped")
+        gradient(0, zw0, grouped0)
 
-        rest0 = [kept([P, PAIR, C1], F32, "rest0_first")]
-        rest_by_sigmoid(rest0[0], a0[0])
-        lead = placed([P, 1, P], F32, "lead", AT_LEAD)
-        expert(0, [placed([P, PACK, P], F32, "zt0", AT_ZT0), placed([P, PACK, P], F32, "zt1", AT_ZT1)], lead)
-        load_words(wet_second[:], wet_rows[:, PASSES:2 * PASSES, :])
-        load_words(wet_rest[:], wet_rows[:, 2 * PASSES:, :])
-        a1 = placed([P, PACK, C1], F32, "a1", AT_A1)
-        nc.sync.dma_start(a1[:], a_rows[:, :, C1:])
-        wgt = kept([P, G, 2 * K], U8, "wgt", "gw1_0")
-        load_words(wgt[:], wgt_words.rearrange("f s p c -> p (f s) c"))
-        wgt_sc = kept([P, G, K], U8, "wgt_sc", "gw0_0")
-        nc.gpsimd.memset(wgt_sc[:].bitcast(I32), 0)
-        load_scales(wgt_sc, wgt_scales.rearrange("f s b k -> (f s) b k"))
-        rest0.append(placed([P, PAIR, C1], F32, "rest0_second", AT_REST0))
-        rest_by_sigmoid(rest0[1], a0[1])
-        expert(1, [kept([P, PACK, P], F32, "zt2"), placed([P, PACK, P], F32, "zt3", AT_ZT3)])
-        ds0 = placed([P, PACK, C1], F32, "ds0", AT_DS0)
-        for h in range(2):
-            nc.scalar.activation(ds0[:, pairs[h], :], a0[h][:], ACT.Sigmoid)
-            nc.gpsimd.tensor_tensor(ds0[:, pairs[h], :], ds0[:, pairs[h], :], rest0[h][:], ALU.mult)
-        expert(2, in_dead_a(a0[1]))
-        expert(3, in_dead_a(a0[0]))
-        sig1 = placed([P, PACK, C1], F32, "sig1", AT_SIG1)
-        nc.scalar.activation(sig1[:], a1[:], ACT.Sigmoid)
-        silu1 = placed([P, PACK, C1], F32, "silu1", AT_SILU1)
-        rest1 = kept([P, PACK, C1], F32, "rest1")
-        for pair in pairs1:
-            nc.scalar.activation(silu1[:, pair, :], a1[:, pair, :], ACT.Silu, scale=-1.0)
-            nc.scalar.activation(rest1[:, pair, :], silu1[:, pair, :], ACT.Copy, scale=-1.0, bias=1.0)
+        zw1 = [kept([P, T], F32, "zw1_0"), kept([P, T], F32, "zw1_1", "a1_1"), kept([P, T], F32, "zw1_2"), kept([P, T], F32, "zw1_3")]
+        by_vector(zw1[0], offs2_t, C1, T, zs[1][:, 0, :])
+        for lo in (0, C2):
+            for r in (2, 3):
+                by_scalar(zw1[r], offs2_t, C1 + lo, C1 + lo + C2, zs[1][:, r, lo:lo + C2])
+        acc2 = second_product(0, grouped0)
+        by_vector(zw1[1], offs2_t, C1, T, zs[1][:, 1, :])
+        grouped1 = kept([P, C1, PACK], BF16, "grouped1", "grouped")
+        gradient(1, zw1, grouped1)
 
-        zw0 = [kept([P, T], F32, "zw0_%d" % r) for r in range(PACK)]
-        for lo, hi in ((0, P), (P, C2), (C2, C1)):
-            for r in range(PACK):
-                scatter_z(zw0, 0, r, lo, hi)
-        grouped0 = placed([P, C1, PACK], BF16, "grouped0", AT_GROUPED0)
-        for r in range(PACK):
-            gradient(zw0, 0, ds0, grouped0, r)
+        ow = [kept([P, T], F32, "ow0"), kept([P, T], F32, "ow1", "a1_1"), kept([P, T], F32, "ow2"), kept([P, T], F32, "ow3")]
 
-        zw1 = [kept([P, T], F32, "zw1_%d" % r) for r in range(last)] + [placed([P, T], F32, "zw1_last", AT_ZW1_LAST)]
-        for r in (1, 2):
-            scatter_z(zw1, 1, r, 0, C2)
-        scatter_z(zw1, 1, 0, 0, C1)
-        scatter_z(zw1, 1, 2, C2, C1)
-        scatter_z(zw1, 1, 1, C2, C2 + P)
-        held = second_product(0, grouped0, kept([P, C1], U32, "codes0", "before_quantize0"))
-        scatter_z(zw1, 1, 1, C2 + P, C1)
-        scatter_z(zw1, 1, last, 0, C1)
-        ds1 = placed([P, PACK, C1], F32, "ds1", AT_DS1)
-        grouped1 = kept([P, C1, PACK], BF16, "grouped1")
-        for pair in pairs1:
-            nc.gpsimd.tensor_tensor(ds1[:, pair, :], sig1[:, pair, :], rest1[:, pair, :], ALU.mult)
-        for r in (0, 2, 1, last):
-            gradient(zw1, 1, ds1, grouped1, r)
+        def leave(f, acc2):
+            dxs = [kept([P, C1], F32, "dxs%d_%d" % (f, c)) for c in range(K // P)]
+            for c in (0, 1):
+                nc.vector.tensor_copy(dxs[c][:], acc2[c][:])
+            for c in (2, 3):
+                nc.scalar.activation(dxs[c][:], acc2[c][:], ACT.Copy)
+            return dxs
 
-        dx_late = placed([P, C1 - P], F32, "dx_late", AT_DS1 + 4 * KIB)
-        nc.scalar.activation(dx_late[:], held[:, P:], ACT.Copy)
-        ow = [kept([P, T], F32, "ow%d" % c) for c in range(PACK)]
-        for c in range(last):
-            scatter_dx(ow, 0, c)
-        nc.vector.tensor_copy(ow[last][:].indirect(offs_t[:, columns(0, P)]), dxs[0][:, last, 0:P])
-        second_product(1, grouped1, kept([P, C1], U32, "codes1"))
-        nc.vector.tensor_copy(ow[last][:].indirect(offs_t[:, columns(P, C1)]), dx_late[:])
-        for c in range(K // P):
-            scatter_dx(ow, 1, c)
+        def scalar_share(f, dxs):
+            for lo in (0, C2):
+                for c in (2, 3):
+                    by_scalar(ow[c], offs_t, f * C1 + lo, f * C1 + lo + C2, dxs[c][:, lo:lo + C2])
+
+        dxs = leave(0, acc2)
+        by_vector(ow[0], offs_t, 0, C1, dxs[0][:])
+        scalar_share(0, dxs)
+        acc2 = second_product(1, grouped1)
+        by_vector(ow[1], offs_t, 0, C1, dxs[1][:])
+        dxs = leave(1, acc2)
+        scalar_share(1, dxs)
+        for c in (0, 1):
+            by_vector(ow[c], offs_t, C1, T, dxs[c][:])
+        for c in (0, 2, 1, 3):
             nc.sync.dma_start(out[c * P:(c + 1) * P, :], ow[c][:])

@@ -1,7 +1,6 @@
 from contextlib import ExitStack
 
 import concourse.mybir as mybir
-from concourse.masks import make_identity
 
 K, T, G, C1, E, C2, H, N = 512, 1024, 2, 512, 4, 256, 512, 1024
 FLOPS = 2 * T * N * H + 2 * T * H * K
@@ -23,18 +22,30 @@ PAIR = 2
 PASSES = N // (P * PACK)
 LIST = 16
 QUADS = 4
-BLOCKS = T // P
+KIB = 1024
+AT_A01 = 0
+AT_LATE = 4 * KIB
+AT_DYS = AT_LATE - KIB // 2
+AT_DYW1 = AT_LATE + 6 * KIB
+AT_ZN23 = AT_DYW1 + 4 * KIB
+AT_GROUPED = AT_ZN23 - 2 * KIB
+AT_WINDOW = [AT_ZN23 + 8 * KIB, AT_ZN23 + 12 * KIB]
+AT_GATE = AT_WINDOW[1] - 2 * KIB
 
 
 def tile_moe_hib_silu_kernel(tc, dy_words, dy_scales, wet_words, wet_scales, wgt_words, wgt_scales, a, gate, offs, offs2, dst, out):
     nc = tc.nc
     with ExitStack() as ctx:
         lists = ctx.enter_context(tc.tile_pool(name="lists", bufs=1))
+        chain = ctx.enter_context(tc.tile_pool(name="chain", bufs=1))
         keep = ctx.enter_context(tc.tile_pool(name="keep", bufs=1))
         ps = ctx.enter_context(tc.psum_pool(name="ps", bufs=1))
 
         def kept(shape, dtype, name, tag=None):
             return keep.tile(shape, dtype, name=name, tag=tag or name, align_bytes=64)
+
+        def placed(shape, dtype, name, at):
+            return chain.tile(shape, dtype, name=name, offset=at, align_bytes=64)
 
         def bank(shape, name, n):
             return ps.tile(shape, F32, name=name, tag="bank%d" % n)
@@ -54,20 +65,13 @@ def tile_moe_hib_silu_kernel(tc, dy_words, dy_scales, wet_words, wet_scales, wgt
         wet_sc_rows = wet_scales.rearrange("e s b i -> (e s) b i")
         dy_rows = dy_words.rearrange("s p t d -> p s (t d)")
 
-        first_sc = kept([P, PASSES, H], U8, "first_sc")
-        late_sc = kept([P, (E - 1) * PASSES, H], U8, "late_sc")
-        wgt_sc = kept([P, G, K], U8, "wgt_sc")
-        dys = kept([P, T], U8, "dys")
-        gs = [kept([P, PASSES, C1], U8, "gs%d" % f) for f in range(G)]
-        ident = kept([P, P], F32, "ident")
-        nc.gpsimd.memset(first_sc[:].bitcast(I32), 0)
+        first_sc = kept([P, E * PASSES, H], U8, "first_sc")
+        dys = chain.tile([P, T], U8, name="dys", offset=AT_DYS, align_bytes=64)
+        gs = kept([P, PASSES, T], U8, "gs")
+        nc.vector.memset(first_sc[:].bitcast(I32), 0)
         nc.gpsimd.memset(dys[32:64, :].bitcast(I32), 0)
         nc.gpsimd.memset(dys[64:P, :].bitcast(I32), 0)
-        nc.gpsimd.memset(gs[0][:].bitcast(I32), 0)
-        make_identity(nc, ident[:])
-        nc.gpsimd.memset(late_sc[:].bitcast(I32), 0)
-        nc.gpsimd.memset(gs[1][:].bitcast(I32), 0)
-        nc.gpsimd.memset(wgt_sc[:].bitcast(I32), 0)
+        nc.gpsimd.memset(gs[:].bitcast(I32), 0)
 
         dst_t = lists.tile([P, T // LIST], U16, name="dst_t")
         offs2_t = lists.tile([P, T // LIST], U16, name="offs2_t")
@@ -75,111 +79,96 @@ def tile_moe_hib_silu_kernel(tc, dy_words, dy_scales, wet_words, wet_scales, wgt
         nc.sync.dma_start(dst_t[:], dst)
         nc.sync.dma_start(dys[0:32, :].bitcast(I32), dy_scales.rearrange("s r t -> r s t").bitcast(I32))
 
-        av = [[kept([P, PAIR, C1], F32, "a%d_%d" % (f, h)) for h in range(2)] for f in range(G)]
-        sg = [[kept([P, PAIR, C1], F32, "sg%d_%d" % (f, h)) for h in range(2)] for f in range(G)]
+        av = {}
+        sg = {(f, h): kept([P, PAIR, C1], F32, "sg%d_%d" % (f, h)) for f in range(G) for h in range(2)}
 
-        def load_a(f, h):
-            nc.sync.dma_start(av[f][h][:], a_rows[:, PAIR * h:PAIR * (h + 1), f * C1:(f + 1) * C1])
+        def load_a(f, h, tile):
+            av[f, h] = tile
+            nc.sync.dma_start(av[f, h][:], a_rows[:, PAIR * h:PAIR * (h + 1), f * C1:(f + 1) * C1])
 
         def sigmoid(f, h):
-            nc.scalar.activation(sg[f][h][:], av[f][h][:], ACT.Sigmoid)
+            nc.scalar.activation(sg[f, h][:], av[f, h][:], ACT.Sigmoid)
 
-        load_a(0, 0)
-        dyw = [kept([P, T], I32, "dyw%d" % s) for s in range(PASSES)]
+        nc.sync.dma_start(offs2_t[:], offs2)
+        nc.sync.dma_start(offs_t[:], offs)
+        dyw = [kept([P, T], I32, "dyw0"), placed([P, T], I32, "dyw1", AT_DYW1)]
         for s in range(PASSES):
             load_words(dyw[s][:], dy_rows[:, s, :])
-        wet_t = [kept([P, PASSES, 2 * H], U8, "wet0"), kept([P, PASSES, 2 * H], U8, "wet1"), kept([P, 2 * PASSES, 2 * H], U8, "wet23")]
-        wet = (wet_t[0][:], wet_t[1][:], wet_t[2][:, 0:PASSES, :], wet_t[2][:, PASSES:, :])
-        wet_sc = [first_sc[:]] + [late_sc[:, PASSES * e:PASSES * (e + 1), :] for e in range(E - 1)]
-        load_words(wet_t[0][:], wet_rows[:, 0:PASSES, :])
-        load_scales(first_sc, wet_sc_rows[0:PASSES])
-        gate_rows = kept([P, P], F32, "gate_rows")
-        nc.sync.dma_start(gate_rows[:], gate[0:P // BLOCKS, :].rearrange("x (b c) -> (x b) c", c=P))
+        wet0 = kept([P, PASSES, 2 * H], U8, "wet0")
+        load_words(wet0[:], wet_rows[:, 0:PASSES, :])
+        load_scales(first_sc, wet_sc_rows)
+        load_a(0, 0, kept([P, PAIR, C1], F32, "a0_0"))
+        gate_t = placed([P, T], F32, "gate_t", AT_GATE)
+        nc.sync.dma_start(gate_t[:], gate)
 
-        picked = [kept([P, C1], U8, "picked%d" % f) for f in range(G)]
-
-        def gather_scales(f):
-            nc.vector.tensor_copy(picked[f][:], dys[:].indirect(dst_t[:, columns(f * C1, (f + 1) * C1)]))
-
-        def move_scales(f):
-            for q in range(QUADS):
-                nc.sync.dma_start(gs[f][32 * q:32 * q + 4].bitcast(I32), picked[f][8 * q:8 * q + 8, :].bitcast(I32))
+        picked = kept([P, T], U8, "picked")
+        for f in range(G):
+            nc.vector.tensor_copy(picked[:, f * C1:(f + 1) * C1], dys[:].indirect(dst_t[:, columns(f * C1, (f + 1) * C1)]))
+        for q in range(QUADS):
+            nc.sync.dma_start(gs[32 * q:32 * q + 4].bitcast(I32), picked[8 * q:8 * q + 8, :].bitcast(I32))
 
         gw = {}
 
         def gather_words(s, lo, hi):
             tile = kept([P, hi - lo], U32, "gw%d_%d" % (s, lo))
             nc.vector.tensor_copy(tile[:], dyw[s][:].bitcast(U32).indirect(dst_t[:, columns(lo, hi)]))
-            for b in range(lo // P, hi // P):
-                gw[s, b] = tile[:, b * P - lo:(b + 1) * P - lo]
+            for e in range(lo // C2, hi // C2):
+                gw[s, e] = tile[:, e * C2 - lo:(e + 1) * C2 - lo]
 
-        gather_scales(0)
-        move_scales(0)
-        gather_scales(1)
         gather_words(0, 0, C1)
         gather_words(1, 0, C2)
         gather_words(1, C2, C1)
         gather_words(0, C1, T)
         gather_words(1, C1, T)
 
-        load_a(0, 1)
-        load_words(wet_t[1][:], wet_rows[:, PASSES:2 * PASSES, :])
-        load_scales(late_sc, wet_sc_rows[PASSES:])
-        move_scales(1)
-        load_a(1, 0)
-        load_a(1, 1)
-        load_words(wet_t[2][:], wet_rows[:, 2 * PASSES:, :])
-        nc.sync.dma_start(offs2_t[:], offs2)
-        nc.sync.dma_start(offs_t[:], offs)
-        wgt = kept([P, G, 2 * K], U8, "wgt")
-        load_words(wgt[:], wgt_words.rearrange("f s p c -> p (f s) c"))
-        load_scales(wgt_sc, wgt_scales.rearrange("f s b k -> (f s) b k"))
+        load_a(0, 1, chain.tile([P, PAIR, C1], F32, name="a0_1", offset=AT_A01, align_bytes=64))
+        wet_sc = [first_sc[:, PASSES * e:PASSES * (e + 1), :] for e in range(E)]
+        wet_late = chain.tile([P, (E - 1) * PASSES, 2 * H], U8, name="wet_late", offset=AT_LATE, align_bytes=64)
+        load_words(wet_late[:], wet_rows[:, PASSES:, :])
+        wet = [wet0[:]] + [wet_late[:, PASSES * n:PASSES * (n + 1), :] for n in range(E - 1)]
+        load_a(1, 1, kept([P, PAIR, C1], F32, "a1_1", "dyw0"))
+        load_a(1, 0, placed([P, PAIR, C1], F32, "a1_0", AT_DYW1))
 
         sigmoid(0, 0)
-        gate_col = kept([P, BLOCKS], F32, "gate_col")
-        gate_ps = bank([P, P], "gate_ps", 7)
-        nc.tensor.transpose(gate_ps[:], gate_rows[:], ident[:])
-        nc.scalar.activation(gate_col[:], gate_ps[:, 0:BLOCKS], ACT.Copy, scale=-1.0)
 
         zs = [kept([P, PACK, C1], F32, "zs%d" % f) for f in range(G)]
 
-        def expert(e):
-            blocks = (2 * e, 2 * e + 1)
-            f = e // 2
-            acc = {b: bank([P, H], "acc", b % 4) for b in blocks}
-            for s in range(PASSES):
-                for b in blocks:
-                    u = b * P - f * C1
-                    nc.tensor.matmul_mx(
-                        out=acc[b][:],
-                        lhsT=gw[s, b].bitcast(FP8X4), lhsT_scale=gs[f][:, s, u:u + P],
-                        rhs=wet[e][:, s, :].bitcast(FP4X4), rhs_scale=wet_sc[e][:, s, :],
-                        start=(s == 0), stop=(s == PASSES - 1))
-            zt = {b: kept([P, PACK, P], F32, "zt", "zt%d" % (b % 4)) for b in blocks}
-            for b in blocks:
-                nc.scalar.activation(zt[b][:], acc[b][:].rearrange("m (p r) -> m r p", r=PACK), ACT.Copy, scale=gate_col[:, b:b + 1])
-            for b in blocks:
-                u = b * P - f * C1
-                turned = bank([P, PACK, P], "turned", 4 + b % 4)
-                for r in range(PACK):
-                    nc.tensor.transpose(turned[:, r, :], zt[b][:, r, :], ident[:])
-                nc.scalar.activation(zs[f][:, :, u:u + P], turned[:], ACT.Copy)
+        def regroup(zn, lo, hi):
+            f, u = divmod(lo, C1)
+            for c in range(H // P):
+                nc.sync.dma_start(zs[f][32 * c:32 * (c + 1), :, u:u + hi - lo], zn[:, c, :])
 
-        def derivative(f):
-            for h in range(2):
-                nc.vector.scalar_tensor_tensor(av[f][h][:], sg[f][h][:], 1.0, av[f][h][:], ALU.subtract, ALU.mult)
-            for h in range(2):
-                nc.vector.scalar_tensor_tensor(sg[f][h][:], av[f][h][:], 1.0, sg[f][h][:], ALU.subtract, ALU.mult)
+        def expert(e, zn):
+            for half in range(2):
+                acc = bank([P, 2, C2], "acc", 2 * e + half)
+                for n in range(2):
+                    c = 2 * half + n
+                    for s in range(PASSES):
+                        nc.tensor.matmul_mx(
+                            out=acc[:, n, :],
+                            lhsT=wet[e][:, s, 2 * P * c:2 * P * (c + 1)].bitcast(FP4X4), lhsT_scale=wet_sc[e][:, s, P * c:P * (c + 1)],
+                            rhs=gw[s, e].bitcast(FP8X4), rhs_scale=gs[:, s, e * C2:(e + 1) * C2],
+                            start=(s == 0), stop=(s == PASSES - 1))
+                weight = gate_t[:, e * C2:(e + 1) * C2].unsqueeze(1).to_broadcast([P, 2, C2])
+                nc.vector.scalar_tensor_tensor(zn[:, 2 * half:2 * half + 2, :], acc[:], -1.0, weight, ALU.mult, ALU.mult)
 
-        expert(0)
-        sigmoid(0, 1)
-        expert(1)
-        sigmoid(1, 0)
-        sigmoid(1, 1)
-        expert(2)
-        expert(3)
-        derivative(0)
-        derivative(1)
+        def derivative_on_vector(f, h):
+            u = [placed([P, C1], F32, "u%d_%d_%d" % (f, h, r), AT_GATE + 2 * KIB * r) for r in range(PAIR)]
+            for r in range(PAIR):
+                nc.vector.scalar_tensor_tensor(u[r][:], sg[f, h][:, r, :], 1.0, av[f, h][:, r, :], ALU.subtract, ALU.mult)
+            for r in range(PAIR):
+                nc.vector.scalar_tensor_tensor(sg[f, h][:, r, :], u[r][:], 1.0, sg[f, h][:, r, :], ALU.subtract, ALU.mult)
+
+        def derivative_on_gpsimd(f, h):
+            u = [kept([P, C1], F32, "u%d" % r) for r in range(PAIR)]
+            for r in range(PAIR):
+                nc.gpsimd.tensor_scalar(u[r][:], sg[f, h][:, r, :], 1.0, -1.0, ALU.mult, ALU.add)
+            for r in range(PAIR):
+                nc.gpsimd.tensor_tensor(u[r][:], u[r][:], av[f, h][:, r, :], ALU.mult)
+            for r in range(PAIR):
+                nc.gpsimd.tensor_scalar(u[r][:], u[r][:], 1.0, -1.0, ALU.mult, ALU.add)
+            for r in range(PAIR):
+                nc.gpsimd.tensor_tensor(sg[f, h][:, r, :], u[r][:], sg[f, h][:, r, :], ALU.mult)
 
         def by_vector(window, offsets, lo, hi, values):
             nc.vector.tensor_copy(window[:].indirect(offsets[:, columns(lo, hi)]), values)
@@ -187,16 +176,20 @@ def tile_moe_hib_silu_kernel(tc, dy_words, dy_scales, wet_words, wet_scales, wgt
         def by_scalar(window, offsets, lo, hi, values):
             nc.scalar.activation(window[:].indirect(offsets[:, columns(lo, hi)]), values, ACT.Copy)
 
-        def gradient(f, zw, grouped):
-            for r in (0, 2, 3, 1):
-                nc.gpsimd.tensor_tensor(grouped[:, :, r], zw[r][:, f * C1:(f + 1) * C1], sg[f][r // PAIR][:, r % PAIR, :], ALU.mult)
+        def scatter_z(by, zw, e, r):
+            f, u = divmod(e * C2, C1)
+            by(zw[r], offs2_t, e * C2, (e + 1) * C2, zs[f][:, r, u:u + C2])
+
+        def gradient(f, zw, grouped, planes):
+            for r in planes:
+                nc.gpsimd.tensor_tensor(grouped[:, :, r], zw[r][:, f * C1:(f + 1) * C1], sg[f, r // PAIR][:, r % PAIR, :], ALU.mult)
 
         def second_product(f, grouped):
             codes = kept([P, C1], U32, "codes%d" % f)
             scales = kept([P, C1], U8, "scales%d" % f)
             nc.vector.quantize_mx(out=codes[:].bitcast(FP8X4), scales=scales[:], in_=grouped[:].rearrange("p j r -> p (j r)"))
             acc2 = [bank([P, C1], "acc2", 4 * f + c) for c in range(K // P)]
-            for c in (2, 0, 3, 1):
+            for c in (0, 2, 1, 3):
                 nc.tensor.matmul_mx(
                     out=acc2[c][:],
                     lhsT=wgt[:, f, 2 * P * c:2 * P * (c + 1)].bitcast(FP4X4), lhsT_scale=wgt_sc[:, f, P * c:P * (c + 1)],
@@ -204,48 +197,65 @@ def tile_moe_hib_silu_kernel(tc, dy_words, dy_scales, wet_words, wet_scales, wgt
                     start=True, stop=True)
             return acc2
 
-        zw0 = [kept([P, T], F32, "zw0_0", "a1_0"), kept([P, T], F32, "zw0_1", "a1_1"), kept([P, C1], F32, "zw0_2", "zt2"), kept([P, C1], F32, "zw0_3", "zt3")]
-        for r in (0, 1):
-            by_vector(zw0[r], offs2_t, 0, C1, zs[0][:, r, :])
-        for lo in (0, C2):
-            for r in (2, 3):
-                by_scalar(zw0[r], offs2_t, lo, lo + C2, zs[0][:, r, lo:lo + C2])
-        grouped0 = kept([P, C1, PACK], BF16, "grouped0", "grouped")
-        gradient(0, zw0, grouped0)
+        derivative_on_gpsimd(0, 0)
+        sigmoid(0, 1)
+        sigmoid(1, 1)
+        sigmoid(1, 0)
+        for e in (0, 1):
+            zn = kept([P, H // P, C2], F32, "zn%d" % e)
+            expert(e, zn[:])
+            regroup(zn, e * C2, (e + 1) * C2)
+        zn = placed([P, H // P, C1], F32, "zn23", AT_ZN23)
+        for e in (2, 3):
+            expert(e, zn[:, :, (e - 2) * C2:(e - 1) * C2])
+        regroup(zn, C1, T)
+        derivative_on_vector(0, 1)
+        derivative_on_vector(1, 1)
+        derivative_on_vector(1, 0)
+        wgt = kept([P, G, 2 * K], U8, "wgt", "zn0")
+        load_words(wgt[:], wgt_words.rearrange("f s p c -> p (f s) c"))
+        wgt_sc = chain.tile([P, G, K], U8, name="wgt_sc", offset=AT_A01, align_bytes=64)
+        nc.gpsimd.memset(wgt_sc[:].bitcast(I32), 0)
+        load_scales(wgt_sc, wgt_scales.rearrange("f s b k -> (f s) b k"))
 
-        zw1 = [kept([P, T], F32, "zw1_0"), kept([P, T], F32, "zw1_1", "a1_1"), kept([P, T], F32, "zw1_2"), kept([P, T], F32, "zw1_3")]
+        zw0 = [placed([P, T], F32, "zw0_0", AT_WINDOW[0])] + [kept([P, C1], F32, "zw0_%d" % r) for r in (1, 2, 3)]
+        for e, r in ((0, 1), (0, 2), (1, 1), (1, 2), (0, 3), (1, 3)):
+            scatter_z(by_scalar, zw0, e, r)
+        by_vector(zw0[0], offs2_t, 0, C1, zs[0][:, 0, :])
+        grouped0 = placed([P, C1, PACK], BF16, "grouped0", AT_GROUPED)
+        gradient(0, zw0, grouped0, (1, 2, 3, 0))
+
+        zw1 = [placed([P, T], F32, "zw1_0", AT_WINDOW[1]), placed([P, T], F32, "zw1_1", AT_WINDOW[0]), kept([P, T], F32, "zw1_2"), kept([P, T], F32, "zw1_3")]
         by_vector(zw1[0], offs2_t, C1, T, zs[1][:, 0, :])
-        for lo in (0, C2):
-            for r in (2, 3):
-                by_scalar(zw1[r], offs2_t, C1 + lo, C1 + lo + C2, zs[1][:, r, lo:lo + C2])
+        for e, r in ((2, 2), (2, 3), (3, 2), (3, 3)):
+            scatter_z(by_scalar, zw1, e, r)
         acc2 = second_product(0, grouped0)
         by_vector(zw1[1], offs2_t, C1, T, zs[1][:, 1, :])
-        grouped1 = kept([P, C1, PACK], BF16, "grouped1", "grouped")
-        gradient(1, zw1, grouped1)
+        grouped1 = placed([P, C1, PACK], BF16, "grouped1", AT_GROUPED)
+        gradient(1, zw1, grouped1, (0, 2, 3, 1))
 
-        ow = [kept([P, T], F32, "ow0"), kept([P, T], F32, "ow1", "a1_1"), kept([P, T], F32, "ow2"), kept([P, T], F32, "ow3")]
+        ow = [kept([P, T], F32, "ow0"), placed([P, T], F32, "ow1", AT_WINDOW[0]), kept([P, T], F32, "ow2"), kept([P, T], F32, "ow3")]
+        dxs = [[kept([P, C1], F32, "dxs%d_%d" % (f, c)) for c in range(K // P)] for f in range(G)]
+
+        def scatter_dx(by, f, c, lo, hi):
+            by(ow[c], offs_t, f * C1 + lo, f * C1 + hi, dxs[f][c][:, lo:hi])
 
         def leave(f, acc2):
-            dxs = [kept([P, C1], F32, "dxs%d_%d" % (f, c)) for c in range(K // P)]
-            for c in (0, 1):
-                nc.vector.tensor_copy(dxs[c][:], acc2[c][:])
+            for c in (0, 2, 1, 3):
+                nc.scalar.activation(dxs[f][c][:], acc2[c][:], ACT.Copy)
+
+        leave(0, acc2)
+        scatter_dx(by_vector, 0, 0, 0, C1)
+        for lo in (0, C2):
             for c in (2, 3):
-                nc.scalar.activation(dxs[c][:], acc2[c][:], ACT.Copy)
-            return dxs
-
-        def scalar_share(f, dxs):
-            for lo in (0, C2):
-                for c in (2, 3):
-                    by_scalar(ow[c], offs_t, f * C1 + lo, f * C1 + lo + C2, dxs[c][:, lo:lo + C2])
-
-        dxs = leave(0, acc2)
-        by_vector(ow[0], offs_t, 0, C1, dxs[0][:])
-        scalar_share(0, dxs)
+                scatter_dx(by_scalar, 0, c, lo, lo + C2)
         acc2 = second_product(1, grouped1)
-        by_vector(ow[1], offs_t, 0, C1, dxs[1][:])
-        dxs = leave(1, acc2)
-        scalar_share(1, dxs)
+        scatter_dx(by_vector, 0, 1, 0, C1)
+        leave(1, acc2)
+        for c in (2, 3):
+            for lo in (0, C2):
+                scatter_dx(by_scalar, 1, c, lo, lo + C2)
         for c in (0, 1):
-            by_vector(ow[c], offs_t, C1, T, dxs[c][:])
+            scatter_dx(by_vector, 1, c, 0, C1)
         for c in (0, 2, 1, 3):
-            nc.sync.dma_start(out[c * P:(c + 1) * P, :], ow[c][:])
+            (nc.scalar if c == 2 else nc.sync).dma_start(out[c * P:(c + 1) * P, :], ow[c][:])

@@ -65,10 +65,10 @@ def tile_moe_hib_silu_kernel(tc, dy_words, dy_scales, wet_words, wet_scales, wgt
         wet_sc_rows = wet_scales.rearrange("e s b i -> (e s) b i")
         dy_rows = dy_words.rearrange("s p t d -> p s (t d)")
 
-        first_sc = kept([P, E * PASSES, H], U8, "first_sc")
+        first_sc = kept([P, 2 * PASSES, H], U8, "first_sc")
         dys = chain.tile([P, T], U8, name="dys", offset=AT_DYS, align_bytes=64)
         gs = kept([P, PASSES, T], U8, "gs")
-        nc.vector.memset(first_sc[:].bitcast(I32), 0)
+        nc.gpsimd.memset(first_sc[:].bitcast(I32), 0)
         nc.gpsimd.memset(dys[32:64, :].bitcast(I32), 0)
         nc.gpsimd.memset(dys[64:P, :].bitcast(I32), 0)
         nc.gpsimd.memset(gs[:].bitcast(I32), 0)
@@ -96,7 +96,7 @@ def tile_moe_hib_silu_kernel(tc, dy_words, dy_scales, wet_words, wet_scales, wgt
             load_words(dyw[s][:], dy_rows[:, s, :])
         wet0 = kept([P, PASSES, 2 * H], U8, "wet0")
         load_words(wet0[:], wet_rows[:, 0:PASSES, :])
-        load_scales(first_sc, wet_sc_rows)
+        load_scales(first_sc, wet_sc_rows[0:2 * PASSES])
         load_a(0, 0, kept([P, PAIR, C1], F32, "a0_0"))
         gate_t = placed([P, T], F32, "gate_t", AT_GATE)
         nc.sync.dma_start(gate_t[:], gate)
@@ -122,10 +122,13 @@ def tile_moe_hib_silu_kernel(tc, dy_words, dy_scales, wet_words, wet_scales, wgt
         gather_words(1, C1, T)
 
         load_a(0, 1, chain.tile([P, PAIR, C1], F32, name="a0_1", offset=AT_A01, align_bytes=64))
-        wet_sc = [first_sc[:, PASSES * e:PASSES * (e + 1), :] for e in range(E)]
+        late_sc = kept([P, 2 * PASSES, H], U8, "late_sc", "picked")
+        wet_sc = [tile[:, PASSES * n:PASSES * (n + 1), :] for tile in (first_sc, late_sc) for n in range(2)]
         wet_late = chain.tile([P, (E - 1) * PASSES, 2 * H], U8, name="wet_late", offset=AT_LATE, align_bytes=64)
         load_words(wet_late[:], wet_rows[:, PASSES:, :])
         wet = [wet0[:]] + [wet_late[:, PASSES * n:PASSES * (n + 1), :] for n in range(E - 1)]
+        nc.gpsimd.memset(late_sc[:].bitcast(I32), 0)
+        load_scales(late_sc, wet_sc_rows[2 * PASSES:])
         load_a(1, 1, kept([P, PAIR, C1], F32, "a1_1", "dyw0"))
         load_a(1, 0, placed([P, PAIR, C1], F32, "a1_0", AT_DYW1))
 
@@ -159,17 +162,6 @@ def tile_moe_hib_silu_kernel(tc, dy_words, dy_scales, wet_words, wet_scales, wgt
             for r in range(PAIR):
                 nc.vector.scalar_tensor_tensor(sg[f, h][:, r, :], u[r][:], 1.0, sg[f, h][:, r, :], ALU.subtract, ALU.mult)
 
-        def derivative_on_gpsimd(f, h):
-            u = [kept([P, C1], F32, "u%d" % r) for r in range(PAIR)]
-            for r in range(PAIR):
-                nc.gpsimd.tensor_scalar(u[r][:], sg[f, h][:, r, :], 1.0, -1.0, ALU.mult, ALU.add)
-            for r in range(PAIR):
-                nc.gpsimd.tensor_tensor(u[r][:], u[r][:], av[f, h][:, r, :], ALU.mult)
-            for r in range(PAIR):
-                nc.gpsimd.tensor_scalar(u[r][:], u[r][:], 1.0, -1.0, ALU.mult, ALU.add)
-            for r in range(PAIR):
-                nc.gpsimd.tensor_tensor(sg[f, h][:, r, :], u[r][:], sg[f, h][:, r, :], ALU.mult)
-
         def by_vector(window, offsets, lo, hi, values):
             nc.vector.tensor_copy(window[:].indirect(offsets[:, columns(lo, hi)]), values)
 
@@ -197,7 +189,6 @@ def tile_moe_hib_silu_kernel(tc, dy_words, dy_scales, wet_words, wet_scales, wgt
                     start=True, stop=True)
             return acc2
 
-        derivative_on_gpsimd(0, 0)
         sigmoid(0, 1)
         sigmoid(1, 1)
         sigmoid(1, 0)
@@ -209,6 +200,7 @@ def tile_moe_hib_silu_kernel(tc, dy_words, dy_scales, wet_words, wet_scales, wgt
         for e in (2, 3):
             expert(e, zn[:, :, (e - 2) * C2:(e - 1) * C2])
         regroup(zn, C1, T)
+        derivative_on_vector(0, 0)
         derivative_on_vector(0, 1)
         derivative_on_vector(1, 1)
         derivative_on_vector(1, 0)

@@ -23,14 +23,13 @@ PASSES = N // (P * PACK)
 LIST = 16
 QUADS = 4
 KIB = 1024
-AT_A01 = 0
-AT_LATE = 4 * KIB
-AT_DYS = AT_LATE - KIB // 2
-AT_DYW1 = AT_LATE + 6 * KIB
-AT_ZN23 = AT_DYW1 + 4 * KIB
-AT_GROUPED = AT_ZN23 - 2 * KIB
-AT_WINDOW = [AT_ZN23 + 8 * KIB, AT_ZN23 + 12 * KIB]
-AT_GATE = AT_WINDOW[1] - 2 * KIB
+AT_A00 = 0
+AT_DYS = 4 * KIB - 64
+AT_GATE0 = 5 * KIB - 128
+AT_U01 = 4 * KIB
+AT_A01 = 8 * KIB
+AT_LAST0 = 14 * KIB
+AT_LAST1 = AT_LAST0 - 2 * KIB
 
 
 def tile_moe_hib_silu_kernel(tc, dy_words, dy_scales, wet_words, wet_scales, wgt_words, wgt_scales, a, gate, offs, offs2, dst, out):
@@ -62,13 +61,15 @@ def tile_moe_hib_silu_kernel(tc, dy_words, dy_scales, wet_words, wet_scales, wgt
 
         a_rows = a.rearrange("(p r) j -> p r j", r=PACK)
         wet_rows = wet_words.rearrange("e s p c -> p (e s) c")
-        wet_sc_rows = wet_scales.rearrange("e s b i -> (e s) b i")
         dy_rows = dy_words.rearrange("s p t d -> p s (t d)")
 
-        first_sc = kept([P, 2 * PASSES, H], U8, "first_sc")
+        wet_sc = kept([P, E * PASSES, H], U8, "wet_sc")
         dys = chain.tile([P, T], U8, name="dys", offset=AT_DYS, align_bytes=64)
         gs = kept([P, PASSES, T], U8, "gs")
-        nc.gpsimd.memset(first_sc[:].bitcast(I32), 0)
+        nc.vector.memset(wet_sc[:].bitcast(I32), 0)
+        unread = kept([P, 2], F32, "unread")
+        nc.gpsimd.memset(unread[:, 0:1], 0.0)
+        nc.scalar.activation(unread[:, 1:2], unread[:, 0:1], ACT.Sigmoid)
         nc.gpsimd.memset(dys[32:64, :].bitcast(I32), 0)
         nc.gpsimd.memset(dys[64:P, :].bitcast(I32), 0)
         nc.gpsimd.memset(gs[:].bitcast(I32), 0)
@@ -79,27 +80,37 @@ def tile_moe_hib_silu_kernel(tc, dy_words, dy_scales, wet_words, wet_scales, wgt
         nc.sync.dma_start(dst_t[:], dst)
         nc.sync.dma_start(dys[0:32, :].bitcast(I32), dy_scales.rearrange("s r t -> r s t").bitcast(I32))
 
+        sc_rows = kept([P, H], U8, "sc_rows")
+        nc.sync.dma_start(sc_rows[:].bitcast(I32), wet_scales.rearrange("e s b i -> b (e s) i").bitcast(I32))
+
         av = {}
-        sg = {(f, h): kept([P, PAIR, C1], F32, "sg%d_%d" % (f, h)) for f in range(G) for h in range(2)}
+        sg = {}
 
         def load_a(f, h, tile):
             av[f, h] = tile
             nc.sync.dma_start(av[f, h][:], a_rows[:, PAIR * h:PAIR * (h + 1), f * C1:(f + 1) * C1])
 
-        def sigmoid(f, h):
+        def sigmoid(f, h, tag=None):
+            sg[f, h] = kept([P, PAIR, C1], F32, "sg%d_%d" % (f, h), tag)
             nc.scalar.activation(sg[f, h][:], av[f, h][:], ACT.Sigmoid)
 
         nc.sync.dma_start(offs2_t[:], offs2)
         nc.sync.dma_start(offs_t[:], offs)
-        dyw = [kept([P, T], I32, "dyw0"), placed([P, T], I32, "dyw1", AT_DYW1)]
+        raw = [placed([P, 2 * PASSES, 2 * H], U8, "raw0", AT_A01), kept([P, 2 * PASSES, 2 * H], U8, "raw1")]
+        load_words(raw[0][:], wet_rows[:, 0:2 * PASSES, :])
+        dyw = [kept([P, T], I32, "dyw%d" % s) for s in range(PASSES)]
         for s in range(PASSES):
             load_words(dyw[s][:], dy_rows[:, s, :])
-        wet0 = kept([P, PASSES, 2 * H], U8, "wet0")
-        load_words(wet0[:], wet_rows[:, 0:PASSES, :])
-        load_scales(first_sc, wet_sc_rows[0:2 * PASSES])
-        load_a(0, 0, kept([P, PAIR, C1], F32, "a0_0"))
-        gate_t = placed([P, T], F32, "gate_t", AT_GATE)
-        nc.sync.dma_start(gate_t[:], gate)
+        load_words(raw[1][:], wet_rows[:, 2 * PASSES:, :])
+
+        sc_sorted = kept([P, H], U8, "sc_sorted")
+        nc.gpsimd.tensor_copy(sc_sorted[:].rearrange("p (r m) -> p r m", r=PACK), sc_rows[:].rearrange("p (m r) -> p r m", r=PACK))
+        for q in range(QUADS):
+            nc.sync.dma_start(wet_sc[32 * q:32 * q + 4].bitcast(I32), sc_sorted[32 * q:32 * (q + 1), :].bitcast(I32))
+        wet = [kept([P, PASSES, 2 * H], U8, "wet%d" % e) for e in range(E)]
+        for e in range(E):
+            words = raw[e // 2][:, PASSES * (e % 2):PASSES * (e % 2 + 1), :].bitcast(U16)
+            nc.scalar.copy(wet[e][:].bitcast(U16).rearrange("p s (r m) -> p s r m", r=PACK), words.rearrange("p s (m r) -> p s r m", r=PACK))
 
         picked = kept([P, T], U8, "picked")
         for f in range(G):
@@ -121,42 +132,35 @@ def tile_moe_hib_silu_kernel(tc, dy_words, dy_scales, wet_words, wet_scales, wgt
         gather_words(0, C1, T)
         gather_words(1, C1, T)
 
-        load_a(0, 1, chain.tile([P, PAIR, C1], F32, name="a0_1", offset=AT_A01, align_bytes=64))
-        late_sc = kept([P, 2 * PASSES, H], U8, "late_sc", "picked")
-        wet_sc = [tile[:, PASSES * n:PASSES * (n + 1), :] for tile in (first_sc, late_sc) for n in range(2)]
-        wet_late = chain.tile([P, (E - 1) * PASSES, 2 * H], U8, name="wet_late", offset=AT_LATE, align_bytes=64)
-        load_words(wet_late[:], wet_rows[:, PASSES:, :])
-        wet = [wet0[:]] + [wet_late[:, PASSES * n:PASSES * (n + 1), :] for n in range(E - 1)]
-        nc.gpsimd.memset(late_sc[:].bitcast(I32), 0)
-        load_scales(late_sc, wet_sc_rows[2 * PASSES:])
+        load_a(0, 0, placed([P, PAIR, C1], F32, "a0_0", AT_A00))
+        gate_t = [placed([P, C1], F32, "gate0", AT_GATE0), kept([P, C1], F32, "gate1", "picked")]
+        nc.sync.dma_start(gate_t[0][:], gate[:, 0:C1])
+        load_a(0, 1, placed([P, PAIR, C1], F32, "a0_1", AT_A01))
+        nc.sync.dma_start(gate_t[1][:], gate[:, C1:])
         load_a(1, 1, kept([P, PAIR, C1], F32, "a1_1", "dyw0"))
-        load_a(1, 0, placed([P, PAIR, C1], F32, "a1_0", AT_DYW1))
+        load_a(1, 0, kept([P, PAIR, C1], F32, "a1_0", "dyw1"))
 
         sigmoid(0, 0)
 
         zs = [kept([P, PACK, C1], F32, "zs%d" % f) for f in range(G)]
 
-        def regroup(zn, lo, hi):
-            f, u = divmod(lo, C1)
-            for c in range(H // P):
-                nc.sync.dma_start(zs[f][32 * c:32 * (c + 1), :, u:u + hi - lo], zn[:, c, :])
-
-        def expert(e, zn):
+        def expert(e):
+            f, u = divmod(e * C2, C1)
             for half in range(2):
-                acc = bank([P, 2, C2], "acc", 2 * e + half)
-                for n in range(2):
-                    c = 2 * half + n
+                acc = bank([P, PAIR, C2], "acc", 2 * e + half)
+                for n in range(PAIR):
+                    r = PAIR * half + n
                     for s in range(PASSES):
                         nc.tensor.matmul_mx(
                             out=acc[:, n, :],
-                            lhsT=wet[e][:, s, 2 * P * c:2 * P * (c + 1)].bitcast(FP4X4), lhsT_scale=wet_sc[e][:, s, P * c:P * (c + 1)],
+                            lhsT=wet[e][:, s, 2 * P * r:2 * P * (r + 1)].bitcast(FP4X4), lhsT_scale=wet_sc[:, PASSES * e + s, P * r:P * (r + 1)],
                             rhs=gw[s, e].bitcast(FP8X4), rhs_scale=gs[:, s, e * C2:(e + 1) * C2],
                             start=(s == 0), stop=(s == PASSES - 1))
-                weight = gate_t[:, e * C2:(e + 1) * C2].unsqueeze(1).to_broadcast([P, 2, C2])
-                nc.vector.scalar_tensor_tensor(zn[:, 2 * half:2 * half + 2, :], acc[:], -1.0, weight, ALU.mult, ALU.mult)
+                weight = gate_t[f][:, u:u + C2].unsqueeze(1).to_broadcast([P, PAIR, C2])
+                nc.vector.scalar_tensor_tensor(zs[f][:, PAIR * half:PAIR * (half + 1), u:u + C2], acc[:], -1.0, weight, ALU.mult, ALU.mult)
 
-        def derivative_on_vector(f, h):
-            u = [placed([P, C1], F32, "u%d_%d_%d" % (f, h, r), AT_GATE + 2 * KIB * r) for r in range(PAIR)]
+        def derivative_on_vector(f, h, at):
+            u = [placed([P, C1], F32, "u%d_%d_%d" % (f, h, r), at + 2 * KIB * r) for r in range(PAIR)]
             for r in range(PAIR):
                 nc.vector.scalar_tensor_tensor(u[r][:], sg[f, h][:, r, :], 1.0, av[f, h][:, r, :], ALU.subtract, ALU.mult)
             for r in range(PAIR):
@@ -190,43 +194,39 @@ def tile_moe_hib_silu_kernel(tc, dy_words, dy_scales, wet_words, wet_scales, wgt
             return acc2
 
         sigmoid(0, 1)
-        sigmoid(1, 1)
-        sigmoid(1, 0)
-        for e in (0, 1):
-            zn = kept([P, H // P, C2], F32, "zn%d" % e)
-            expert(e, zn[:])
-            regroup(zn, e * C2, (e + 1) * C2)
-        zn = placed([P, H // P, C1], F32, "zn23", AT_ZN23)
-        for e in (2, 3):
-            expert(e, zn[:, :, (e - 2) * C2:(e - 1) * C2])
-        regroup(zn, C1, T)
-        derivative_on_vector(0, 0)
-        derivative_on_vector(0, 1)
-        derivative_on_vector(1, 1)
-        derivative_on_vector(1, 0)
-        wgt = kept([P, G, 2 * K], U8, "wgt", "zn0")
+        expert(0)
+        derivative_on_vector(0, 0, AT_LAST0)
+        expert(1)
+        derivative_on_vector(0, 1, AT_U01)
+        expert(2)
+        expert(3)
+        wgt = kept([P, G, 2 * K], U8, "wgt", "wet0")
         load_words(wgt[:], wgt_words.rearrange("f s p c -> p (f s) c"))
-        wgt_sc = chain.tile([P, G, K], U8, name="wgt_sc", offset=AT_A01, align_bytes=64)
+        wgt_sc = chain.tile([P, G, K], U8, name="wgt_sc", offset=AT_A00, align_bytes=64)
         nc.gpsimd.memset(wgt_sc[:].bitcast(I32), 0)
         load_scales(wgt_sc, wgt_scales.rearrange("f s b k -> (f s) b k"))
 
-        zw0 = [placed([P, T], F32, "zw0_0", AT_WINDOW[0])] + [kept([P, C1], F32, "zw0_%d" % r) for r in (1, 2, 3)]
+        zw0 = [kept([P, T], F32, "zw0_0"), kept([P, C1], F32, "zw0_1"), kept([P, C1], F32, "zw0_2"), placed([P, T], F32, "zw0_3", AT_LAST0)]
         for e, r in ((0, 1), (0, 2), (1, 1), (1, 2), (0, 3), (1, 3)):
             scatter_z(by_scalar, zw0, e, r)
+        sigmoid(1, 1, "wet2")
+        sigmoid(1, 0, "wet3")
         by_vector(zw0[0], offs2_t, 0, C1, zs[0][:, 0, :])
-        grouped0 = placed([P, C1, PACK], BF16, "grouped0", AT_GROUPED)
-        gradient(0, zw0, grouped0, (1, 2, 3, 0))
+        grouped0 = placed([P, C1, PACK], BF16, "grouped0", AT_A01)
+        gradient(0, zw0, grouped0, (1, 2, 0, 3))
 
-        zw1 = [placed([P, T], F32, "zw1_0", AT_WINDOW[1]), placed([P, T], F32, "zw1_1", AT_WINDOW[0]), kept([P, T], F32, "zw1_2"), kept([P, T], F32, "zw1_3")]
+        zw1 = [kept([P, T], F32, "zw1_0"), placed([P, T], F32, "zw1_1", AT_LAST1), kept([P, T], F32, "zw1_2"), kept([P, T], F32, "zw1_3")]
         by_vector(zw1[0], offs2_t, C1, T, zs[1][:, 0, :])
         for e, r in ((2, 2), (2, 3), (3, 2), (3, 3)):
             scatter_z(by_scalar, zw1, e, r)
         acc2 = second_product(0, grouped0)
+        derivative_on_vector(1, 1, AT_LAST0)
+        derivative_on_vector(1, 0, AT_LAST0)
         by_vector(zw1[1], offs2_t, C1, T, zs[1][:, 1, :])
-        grouped1 = placed([P, C1, PACK], BF16, "grouped1", AT_GROUPED)
+        grouped1 = placed([P, C1, PACK], BF16, "grouped1", AT_A01)
         gradient(1, zw1, grouped1, (0, 2, 3, 1))
 
-        ow = [kept([P, T], F32, "ow0"), placed([P, T], F32, "ow1", AT_WINDOW[0]), kept([P, T], F32, "ow2"), kept([P, T], F32, "ow3")]
+        ow = [kept([P, T], F32, "ow0"), placed([P, T], F32, "ow1", AT_LAST1), kept([P, T], F32, "ow2"), kept([P, T], F32, "ow3")]
         dxs = [[kept([P, C1], F32, "dxs%d_%d" % (f, c)) for c in range(K // P)] for f in range(G)]
 
         def scatter_dx(by, f, c, lo, hi):

@@ -23,7 +23,9 @@ PASSES = N // (P * PACK)
 LIST = 16
 QUADS = 4
 KIB = 1024
-AT_A00 = 0
+AT_RAW1 = 0
+AT_A00 = 18 * KIB
+AT_ZS0 = AT_A00 + 2 * KIB
 AT_DYS = 4 * KIB - 64
 AT_GATE0 = 5 * KIB - 128
 AT_U01 = 4 * KIB
@@ -96,22 +98,25 @@ def tile_moe_hib_silu_kernel(tc, dy_words, dy_scales, wet_words, wet_scales, wgt
 
         nc.sync.dma_start(offs2_t[:], offs2)
         nc.sync.dma_start(offs_t[:], offs)
-        raw = [placed([P, 2 * PASSES, 2 * H], U8, "raw0", AT_A01), kept([P, 2 * PASSES, 2 * H], U8, "raw1")]
+        raw = [placed([P, 2 * PASSES, 2 * H], U8, "raw0", AT_A01), placed([P, 2 * PASSES, 2 * H], U8, "raw1", AT_RAW1)]
         load_words(raw[0][:], wet_rows[:, 0:2 * PASSES, :])
         dyw = [kept([P, T], I32, "dyw%d" % s) for s in range(PASSES)]
         for s in range(PASSES):
             load_words(dyw[s][:], dy_rows[:, s, :])
-        load_words(raw[1][:], wet_rows[:, 2 * PASSES:, :])
+        load_a(0, 0, placed([P, PAIR, C1], F32, "a0_0", AT_A00))
 
         sc_sorted = kept([P, H], U8, "sc_sorted")
         nc.gpsimd.tensor_copy(sc_sorted[:].rearrange("p (r m) -> p r m", r=PACK), sc_rows[:].rearrange("p (m r) -> p r m", r=PACK))
         for q in range(QUADS):
             nc.sync.dma_start(wet_sc[32 * q:32 * q + 4].bitcast(I32), sc_sorted[32 * q:32 * (q + 1), :].bitcast(I32))
         wet = [kept([P, PASSES, 2 * H], U8, "wet%d" % e) for e in range(E)]
-        for e in range(E):
+
+        def sort_columns(e):
             words = raw[e // 2][:, PASSES * (e % 2):PASSES * (e % 2 + 1), :].bitcast(U16)
             nc.scalar.copy(wet[e][:].bitcast(U16).rearrange("p s (r m) -> p s r m", r=PACK), words.rearrange("p s (m r) -> p s r m", r=PACK))
 
+        sort_columns(0)
+        sort_columns(1)
         picked = kept([P, T], U8, "picked")
         for f in range(G):
             nc.vector.tensor_copy(picked[:, f * C1:(f + 1) * C1], dys[:].indirect(dst_t[:, columns(f * C1, (f + 1) * C1)]))
@@ -132,7 +137,7 @@ def tile_moe_hib_silu_kernel(tc, dy_words, dy_scales, wet_words, wet_scales, wgt
         gather_words(0, C1, T)
         gather_words(1, C1, T)
 
-        load_a(0, 0, placed([P, PAIR, C1], F32, "a0_0", AT_A00))
+        load_words(raw[1][:], wet_rows[:, 2 * PASSES:, :])
         gate_t = [placed([P, C1], F32, "gate0", AT_GATE0), kept([P, C1], F32, "gate1", "picked")]
         nc.sync.dma_start(gate_t[0][:], gate[:, 0:C1])
         load_a(0, 1, placed([P, PAIR, C1], F32, "a0_1", AT_A01))
@@ -141,8 +146,10 @@ def tile_moe_hib_silu_kernel(tc, dy_words, dy_scales, wet_words, wet_scales, wgt
         load_a(1, 0, kept([P, PAIR, C1], F32, "a1_0", "dyw1"))
 
         sigmoid(0, 0)
+        sort_columns(2)
+        sort_columns(3)
 
-        zs = [kept([P, PACK, C1], F32, "zs%d" % f) for f in range(G)]
+        zs = [placed([P, PACK, C1], F32, "zs0", AT_ZS0), kept([P, PACK, C1], F32, "zs1")]
 
         def expert(e):
             f, u = divmod(e * C2, C1)
@@ -194,8 +201,8 @@ def tile_moe_hib_silu_kernel(tc, dy_words, dy_scales, wet_words, wet_scales, wgt
             return acc2
 
         sigmoid(0, 1)
-        expert(0)
         derivative_on_vector(0, 0, AT_LAST0)
+        expert(0)
         expert(1)
         derivative_on_vector(0, 1, AT_U01)
         expert(2)
@@ -243,11 +250,13 @@ def tile_moe_hib_silu_kernel(tc, dy_words, dy_scales, wet_words, wet_scales, wgt
                 scatter_dx(by_scalar, 0, c, lo, lo + C2)
         acc2 = second_product(1, grouped1)
         scatter_dx(by_vector, 0, 1, 0, C1)
-        leave(1, acc2)
+        for c in (0, 2, 3):
+            nc.scalar.activation(dxs[1][c][:], acc2[c][:], ACT.Copy)
+        nc.vector.tensor_copy(dxs[1][1][:], acc2[1][:])
         for c in (2, 3):
             for lo in (0, C2):
                 scatter_dx(by_scalar, 1, c, lo, lo + C2)
         for c in (0, 1):
             scatter_dx(by_vector, 1, c, 0, C1)
         for c in (0, 2, 1, 3):
-            (nc.scalar if c == 2 else nc.sync).dma_start(out[c * P:(c + 1) * P, :], ow[c][:])
+            (nc.scalar if c >= 2 else nc.sync).dma_start(out[c * P:(c + 1) * P, :], ow[c][:])

@@ -21,10 +21,14 @@ PACK = 4
 PAIR = 2
 PASSES = N // (P * PACK)
 LIST = 16
+BY_PORT = (0, 2, 1, 3)
 QUADS = 4
 KIB = 1024
 AT_RAW1 = 0
 AT_A00 = 18 * KIB
+AT_GROUPED = 28 * KIB
+AT_GATE1 = AT_GROUPED + KIB
+AT_A11 = 34 * KIB
 AT_ZS0 = AT_A00 + 2 * KIB
 AT_DYS = 4 * KIB - 64
 AT_GATE0 = 5 * KIB - 128
@@ -55,7 +59,7 @@ def tile_moe_hib_silu_kernel(tc, dy_words, dy_scales, wet_words, wet_scales, wgt
             nc.sync.dma_start(tile.bitcast(I32), words.bitcast(I32))
 
         def load_scales(tile, scales):
-            for q in range(QUADS):
+            for q in BY_PORT:
                 nc.sync.dma_start(tile[32 * q:32 * q + 4].bitcast(I32), scales[:, 4 * q:4 * q + 4, :].rearrange("s b t -> b s t").bitcast(I32))
 
         def columns(lo, hi):
@@ -100,14 +104,14 @@ def tile_moe_hib_silu_kernel(tc, dy_words, dy_scales, wet_words, wet_scales, wgt
         nc.sync.dma_start(offs_t[:], offs)
         raw = [placed([P, 2 * PASSES, 2 * H], U8, "raw0", AT_A01), placed([P, 2 * PASSES, 2 * H], U8, "raw1", AT_RAW1)]
         load_words(raw[0][:], wet_rows[:, 0:2 * PASSES, :])
-        dyw = [kept([P, T], I32, "dyw%d" % s) for s in range(PASSES)]
+        dyw = [placed([P, T], I32, "dyw0", AT_A11), kept([P, T], I32, "dyw1")]
         for s in range(PASSES):
             load_words(dyw[s][:], dy_rows[:, s, :])
         load_a(0, 0, placed([P, PAIR, C1], F32, "a0_0", AT_A00))
 
         sc_sorted = kept([P, H], U8, "sc_sorted")
         nc.gpsimd.tensor_copy(sc_sorted[:].rearrange("p (r m) -> p r m", r=PACK), sc_rows[:].rearrange("p (m r) -> p r m", r=PACK))
-        for q in range(QUADS):
+        for q in BY_PORT:
             nc.sync.dma_start(wet_sc[32 * q:32 * q + 4].bitcast(I32), sc_sorted[32 * q:32 * (q + 1), :].bitcast(I32))
         wet = [kept([P, PASSES, 2 * H], U8, "wet%d" % e) for e in range(E)]
 
@@ -117,10 +121,10 @@ def tile_moe_hib_silu_kernel(tc, dy_words, dy_scales, wet_words, wet_scales, wgt
 
         sort_columns(0)
         sort_columns(1)
-        picked = kept([P, T], U8, "picked")
+        picked = placed([P, T], U8, "picked", AT_GATE1)
         for f in range(G):
             nc.vector.tensor_copy(picked[:, f * C1:(f + 1) * C1], dys[:].indirect(dst_t[:, columns(f * C1, (f + 1) * C1)]))
-        for q in range(QUADS):
+        for q in BY_PORT:
             nc.sync.dma_start(gs[32 * q:32 * q + 4].bitcast(I32), picked[8 * q:8 * q + 8, :].bitcast(I32))
 
         gw = {}
@@ -138,11 +142,11 @@ def tile_moe_hib_silu_kernel(tc, dy_words, dy_scales, wet_words, wet_scales, wgt
         gather_words(1, C1, T)
 
         load_words(raw[1][:], wet_rows[:, 2 * PASSES:, :])
-        gate_t = [placed([P, C1], F32, "gate0", AT_GATE0), kept([P, C1], F32, "gate1", "picked")]
+        gate_t = [placed([P, C1], F32, "gate0", AT_GATE0), placed([P, C1], F32, "gate1", AT_GATE1)]
         nc.sync.dma_start(gate_t[0][:], gate[:, 0:C1])
         load_a(0, 1, placed([P, PAIR, C1], F32, "a0_1", AT_A01))
         nc.sync.dma_start(gate_t[1][:], gate[:, C1:])
-        load_a(1, 1, kept([P, PAIR, C1], F32, "a1_1", "dyw0"))
+        load_a(1, 1, placed([P, PAIR, C1], F32, "a1_1", AT_A11))
         load_a(1, 0, kept([P, PAIR, C1], F32, "a1_0", "dyw1"))
 
         sigmoid(0, 0)
@@ -205,32 +209,32 @@ def tile_moe_hib_silu_kernel(tc, dy_words, dy_scales, wet_words, wet_scales, wgt
         expert(0)
         expert(1)
         derivative_on_vector(0, 1, AT_U01)
+        sigmoid(1, 1, "wet1")
         expert(2)
         expert(3)
+        derivative_on_vector(1, 1, AT_GROUPED)
         wgt = kept([P, G, 2 * K], U8, "wgt", "wet0")
         load_words(wgt[:], wgt_words.rearrange("f s p c -> p (f s) c"))
         wgt_sc = chain.tile([P, G, K], U8, name="wgt_sc", offset=AT_A00, align_bytes=64)
         nc.gpsimd.memset(wgt_sc[:].bitcast(I32), 0)
         load_scales(wgt_sc, wgt_scales.rearrange("f s b k -> (f s) b k"))
 
-        zw0 = [kept([P, T], F32, "zw0_0"), kept([P, C1], F32, "zw0_1"), kept([P, C1], F32, "zw0_2"), placed([P, T], F32, "zw0_3", AT_LAST0)]
+        zw0 = [placed([P, T], F32, "zw0_0", AT_A11 - 2 * KIB), kept([P, C1], F32, "zw0_1"), kept([P, C1], F32, "zw0_2"), placed([P, T], F32, "zw0_3", AT_LAST0)]
         for e, r in ((0, 1), (0, 2), (1, 1), (1, 2), (0, 3), (1, 3)):
             scatter_z(by_scalar, zw0, e, r)
-        sigmoid(1, 1, "wet2")
         sigmoid(1, 0, "wet3")
         by_vector(zw0[0], offs2_t, 0, C1, zs[0][:, 0, :])
-        grouped0 = placed([P, C1, PACK], BF16, "grouped0", AT_A01)
+        grouped0 = placed([P, C1, PACK], BF16, "grouped0", AT_GROUPED)
         gradient(0, zw0, grouped0, (1, 2, 0, 3))
 
-        zw1 = [kept([P, T], F32, "zw1_0"), placed([P, T], F32, "zw1_1", AT_LAST1), kept([P, T], F32, "zw1_2"), kept([P, T], F32, "zw1_3")]
+        zw1 = [placed([P, T], F32, "zw1_0", AT_A11 + 2 * KIB), placed([P, T], F32, "zw1_1", AT_LAST1), kept([P, T], F32, "zw1_2"), kept([P, T], F32, "zw1_3")]
         by_vector(zw1[0], offs2_t, C1, T, zs[1][:, 0, :])
         for e, r in ((2, 2), (2, 3), (3, 2), (3, 3)):
             scatter_z(by_scalar, zw1, e, r)
         acc2 = second_product(0, grouped0)
-        derivative_on_vector(1, 1, AT_LAST0)
         derivative_on_vector(1, 0, AT_LAST0)
         by_vector(zw1[1], offs2_t, C1, T, zs[1][:, 1, :])
-        grouped1 = placed([P, C1, PACK], BF16, "grouped1", AT_A01)
+        grouped1 = placed([P, C1, PACK], BF16, "grouped1", AT_GROUPED)
         gradient(1, zw1, grouped1, (0, 2, 3, 1))
 
         ow = [kept([P, T], F32, "ow0"), placed([P, T], F32, "ow1", AT_LAST1), kept([P, T], F32, "ow2"), kept([P, T], F32, "ow3")]

@@ -24,18 +24,17 @@ LIST = 16
 BY_PORT = (0, 2, 1, 3)
 QUADS = 4
 KIB = 1024
-AT_RAW1 = 0
-AT_A00 = 18 * KIB
-AT_GROUPED = 28 * KIB
-AT_GATE1 = AT_GROUPED + KIB
-AT_A11 = 34 * KIB
+AT_HIGH = 4 * KIB
+AT_DYS = AT_HIGH + 8 * KIB - 64
+AT_GATE0 = AT_DYS + KIB - 64
+AT_ZW00 = 2 * KIB
+AT_ZS1 = 6 * KIB
+AT_A00 = 40 * KIB
 AT_ZS0 = AT_A00 + 2 * KIB
-AT_DYS = 4 * KIB - 64
-AT_GATE0 = 5 * KIB - 128
-AT_U01 = 4 * KIB
-AT_A01 = 8 * KIB
+AT_U01 = 28 * KIB
+AT_U00 = 34 * KIB
 AT_LAST0 = 14 * KIB
-AT_LAST1 = AT_LAST0 - 2 * KIB
+AT_LAST1 = AT_LAST0 + 2 * KIB
 
 
 def tile_moe_hib_silu_kernel(tc, dy_words, dy_scales, wet_words, wet_scales, wgt_words, wgt_scales, a, gate, offs, offs2, dst, out):
@@ -102,18 +101,19 @@ def tile_moe_hib_silu_kernel(tc, dy_words, dy_scales, wet_words, wet_scales, wgt
 
         nc.sync.dma_start(offs2_t[:], offs2)
         nc.sync.dma_start(offs_t[:], offs)
-        raw = [placed([P, 2 * PASSES, 2 * H], U8, "raw0", AT_A01), placed([P, 2 * PASSES, 2 * H], U8, "raw1", AT_RAW1)]
+        raw = [kept([P, 2 * PASSES, 2 * H], U8, "raw0"), kept([P, 2 * PASSES, 2 * H], U8, "raw1")]
         load_words(raw[0][:], wet_rows[:, 0:2 * PASSES, :])
-        dyw = [placed([P, T], I32, "dyw0", AT_A11), kept([P, T], I32, "dyw1")]
+        dyw = [kept([P, T], I32, "dyw%d" % s) for s in range(PASSES)]
         for s in range(PASSES):
             load_words(dyw[s][:], dy_rows[:, s, :])
         load_a(0, 0, placed([P, PAIR, C1], F32, "a0_0", AT_A00))
+        load_words(raw[1][:], wet_rows[:, 2 * PASSES:, :])
 
         sc_sorted = kept([P, H], U8, "sc_sorted")
         nc.gpsimd.tensor_copy(sc_sorted[:].rearrange("p (r m) -> p r m", r=PACK), sc_rows[:].rearrange("p (m r) -> p r m", r=PACK))
         for q in BY_PORT:
             nc.sync.dma_start(wet_sc[32 * q:32 * q + 4].bitcast(I32), sc_sorted[32 * q:32 * (q + 1), :].bitcast(I32))
-        wet = [kept([P, PASSES, 2 * H], U8, "wet%d" % e) for e in range(E)]
+        wet = [placed([P, PASSES, 2 * H], U8, "wet0", AT_U01 + KIB)] + [kept([P, PASSES, 2 * H], U8, "wet%d" % e) for e in range(1, E)]
 
         def sort_columns(e):
             words = raw[e // 2][:, PASSES * (e % 2):PASSES * (e % 2 + 1), :].bitcast(U16)
@@ -121,7 +121,7 @@ def tile_moe_hib_silu_kernel(tc, dy_words, dy_scales, wet_words, wet_scales, wgt
 
         sort_columns(0)
         sort_columns(1)
-        picked = placed([P, T], U8, "picked", AT_GATE1)
+        picked = kept([P, T], U8, "picked")
         for f in range(G):
             nc.vector.tensor_copy(picked[:, f * C1:(f + 1) * C1], dys[:].indirect(dst_t[:, columns(f * C1, (f + 1) * C1)]))
         for q in BY_PORT:
@@ -141,19 +141,20 @@ def tile_moe_hib_silu_kernel(tc, dy_words, dy_scales, wet_words, wet_scales, wgt
         gather_words(0, C1, T)
         gather_words(1, C1, T)
 
-        load_words(raw[1][:], wet_rows[:, 2 * PASSES:, :])
-        gate_t = [placed([P, C1], F32, "gate0", AT_GATE0), placed([P, C1], F32, "gate1", AT_GATE1)]
+        a_high = placed([P, PAIR, T], F32, "a_high", AT_HIGH)
+        nc.sync.dma_start(a_high[:], a_rows[:, PAIR:, :])
+        for f in range(G):
+            av[f, 1] = a_high[:, :, f * C1:(f + 1) * C1]
+        gate_t = [placed([P, C1], F32, "gate0", AT_GATE0), kept([P, C1], F32, "gate1", "picked")]
         nc.sync.dma_start(gate_t[0][:], gate[:, 0:C1])
-        load_a(0, 1, placed([P, PAIR, C1], F32, "a0_1", AT_A01))
         nc.sync.dma_start(gate_t[1][:], gate[:, C1:])
-        load_a(1, 1, placed([P, PAIR, C1], F32, "a1_1", AT_A11))
-        load_a(1, 0, kept([P, PAIR, C1], F32, "a1_0", "dyw1"))
+        load_a(1, 0, kept([P, PAIR, C1], F32, "a1_0", "dyw0"))
 
         sigmoid(0, 0)
         sort_columns(2)
         sort_columns(3)
 
-        zs = [placed([P, PACK, C1], F32, "zs0", AT_ZS0), kept([P, PACK, C1], F32, "zs1")]
+        zs = [placed([P, PACK, C1], F32, "zs0", AT_ZS0), placed([P, PACK, C1], F32, "zs1", AT_ZS1)]
 
         def expert(e):
             f, u = divmod(e * C2, C1)
@@ -171,7 +172,7 @@ def tile_moe_hib_silu_kernel(tc, dy_words, dy_scales, wet_words, wet_scales, wgt
                 nc.vector.scalar_tensor_tensor(zs[f][:, PAIR * half:PAIR * (half + 1), u:u + C2], acc[:], -1.0, weight, ALU.mult, ALU.mult)
 
         def derivative_on_vector(f, h, at):
-            u = [placed([P, C1], F32, "u%d_%d_%d" % (f, h, r), at + 2 * KIB * r) for r in range(PAIR)]
+            u = [placed([P, C1], F32, "u%d_%d_%d" % (f, h, r), at + 2 * KIB * (1 - r)) for r in range(PAIR)]
             for r in range(PAIR):
                 nc.vector.scalar_tensor_tensor(u[r][:], sg[f, h][:, r, :], 1.0, av[f, h][:, r, :], ALU.subtract, ALU.mult)
             for r in range(PAIR):
@@ -205,36 +206,36 @@ def tile_moe_hib_silu_kernel(tc, dy_words, dy_scales, wet_words, wet_scales, wgt
             return acc2
 
         sigmoid(0, 1)
-        derivative_on_vector(0, 0, AT_LAST0)
+        sigmoid(1, 1)
+        derivative_on_vector(0, 0, AT_U00)
         expert(0)
-        expert(1)
         derivative_on_vector(0, 1, AT_U01)
-        sigmoid(1, 1, "wet1")
+        expert(1)
+        derivative_on_vector(1, 1, AT_U01)
+        zw0 = [placed([P, T], F32, "zw0_0", AT_ZW00), kept([P, C1], F32, "zw0_1"), kept([P, C1], F32, "zw0_2"), placed([P, T], F32, "zw0_3", AT_LAST0)]
+        by_vector(zw0[0], offs2_t, 0, C1, zs[0][:, 0, :])
         expert(2)
         expert(3)
-        derivative_on_vector(1, 1, AT_GROUPED)
-        wgt = kept([P, G, 2 * K], U8, "wgt", "wet0")
+        wgt = kept([P, G, 2 * K], U8, "wgt", "wet1")
         load_words(wgt[:], wgt_words.rearrange("f s p c -> p (f s) c"))
         wgt_sc = chain.tile([P, G, K], U8, name="wgt_sc", offset=AT_A00, align_bytes=64)
         nc.gpsimd.memset(wgt_sc[:].bitcast(I32), 0)
         load_scales(wgt_sc, wgt_scales.rearrange("f s b k -> (f s) b k"))
 
-        zw0 = [placed([P, T], F32, "zw0_0", AT_A11 - 2 * KIB), kept([P, C1], F32, "zw0_1"), kept([P, C1], F32, "zw0_2"), placed([P, T], F32, "zw0_3", AT_LAST0)]
         for e, r in ((0, 1), (0, 2), (1, 1), (1, 2), (0, 3), (1, 3)):
             scatter_z(by_scalar, zw0, e, r)
-        sigmoid(1, 0, "wet3")
-        by_vector(zw0[0], offs2_t, 0, C1, zs[0][:, 0, :])
-        grouped0 = placed([P, C1, PACK], BF16, "grouped0", AT_GROUPED)
+        sigmoid(1, 0, "picked")
+        grouped0 = placed([P, C1, PACK], BF16, "grouped0", AT_U01)
         gradient(0, zw0, grouped0, (1, 2, 0, 3))
 
-        zw1 = [placed([P, T], F32, "zw1_0", AT_A11 + 2 * KIB), placed([P, T], F32, "zw1_1", AT_LAST1), kept([P, T], F32, "zw1_2"), kept([P, T], F32, "zw1_3")]
+        zw1 = [kept([P, T], F32, "zw1_0"), placed([P, T], F32, "zw1_1", AT_LAST1), kept([P, T], F32, "zw1_2"), kept([P, T], F32, "zw1_3")]
         by_vector(zw1[0], offs2_t, C1, T, zs[1][:, 0, :])
         for e, r in ((2, 2), (2, 3), (3, 2), (3, 3)):
             scatter_z(by_scalar, zw1, e, r)
         acc2 = second_product(0, grouped0)
         derivative_on_vector(1, 0, AT_LAST0)
         by_vector(zw1[1], offs2_t, C1, T, zs[1][:, 1, :])
-        grouped1 = placed([P, C1, PACK], BF16, "grouped1", AT_GROUPED)
+        grouped1 = placed([P, C1, PACK], BF16, "grouped1", AT_U01)
         gradient(1, zw1, grouped1, (0, 2, 3, 1))
 
         ow = [kept([P, T], F32, "ow0"), placed([P, T], F32, "ow1", AT_LAST1), kept([P, T], F32, "ow2"), kept([P, T], F32, "ow3")]

@@ -24,17 +24,23 @@ LIST = 16
 BY_PORT = (0, 2, 1, 3)
 QUADS = 4
 KIB = 1024
-AT_HIGH = 4 * KIB
-AT_DYS = AT_HIGH + 8 * KIB - 64
-AT_GATE0 = AT_DYS + KIB - 64
-AT_ZW00 = 2 * KIB
-AT_ZS1 = 6 * KIB
-AT_A00 = 40 * KIB
-AT_ZS0 = AT_A00 + 2 * KIB
-AT_U01 = 28 * KIB
-AT_U00 = 34 * KIB
-AT_LAST0 = 14 * KIB
-AT_LAST1 = AT_LAST0 + 2 * KIB
+EARLY = 192
+AT_A11 = 0
+AT_SC_ROWS = AT_A11 + 4 * KIB - 64
+AT_A01 = 15 * KIB
+AT_A00 = 24 * KIB
+AT_WET_LATE = AT_A00 - 4 * KIB + 64
+AT_H00 = 34 * KIB
+AT_H01 = 42 * KIB
+AT_ZW00 = AT_H01 - 2 * KIB
+AT_LAST0 = AT_H01 + 2 * KIB
+AT_W11 = 52 * KIB
+AT_ZS1 = AT_W11 + 64
+AT_W10 = 62 * KIB
+AT_W01 = 68 * KIB
+AT_GATE1 = AT_W01 - 2 * KIB + 64
+AT_WGT = AT_W01 + 64
+AT_SG10 = AT_WGT + 3 * KIB
 
 
 def tile_moe_hib_silu_kernel(tc, dy_words, dy_scales, wet_words, wet_scales, wgt_words, wgt_scales, a, gate, offs, offs2, dst, out):
@@ -69,12 +75,12 @@ def tile_moe_hib_silu_kernel(tc, dy_words, dy_scales, wet_words, wet_scales, wgt
         dy_rows = dy_words.rearrange("s p t d -> p s (t d)")
 
         wet_sc = kept([P, E * PASSES, H], U8, "wet_sc")
-        dys = chain.tile([P, T], U8, name="dys", offset=AT_DYS, align_bytes=64)
+        dys = kept([P, T], U8, "dys")
         gs = kept([P, PASSES, T], U8, "gs")
         nc.vector.memset(wet_sc[:].bitcast(I32), 0)
         unread = kept([P, 2], F32, "unread")
         nc.gpsimd.memset(unread[:, 0:1], 0.0)
-        nc.scalar.activation(unread[:, 1:2], unread[:, 0:1], ACT.Sigmoid)
+        nc.scalar.activation(unread[:, 1:2], unread[:, 0:1], ACT.Silu)
         nc.gpsimd.memset(dys[32:64, :].bitcast(I32), 0)
         nc.gpsimd.memset(dys[64:P, :].bitcast(I32), 0)
         nc.gpsimd.memset(gs[:].bitcast(I32), 0)
@@ -85,42 +91,31 @@ def tile_moe_hib_silu_kernel(tc, dy_words, dy_scales, wet_words, wet_scales, wgt
         nc.sync.dma_start(dst_t[:], dst)
         nc.sync.dma_start(dys[0:32, :].bitcast(I32), dy_scales.rearrange("s r t -> r s t").bitcast(I32))
 
-        sc_rows = kept([P, H], U8, "sc_rows")
+        sc_rows = placed([P, H], U8, "sc_rows", AT_SC_ROWS)
         nc.sync.dma_start(sc_rows[:].bitcast(I32), wet_scales.rearrange("e s b i -> b (e s) i").bitcast(I32))
 
         av = {}
-        sg = {}
 
         def load_a(f, h, tile):
             av[f, h] = tile
             nc.sync.dma_start(av[f, h][:], a_rows[:, PAIR * h:PAIR * (h + 1), f * C1:(f + 1) * C1])
 
-        def sigmoid(f, h, tag=None):
-            sg[f, h] = kept([P, PAIR, C1], F32, "sg%d_%d" % (f, h), tag)
-            nc.scalar.activation(sg[f, h][:], av[f, h][:], ACT.Sigmoid)
-
+        dyw = [kept([P, T], I32, "dyw%d" % s) for s in range(PASSES)]
+        load_a(0, 0, placed([P, PAIR, C1], F32, "a0_0", AT_A00))
+        load_words(dyw[0][:], dy_rows[:, 0, :])
+        load_a(0, 1, placed([P, PAIR, C1], F32, "a0_1", AT_A01))
+        load_words(dyw[1][:], dy_rows[:, 1, :])
+        raw = [kept([P, 2 * PASSES, 2 * H], U8, "raw0"), placed([P, 2 * PASSES, 2 * H], U8, "raw1", AT_A01)]
+        load_words(raw[0][:], wet_rows[:, 0:2 * PASSES, :])
         nc.sync.dma_start(offs2_t[:], offs2)
         nc.sync.dma_start(offs_t[:], offs)
-        raw = [kept([P, 2 * PASSES, 2 * H], U8, "raw0"), kept([P, 2 * PASSES, 2 * H], U8, "raw1")]
-        load_words(raw[0][:], wet_rows[:, 0:2 * PASSES, :])
-        dyw = [kept([P, T], I32, "dyw%d" % s) for s in range(PASSES)]
-        for s in range(PASSES):
-            load_words(dyw[s][:], dy_rows[:, s, :])
-        load_a(0, 0, placed([P, PAIR, C1], F32, "a0_0", AT_A00))
-        load_words(raw[1][:], wet_rows[:, 2 * PASSES:, :])
 
         sc_sorted = kept([P, H], U8, "sc_sorted")
         nc.gpsimd.tensor_copy(sc_sorted[:].rearrange("p (r m) -> p r m", r=PACK), sc_rows[:].rearrange("p (m r) -> p r m", r=PACK))
         for q in BY_PORT:
             nc.sync.dma_start(wet_sc[32 * q:32 * q + 4].bitcast(I32), sc_sorted[32 * q:32 * (q + 1), :].bitcast(I32))
-        wet = [placed([P, PASSES, 2 * H], U8, "wet0", AT_U01 + KIB)] + [kept([P, PASSES, 2 * H], U8, "wet%d" % e) for e in range(1, E)]
+        load_a(1, 1, placed([P, PAIR, C1], F32, "a1_1", AT_A11))
 
-        def sort_columns(e):
-            words = raw[e // 2][:, PASSES * (e % 2):PASSES * (e % 2 + 1), :].bitcast(U16)
-            nc.scalar.copy(wet[e][:].bitcast(U16).rearrange("p s (r m) -> p s r m", r=PACK), words.rearrange("p s (m r) -> p s r m", r=PACK))
-
-        sort_columns(0)
-        sort_columns(1)
         picked = kept([P, T], U8, "picked")
         for f in range(G):
             nc.vector.tensor_copy(picked[:, f * C1:(f + 1) * C1], dys[:].indirect(dst_t[:, columns(f * C1, (f + 1) * C1)]))
@@ -128,55 +123,84 @@ def tile_moe_hib_silu_kernel(tc, dy_words, dy_scales, wet_words, wet_scales, wgt
             nc.sync.dma_start(gs[32 * q:32 * q + 4].bitcast(I32), picked[8 * q:8 * q + 8, :].bitcast(I32))
 
         gw = {}
+        for s in range(PASSES):
+            for f in range(G):
+                tile = kept([P, C1], U32, "gw%d_%d" % (s, f))
+                nc.vector.tensor_copy(tile[:], dyw[s][:].bitcast(U32).indirect(dst_t[:, columns(f * C1, (f + 1) * C1)]))
+                for u in (0, C2):
+                    gw[s, (f * C1 + u) // C2] = tile[:, u:u + C2]
 
-        def gather_words(s, lo, hi):
-            tile = kept([P, hi - lo], U32, "gw%d_%d" % (s, lo))
-            nc.vector.tensor_copy(tile[:], dyw[s][:].bitcast(U32).indirect(dst_t[:, columns(lo, hi)]))
-            for e in range(lo // C2, hi // C2):
-                gw[s, e] = tile[:, e * C2 - lo:(e + 1) * C2 - lo]
-
-        gather_words(0, 0, C1)
-        gather_words(1, 0, C2)
-        gather_words(1, C2, C1)
-        gather_words(0, C1, T)
-        gather_words(1, C1, T)
-
-        a_high = placed([P, PAIR, T], F32, "a_high", AT_HIGH)
-        nc.sync.dma_start(a_high[:], a_rows[:, PAIR:, :])
-        for f in range(G):
-            av[f, 1] = a_high[:, :, f * C1:(f + 1) * C1]
-        gate_t = [placed([P, C1], F32, "gate0", AT_GATE0), kept([P, C1], F32, "gate1", "picked")]
-        nc.sync.dma_start(gate_t[0][:], gate[:, 0:C1])
-        nc.sync.dma_start(gate_t[1][:], gate[:, C1:])
         load_a(1, 0, kept([P, PAIR, C1], F32, "a1_0", "dyw0"))
 
-        sigmoid(0, 0)
-        sort_columns(2)
-        sort_columns(3)
+        wet = {}
 
-        zs = [placed([P, PACK, C1], F32, "zs0", AT_ZS0), placed([P, PACK, C1], F32, "zs1", AT_ZS1)]
+        def sort_columns(copy, e, count, tile):
+            first_pass = PASSES * (e % 2)
+            words = raw[e // 2][:, first_pass:first_pass + PASSES * count, :].bitcast(U16)
+            copy(tile[:].bitcast(U16).rearrange("p s (r m) -> p s r m", r=PACK), words.rearrange("p s (m r) -> p s r m", r=PACK))
+            for n in range(count):
+                wet[e + n] = tile[:, PASSES * n:PASSES * (n + 1), :]
+
+        th = {(0, 0): placed([P, PAIR, C1], F32, "th0_0", AT_H00), (0, 1): placed([P, PAIR, C1], F32, "th0_1", AT_H01),
+              (1, 1): kept([P, PAIR, C1], F32, "th1_1"), (1, 0): kept([P, PAIR, C1], F32, "th1_0")}
+        ns = {(0, 0): kept([P, PAIR, C1], F32, "ns0_0"), (0, 1): placed([P, PAIR, C1], F32, "ns0_1", AT_W01),
+              (1, 1): placed([P, PAIR, C1], F32, "ns1_1", AT_W11)}
+        ns_last = [placed([P, C1], F32, "ns1_0_0", AT_W10), kept([P, C1], F32, "ns1_0_1")]
+        sg = {}
+
+        def functions(f, h):
+            nc.scalar.activation(th[f, h][:], av[f, h][:], ACT.Tanh, scale=0.5)
+            nc.scalar.activation(ns[f, h][:], av[f, h][:], ACT.Silu, scale=-1.0)
+
+        functions(0, 0)
+        functions(0, 1)
+        sort_columns(nc.scalar.copy, 0, 1, kept([P, PASSES, 2 * H], U8, "wet0"))
+        functions(1, 1)
+        nc.scalar.activation(th[1, 0][:], av[1, 0][:], ACT.Tanh, scale=0.5)
+        for r in range(PAIR):
+            nc.scalar.activation(ns_last[r][:], av[1, 0][:, r, :], ACT.Silu, scale=-1.0)
+
+        def sigmoid(f, h, tile):
+            sg[f, h] = tile
+            nc.gpsimd.tensor_scalar(tile[:], th[f, h][:], 0.5, 0.5, ALU.mult, ALU.add)
+
+        for h in range(2):
+            sigmoid(0, h, th[0, h])
+
+        gate_early = placed([P, C1], F32, "gate_early", AT_A00)
+        nc.sync.dma_start(gate_early[:], gate[:, 0:C1])
+        gates = [gate_early[:, 0:C2], gate_early[:, C2:]]
+        load_words(raw[1][:], wet_rows[:, 2 * PASSES:, :])
+
+        zs = [kept([P, PACK, C1], F32, "zs0")]
+
+        def half_expert(e, half):
+            f, u = divmod(e * C2, C1)
+            acc = bank([P, PAIR, C2], "acc", 2 * e + half)
+            for n in range(PAIR):
+                r = PAIR * half + n
+                for s in range(PASSES):
+                    nc.tensor.matmul_mx(
+                        out=acc[:, n, :],
+                        lhsT=wet[e][:, s, 2 * P * r:2 * P * (r + 1)].bitcast(FP4X4), lhsT_scale=wet_sc[:, PASSES * e + s, P * r:P * (r + 1)],
+                        rhs=gw[s, e].bitcast(FP8X4), rhs_scale=gs[:, s, e * C2:(e + 1) * C2],
+                        start=(s == 0), stop=(s == PASSES - 1))
+            weight = gates[e].unsqueeze(1).to_broadcast([P, PAIR, C2])
+            nc.vector.scalar_tensor_tensor(zs[f][:, PAIR * half:PAIR * (half + 1), u:u + C2], acc[:], -1.0, weight, ALU.mult, ALU.mult)
 
         def expert(e):
-            f, u = divmod(e * C2, C1)
             for half in range(2):
-                acc = bank([P, PAIR, C2], "acc", 2 * e + half)
-                for n in range(PAIR):
-                    r = PAIR * half + n
-                    for s in range(PASSES):
-                        nc.tensor.matmul_mx(
-                            out=acc[:, n, :],
-                            lhsT=wet[e][:, s, 2 * P * r:2 * P * (r + 1)].bitcast(FP4X4), lhsT_scale=wet_sc[:, PASSES * e + s, P * r:P * (r + 1)],
-                            rhs=gw[s, e].bitcast(FP8X4), rhs_scale=gs[:, s, e * C2:(e + 1) * C2],
-                            start=(s == 0), stop=(s == PASSES - 1))
-                weight = gate_t[f][:, u:u + C2].unsqueeze(1).to_broadcast([P, PAIR, C2])
-                nc.vector.scalar_tensor_tensor(zs[f][:, PAIR * half:PAIR * (half + 1), u:u + C2], acc[:], -1.0, weight, ALU.mult, ALU.mult)
+                half_expert(e, half)
 
-        def derivative_on_vector(f, h, at):
-            u = [placed([P, C1], F32, "u%d_%d_%d" % (f, h, r), at + 2 * KIB * (1 - r)) for r in range(PAIR)]
-            for r in range(PAIR):
-                nc.vector.scalar_tensor_tensor(u[r][:], sg[f, h][:, r, :], 1.0, av[f, h][:, r, :], ALU.subtract, ALU.mult)
-            for r in range(PAIR):
-                nc.vector.scalar_tensor_tensor(sg[f, h][:, r, :], u[r][:], 1.0, sg[f, h][:, r, :], ALU.subtract, ALU.mult)
+        slope = {}
+
+        def derivative(tile, minus_silu, sigm):
+            nc.vector.scalar_tensor_tensor(tile, minus_silu, 1.0, sigm, ALU.subtract, ALU.mult)
+
+        def derivative_pair(f, h, tile):
+            derivative(tile[:], ns[f, h][:], sg[f, h][:])
+            for n in range(PAIR):
+                slope[f, PAIR * h + n] = tile[:, n, :]
 
         def by_vector(window, offsets, lo, hi, values):
             nc.vector.tensor_copy(window[:].indirect(offsets[:, columns(lo, hi)]), values)
@@ -190,7 +214,7 @@ def tile_moe_hib_silu_kernel(tc, dy_words, dy_scales, wet_words, wet_scales, wgt
 
         def gradient(f, zw, grouped, planes):
             for r in planes:
-                nc.gpsimd.tensor_tensor(grouped[:, :, r], zw[r][:, f * C1:(f + 1) * C1], sg[f, r // PAIR][:, r % PAIR, :], ALU.mult)
+                nc.gpsimd.tensor_tensor(grouped[:, :, r], zw[r][:, f * C1:(f + 1) * C1], slope[f, r], ALU.mult)
 
         def second_product(f, grouped):
             codes = kept([P, C1], U32, "codes%d" % f)
@@ -205,56 +229,67 @@ def tile_moe_hib_silu_kernel(tc, dy_words, dy_scales, wet_words, wet_scales, wgt
                     start=True, stop=True)
             return acc2
 
-        sigmoid(0, 1)
-        sigmoid(1, 1)
-        derivative_on_vector(0, 0, AT_U00)
+        sort_columns(nc.vector.tensor_copy, 1, 1, kept([P, PASSES, 2 * H], U8, "wet1"))
+        derivative_pair(0, 0, kept([P, PAIR, C1], F32, "slope0_0", "raw0"))
+        derivative_pair(0, 1, placed([P, PAIR, C1], F32, "slope0_1", AT_H00))
+        sigmoid(1, 1, placed([P, PAIR, C1], F32, "sg1_1", AT_H01))
+        sigmoid(1, 0, placed([P, PAIR, C1], F32, "sg1_0", AT_SG10))
         expert(0)
-        derivative_on_vector(0, 1, AT_U01)
         expert(1)
-        derivative_on_vector(1, 1, AT_U01)
-        zw0 = [placed([P, T], F32, "zw0_0", AT_ZW00), kept([P, C1], F32, "zw0_1"), kept([P, C1], F32, "zw0_2"), placed([P, T], F32, "zw0_3", AT_LAST0)]
+        sort_columns(nc.vector.tensor_copy, 2, 2, placed([P, 2 * PASSES, 2 * H], U8, "wet_late", AT_WET_LATE))
+        derivative_pair(1, 1, placed([P, PAIR, C1], F32, "slope1_1", AT_A01))
+        zw0 = [placed([P, T], F32, "zw0_0", AT_ZW00), kept([P, C1], F32, "zw0_1"), kept([P, C1], F32, "zw0_2"), placed([P, C1], F32, "zw0_3", AT_LAST0)]
         by_vector(zw0[0], offs2_t, 0, C1, zs[0][:, 0, :])
+        gate_late = placed([P, C1], F32, "gate_late", AT_GATE1)
+        nc.sync.dma_start(gate_late[:], gate[:, C1:])
+        gates.extend([gate_late[:, 0:C2], gate_late[:, C2:]])
+        zs.append(placed([P, PACK, C1], F32, "zs1", AT_ZS1))
         expert(2)
         expert(3)
-        wgt = kept([P, G, 2 * K], U8, "wgt", "wet1")
+        wgt = placed([P, G, 2 * K], U8, "wgt", AT_WGT)
         load_words(wgt[:], wgt_words.rearrange("f s p c -> p (f s) c"))
-        wgt_sc = chain.tile([P, G, K], U8, name="wgt_sc", offset=AT_A00, align_bytes=64)
+        wgt_sc = placed([P, G, K], U8, "wgt_sc", AT_WGT + 2 * KIB)
         nc.gpsimd.memset(wgt_sc[:].bitcast(I32), 0)
         load_scales(wgt_sc, wgt_scales.rearrange("f s b k -> (f s) b k"))
 
         for e, r in ((0, 1), (0, 2), (1, 1), (1, 2), (0, 3), (1, 3)):
             scatter_z(by_scalar, zw0, e, r)
-        sigmoid(1, 0, "picked")
-        grouped0 = placed([P, C1, PACK], BF16, "grouped0", AT_U01)
+        grouped0 = kept([P, C1, PACK], BF16, "grouped0", "grouped")
         gradient(0, zw0, grouped0, (1, 2, 0, 3))
 
-        zw1 = [kept([P, T], F32, "zw1_0"), placed([P, T], F32, "zw1_1", AT_LAST1), kept([P, T], F32, "zw1_2"), kept([P, T], F32, "zw1_3")]
+        zw1 = [kept([P, T], F32, "zw1_0"), placed([P, T], F32, "zw1_1", AT_W10), kept([P, T], F32, "zw1_2"), kept([P, T], F32, "zw1_3")]
         by_vector(zw1[0], offs2_t, C1, T, zs[1][:, 0, :])
         for e, r in ((2, 2), (2, 3), (3, 2), (3, 3)):
             scatter_z(by_scalar, zw1, e, r)
         acc2 = second_product(0, grouped0)
-        derivative_on_vector(1, 0, AT_LAST0)
+        last = placed([P, PAIR, C1], F32, "slope1_0", AT_LAST0)
+        for r in range(PAIR):
+            slope[1, r] = last[:, r, :]
+            derivative(last[:, r, :], ns_last[r][:], sg[1, 0][:, r, :])
         by_vector(zw1[1], offs2_t, C1, T, zs[1][:, 1, :])
-        grouped1 = placed([P, C1, PACK], BF16, "grouped1", AT_U01)
+        grouped1 = kept([P, C1, PACK], BF16, "grouped1", "grouped")
         gradient(1, zw1, grouped1, (0, 2, 3, 1))
 
-        ow = [kept([P, T], F32, "ow0"), placed([P, T], F32, "ow1", AT_LAST1), kept([P, T], F32, "ow2"), kept([P, T], F32, "ow3")]
+        ow = [kept([P, T], F32, "ow%d" % c) for c in range(K // P)]
         dxs = [[kept([P, C1], F32, "dxs%d_%d" % (f, c)) for c in range(K // P)] for f in range(G)]
 
         def scatter_dx(by, f, c, lo, hi):
             by(ow[c], offs_t, f * C1 + lo, f * C1 + hi, dxs[f][c][:, lo:hi])
 
-        def leave(f, acc2):
-            for c in (0, 2, 1, 3):
-                nc.scalar.activation(dxs[f][c][:], acc2[c][:], ACT.Copy)
-
-        leave(0, acc2)
+        held = acc2[1]
+        for c in (0, 2):
+            nc.scalar.activation(dxs[0][c][:], acc2[c][:], ACT.Copy)
+        nc.scalar.activation(dxs[0][1][:, 0:EARLY], held[:, 0:EARLY], ACT.Copy)
+        nc.scalar.activation(dxs[0][3][:], acc2[3][:], ACT.Copy)
         scatter_dx(by_vector, 0, 0, 0, C1)
+        scatter_dx(by_vector, 0, 1, 0, EARLY)
         for lo in (0, C2):
             for c in (2, 3):
                 scatter_dx(by_scalar, 0, c, lo, lo + C2)
         acc2 = second_product(1, grouped1)
-        scatter_dx(by_vector, 0, 1, 0, C1)
+        dx_late = placed([P, C1 - EARLY], F32, "dx_late", AT_W10)
+        nc.vector.tensor_copy(dx_late[:], held[:, EARLY:])
+        by_vector(ow[1], offs_t, EARLY, C1, dx_late[:])
         for c in (0, 2, 3):
             nc.scalar.activation(dxs[1][c][:], acc2[c][:], ACT.Copy)
         nc.vector.tensor_copy(dxs[1][1][:], acc2[1][:])

@@ -26,21 +26,28 @@ QUADS = 4
 KIB = 1024
 EARLY = 192
 AT_A11 = 0
-AT_SC_ROWS = AT_A11 + 4 * KIB - 64
-AT_A01 = 15 * KIB
-AT_A00 = 24 * KIB
-AT_WET_LATE = AT_A00 - 4 * KIB + 64
-AT_H00 = 34 * KIB
-AT_H01 = 42 * KIB
-AT_ZW00 = AT_H01 - 2 * KIB
-AT_LAST0 = AT_H01 + 2 * KIB
-AT_W11 = 52 * KIB
+AT_DYS = AT_A11 + 4 * KIB - 64
+AT_SC_SORTED = AT_DYS + T - 64
+AT_A01 = 16 * KIB
+AT_GATE0 = AT_A01 - 2 * KIB + 64
+AT_WET_LATE = AT_GATE0 - 4 * KIB + 64
+AT_A00 = AT_WET_LATE - 4 * KIB + 64
+AT_WET_SC1 = AT_A01 + 64
+AT_GS1 = AT_WET_SC1 + 2 * KIB
+AT_RAW1 = AT_GS1 + KIB
+AT_H00 = 28 * KIB
+AT_SG11 = 42 * KIB
+AT_H01 = AT_SG11 - 4 * KIB + 64
+AT_SG10 = AT_H01 - 4 * KIB + 64
+AT_ZW00 = AT_SG11 - 2 * KIB
+AT_LAST0 = AT_SG11 + 2 * KIB
+AT_GATE1 = AT_LAST0 + 3 * KIB
+AT_CODES0 = AT_LAST0 + 4 * KIB
+AT_W01 = AT_GATE1 + 2 * KIB - 64
+AT_WGT = AT_CODES0 + 2 * KIB
+AT_W11 = 54 * KIB
 AT_ZS1 = AT_W11 + 64
-AT_W10 = 62 * KIB
-AT_W01 = 68 * KIB
-AT_GATE1 = AT_W01 - 2 * KIB + 64
-AT_WGT = AT_W01 + 64
-AT_SG10 = AT_WGT + 3 * KIB
+AT_W10 = 64 * KIB
 
 
 def tile_moe_hib_silu_kernel(tc, dy_words, dy_scales, wet_words, wet_scales, wgt_words, wgt_scales, a, gate, offs, offs2, dst, out):
@@ -74,16 +81,16 @@ def tile_moe_hib_silu_kernel(tc, dy_words, dy_scales, wet_words, wet_scales, wgt
         wet_rows = wet_words.rearrange("e s p c -> p (e s) c")
         dy_rows = dy_words.rearrange("s p t d -> p s (t d)")
 
-        wet_sc = kept([P, E * PASSES, H], U8, "wet_sc")
-        dys = kept([P, T], U8, "dys")
-        gs = kept([P, PASSES, T], U8, "gs")
-        nc.vector.memset(wet_sc[:].bitcast(I32), 0)
+        wet_sc = [kept([P, 2 * PASSES, H], U8, "wet_sc0")]
+        dys = placed([P, T], U8, "dys", AT_DYS)
+        gs = [kept([P, PASSES, C1], U8, "gs0")]
+        nc.vector.memset(wet_sc[0][:].bitcast(I32), 0)
         unread = kept([P, 2], F32, "unread")
         nc.gpsimd.memset(unread[:, 0:1], 0.0)
         nc.scalar.activation(unread[:, 1:2], unread[:, 0:1], ACT.Silu)
         nc.gpsimd.memset(dys[32:64, :].bitcast(I32), 0)
         nc.gpsimd.memset(dys[64:P, :].bitcast(I32), 0)
-        nc.gpsimd.memset(gs[:].bitcast(I32), 0)
+        nc.gpsimd.memset(gs[0][:].bitcast(I32), 0)
 
         dst_t = lists.tile([P, T // LIST], U16, name="dst_t")
         offs2_t = lists.tile([P, T // LIST], U16, name="offs2_t")
@@ -91,8 +98,9 @@ def tile_moe_hib_silu_kernel(tc, dy_words, dy_scales, wet_words, wet_scales, wgt
         nc.sync.dma_start(dst_t[:], dst)
         nc.sync.dma_start(dys[0:32, :].bitcast(I32), dy_scales.rearrange("s r t -> r s t").bitcast(I32))
 
-        sc_rows = placed([P, H], U8, "sc_rows", AT_SC_ROWS)
-        nc.sync.dma_start(sc_rows[:].bitcast(I32), wet_scales.rearrange("e s b i -> b (e s) i").bitcast(I32))
+        sc_rows = kept([P, H], U8, "sc_rows")
+        for f in range(G):
+            nc.sync.dma_start(sc_rows[64 * f:64 * (f + 1), :].bitcast(I32), wet_scales[2 * f:2 * (f + 1)].rearrange("e s b i -> b (e s) i").bitcast(I32))
 
         av = {}
 
@@ -103,24 +111,30 @@ def tile_moe_hib_silu_kernel(tc, dy_words, dy_scales, wet_words, wet_scales, wgt
         dyw = [kept([P, T], I32, "dyw%d" % s) for s in range(PASSES)]
         load_a(0, 0, placed([P, PAIR, C1], F32, "a0_0", AT_A00))
         load_words(dyw[0][:], dy_rows[:, 0, :])
-        load_a(0, 1, placed([P, PAIR, C1], F32, "a0_1", AT_A01))
-        load_words(dyw[1][:], dy_rows[:, 1, :])
-        raw = [kept([P, 2 * PASSES, 2 * H], U8, "raw0"), placed([P, 2 * PASSES, 2 * H], U8, "raw1", AT_A01)]
-        load_words(raw[0][:], wet_rows[:, 0:2 * PASSES, :])
         nc.sync.dma_start(offs2_t[:], offs2)
         nc.sync.dma_start(offs_t[:], offs)
+        load_a(0, 1, placed([P, PAIR, C1], F32, "a0_1", AT_A01))
+        load_words(dyw[1][:], dy_rows[:, 1, :])
+        raw = [kept([P, 2 * PASSES, 2 * H], U8, "raw0"), placed([P, 2 * PASSES, 2 * H], U8, "raw1", AT_RAW1)]
+        load_words(raw[0][:], wet_rows[:, 0:2 * PASSES, :])
 
-        sc_sorted = kept([P, H], U8, "sc_sorted")
-        nc.gpsimd.tensor_copy(sc_sorted[:].rearrange("p (r m) -> p r m", r=PACK), sc_rows[:].rearrange("p (m r) -> p r m", r=PACK))
-        for q in BY_PORT:
-            nc.sync.dma_start(wet_sc[32 * q:32 * q + 4].bitcast(I32), sc_sorted[32 * q:32 * (q + 1), :].bitcast(I32))
-        load_a(1, 1, placed([P, PAIR, C1], F32, "a1_1", AT_A11))
-
-        picked = kept([P, T], U8, "picked")
+        picked = [kept([P, C1], U8, "picked%d" % f) for f in range(G)]
         for f in range(G):
-            nc.vector.tensor_copy(picked[:, f * C1:(f + 1) * C1], dys[:].indirect(dst_t[:, columns(f * C1, (f + 1) * C1)]))
-        for q in BY_PORT:
-            nc.sync.dma_start(gs[32 * q:32 * q + 4].bitcast(I32), picked[8 * q:8 * q + 8, :].bitcast(I32))
+            nc.vector.tensor_copy(picked[f][:], dys[:].indirect(dst_t[:, columns(f * C1, (f + 1) * C1)]))
+        sc_sorted = placed([P, H], U8, "sc_sorted", AT_SC_SORTED)
+        nc.gpsimd.tensor_copy(sc_sorted[:].rearrange("p (r m) -> p r m", r=PACK), sc_rows[:].rearrange("p (m r) -> p r m", r=PACK))
+
+        def place_picked(f):
+            for q in BY_PORT:
+                nc.sync.dma_start(gs[f][32 * q:32 * q + 4].bitcast(I32), picked[f][8 * q:8 * q + 8, :].bitcast(I32))
+
+        def place_sorted(f):
+            for q in BY_PORT:
+                nc.sync.dma_start(wet_sc[f][32 * q:32 * q + 4].bitcast(I32), sc_sorted[64 * f + 16 * q:64 * f + 16 * (q + 1), :].bitcast(I32))
+
+        place_picked(0)
+        load_a(1, 1, placed([P, PAIR, C1], F32, "a1_1", AT_A11))
+        place_sorted(0)
 
         gw = {}
         for s in range(PASSES):
@@ -130,7 +144,7 @@ def tile_moe_hib_silu_kernel(tc, dy_words, dy_scales, wet_words, wet_scales, wgt
                 for u in (0, C2):
                     gw[s, (f * C1 + u) // C2] = tile[:, u:u + C2]
 
-        load_a(1, 0, kept([P, PAIR, C1], F32, "a1_0", "dyw0"))
+        load_a(1, 0, placed([P, PAIR, C1], F32, "a1_0", AT_A00))
 
         wet = {}
 
@@ -167,10 +181,16 @@ def tile_moe_hib_silu_kernel(tc, dy_words, dy_scales, wet_words, wet_scales, wgt
         for h in range(2):
             sigmoid(0, h, th[0, h])
 
-        gate_early = placed([P, C1], F32, "gate_early", AT_A00)
+        gate_early = placed([P, C1], F32, "gate_early", AT_GATE0)
         nc.sync.dma_start(gate_early[:], gate[:, 0:C1])
         gates = [gate_early[:, 0:C2], gate_early[:, C2:]]
         load_words(raw[1][:], wet_rows[:, 2 * PASSES:, :])
+        wet_sc.append(placed([P, 2 * PASSES, H], U8, "wet_sc1", AT_WET_SC1))
+        gs.append(placed([P, PASSES, C1], U8, "gs1", AT_GS1))
+        nc.gpsimd.memset(wet_sc[1][:].bitcast(I32), 0)
+        nc.gpsimd.memset(gs[1][:].bitcast(I32), 0)
+        place_sorted(1)
+        place_picked(1)
 
         zs = [kept([P, PACK, C1], F32, "zs0")]
 
@@ -182,8 +202,8 @@ def tile_moe_hib_silu_kernel(tc, dy_words, dy_scales, wet_words, wet_scales, wgt
                 for s in range(PASSES):
                     nc.tensor.matmul_mx(
                         out=acc[:, n, :],
-                        lhsT=wet[e][:, s, 2 * P * r:2 * P * (r + 1)].bitcast(FP4X4), lhsT_scale=wet_sc[:, PASSES * e + s, P * r:P * (r + 1)],
-                        rhs=gw[s, e].bitcast(FP8X4), rhs_scale=gs[:, s, e * C2:(e + 1) * C2],
+                        lhsT=wet[e][:, s, 2 * P * r:2 * P * (r + 1)].bitcast(FP4X4), lhsT_scale=wet_sc[f][:, PASSES * (e % 2) + s, P * r:P * (r + 1)],
+                        rhs=gw[s, e].bitcast(FP8X4), rhs_scale=gs[f][:, s, u:u + C2],
                         start=(s == 0), stop=(s == PASSES - 1))
             weight = gates[e].unsqueeze(1).to_broadcast([P, PAIR, C2])
             nc.vector.scalar_tensor_tensor(zs[f][:, PAIR * half:PAIR * (half + 1), u:u + C2], acc[:], -1.0, weight, ALU.mult, ALU.mult)
@@ -216,8 +236,7 @@ def tile_moe_hib_silu_kernel(tc, dy_words, dy_scales, wet_words, wet_scales, wgt
             for r in planes:
                 nc.gpsimd.tensor_tensor(grouped[:, :, r], zw[r][:, f * C1:(f + 1) * C1], slope[f, r], ALU.mult)
 
-        def second_product(f, grouped):
-            codes = kept([P, C1], U32, "codes%d" % f)
+        def second_product(f, grouped, codes):
             scales = kept([P, C1], U8, "scales%d" % f)
             nc.vector.quantize_mx(out=codes[:].bitcast(FP8X4), scales=scales[:], in_=grouped[:].rearrange("p j r -> p (j r)"))
             acc2 = [bank([P, C1], "acc2", 4 * f + c) for c in range(K // P)]
@@ -232,12 +251,12 @@ def tile_moe_hib_silu_kernel(tc, dy_words, dy_scales, wet_words, wet_scales, wgt
         sort_columns(nc.vector.tensor_copy, 1, 1, kept([P, PASSES, 2 * H], U8, "wet1"))
         derivative_pair(0, 0, kept([P, PAIR, C1], F32, "slope0_0", "raw0"))
         derivative_pair(0, 1, placed([P, PAIR, C1], F32, "slope0_1", AT_H00))
-        sigmoid(1, 1, placed([P, PAIR, C1], F32, "sg1_1", AT_H01))
+        sigmoid(1, 1, placed([P, PAIR, C1], F32, "sg1_1", AT_SG11))
         sigmoid(1, 0, placed([P, PAIR, C1], F32, "sg1_0", AT_SG10))
         expert(0)
         expert(1)
         sort_columns(nc.vector.tensor_copy, 2, 2, placed([P, 2 * PASSES, 2 * H], U8, "wet_late", AT_WET_LATE))
-        derivative_pair(1, 1, placed([P, PAIR, C1], F32, "slope1_1", AT_A01))
+        derivative_pair(1, 1, placed([P, PAIR, C1], F32, "slope1_1", AT_RAW1))
         zw0 = [placed([P, T], F32, "zw0_0", AT_ZW00), kept([P, C1], F32, "zw0_1"), kept([P, C1], F32, "zw0_2"), placed([P, C1], F32, "zw0_3", AT_LAST0)]
         by_vector(zw0[0], offs2_t, 0, C1, zs[0][:, 0, :])
         gate_late = placed([P, C1], F32, "gate_late", AT_GATE1)
@@ -261,7 +280,7 @@ def tile_moe_hib_silu_kernel(tc, dy_words, dy_scales, wet_words, wet_scales, wgt
         by_vector(zw1[0], offs2_t, C1, T, zs[1][:, 0, :])
         for e, r in ((2, 2), (2, 3), (3, 2), (3, 3)):
             scatter_z(by_scalar, zw1, e, r)
-        acc2 = second_product(0, grouped0)
+        acc2 = second_product(0, grouped0, placed([P, C1], U32, "codes0", AT_CODES0))
         last = placed([P, PAIR, C1], F32, "slope1_0", AT_LAST0)
         for r in range(PAIR):
             slope[1, r] = last[:, r, :]
@@ -286,7 +305,7 @@ def tile_moe_hib_silu_kernel(tc, dy_words, dy_scales, wet_words, wet_scales, wgt
         for lo in (0, C2):
             for c in (2, 3):
                 scatter_dx(by_scalar, 0, c, lo, lo + C2)
-        acc2 = second_product(1, grouped1)
+        acc2 = second_product(1, grouped1, kept([P, C1], U32, "codes1"))
         dx_late = placed([P, C1 - EARLY], F32, "dx_late", AT_W10)
         nc.vector.tensor_copy(dx_late[:], held[:, EARLY:])
         by_vector(ow[1], offs_t, EARLY, C1, dx_late[:])

@@ -24,30 +24,30 @@ LIST = 16
 BY_PORT = (0, 2, 1, 3)
 QUADS = 4
 KIB = 1024
-EARLY = 192
+EARLY = 224
 AT_A11 = 0
 AT_DYS = AT_A11 + 4 * KIB - 64
 AT_SC_SORTED = AT_DYS + T - 64
 AT_A01 = 16 * KIB
 AT_GATE0 = AT_A01 - 2 * KIB + 64
-AT_WET_LATE = AT_GATE0 - 4 * KIB + 64
-AT_A00 = AT_WET_LATE - 4 * KIB + 64
 AT_WET_SC1 = AT_A01 + 64
 AT_GS1 = AT_WET_SC1 + 2 * KIB
 AT_RAW1 = AT_GS1 + KIB
-AT_H00 = 28 * KIB
-AT_SG11 = 42 * KIB
-AT_H01 = AT_SG11 - 4 * KIB + 64
-AT_SG10 = AT_H01 - 4 * KIB + 64
-AT_ZW00 = AT_SG11 - 2 * KIB
-AT_LAST0 = AT_SG11 + 2 * KIB
-AT_GATE1 = AT_LAST0 + 3 * KIB
-AT_CODES0 = AT_LAST0 + 4 * KIB
-AT_W01 = AT_GATE1 + 2 * KIB - 64
-AT_WGT = AT_CODES0 + 2 * KIB
-AT_W11 = 54 * KIB
-AT_ZS1 = AT_W11 + 64
-AT_W10 = 64 * KIB
+AT_SG10 = 34 * KIB
+AT_H01 = AT_SG10 - 64
+AT_SG11 = AT_H01 - 4 * KIB + 64
+AT_ZW00 = AT_SG10
+AT_W10 = 42 * KIB
+AT_LAST0 = AT_W10 - 2 * KIB + 64
+AT_LAST1 = AT_LAST0 - 2 * KIB
+AT_ZS1 = AT_W10 + 64
+AT_W01 = 54 * KIB
+AT_GATE1 = AT_W01 - 2 * KIB + 64
+AT_WGT = AT_W01 + 64
+AT_ZS0 = AT_WGT + 3 * KIB
+AT_A00 = 72 * KIB
+AT_SLOPE11 = AT_A00 - 4 * KIB + 64
+AT_WET_LATE = AT_A00 + 4 * KIB - 64
 
 
 def tile_moe_hib_silu_kernel(tc, dy_words, dy_scales, wet_words, wet_scales, wgt_words, wgt_scales, a, gate, offs, offs2, dst, out):
@@ -112,11 +112,11 @@ def tile_moe_hib_silu_kernel(tc, dy_words, dy_scales, wet_words, wet_scales, wgt
         load_a(0, 0, placed([P, PAIR, C1], F32, "a0_0", AT_A00))
         load_words(dyw[0][:], dy_rows[:, 0, :])
         nc.sync.dma_start(offs2_t[:], offs2)
-        nc.sync.dma_start(offs_t[:], offs)
         load_a(0, 1, placed([P, PAIR, C1], F32, "a0_1", AT_A01))
         load_words(dyw[1][:], dy_rows[:, 1, :])
         raw = [kept([P, 2 * PASSES, 2 * H], U8, "raw0"), placed([P, 2 * PASSES, 2 * H], U8, "raw1", AT_RAW1)]
         load_words(raw[0][:], wet_rows[:, 0:2 * PASSES, :])
+        nc.sync.dma_start(offs_t[:], offs)
 
         picked = [kept([P, C1], U8, "picked%d" % f) for f in range(G)]
         for f in range(G):
@@ -155,11 +155,10 @@ def tile_moe_hib_silu_kernel(tc, dy_words, dy_scales, wet_words, wet_scales, wgt
             for n in range(count):
                 wet[e + n] = tile[:, PASSES * n:PASSES * (n + 1), :]
 
-        th = {(0, 0): placed([P, PAIR, C1], F32, "th0_0", AT_H00), (0, 1): placed([P, PAIR, C1], F32, "th0_1", AT_H01),
-              (1, 1): kept([P, PAIR, C1], F32, "th1_1"), (1, 0): kept([P, PAIR, C1], F32, "th1_0")}
+        th = {(0, 0): kept([P, PAIR, C1], F32, "th0_0"), (0, 1): placed([P, PAIR, C1], F32, "th0_1", AT_H01),
+              (1, 1): kept([P, PAIR, C1], F32, "th1_1"), (1, 0): kept([P, PAIR, C1], F32, "th1_0", "grouped")}
         ns = {(0, 0): kept([P, PAIR, C1], F32, "ns0_0"), (0, 1): placed([P, PAIR, C1], F32, "ns0_1", AT_W01),
-              (1, 1): placed([P, PAIR, C1], F32, "ns1_1", AT_W11)}
-        ns_last = [placed([P, C1], F32, "ns1_0_0", AT_W10), kept([P, C1], F32, "ns1_0_1")]
+              (1, 1): kept([P, PAIR, C1], F32, "ns1_1"), (1, 0): placed([P, PAIR, C1], F32, "ns1_0", AT_W10)}
         sg = {}
 
         def functions(f, h):
@@ -170,9 +169,7 @@ def tile_moe_hib_silu_kernel(tc, dy_words, dy_scales, wet_words, wet_scales, wgt
         functions(0, 1)
         sort_columns(nc.scalar.copy, 0, 1, kept([P, PASSES, 2 * H], U8, "wet0"))
         functions(1, 1)
-        nc.scalar.activation(th[1, 0][:], av[1, 0][:], ACT.Tanh, scale=0.5)
-        for r in range(PAIR):
-            nc.scalar.activation(ns_last[r][:], av[1, 0][:, r, :], ACT.Silu, scale=-1.0)
+        functions(1, 0)
 
         def sigmoid(f, h, tile):
             sg[f, h] = tile
@@ -192,7 +189,7 @@ def tile_moe_hib_silu_kernel(tc, dy_words, dy_scales, wet_words, wet_scales, wgt
         place_sorted(1)
         place_picked(1)
 
-        zs = [kept([P, PACK, C1], F32, "zs0")]
+        zs = [placed([P, PACK, C1], F32, "zs0", AT_ZS0)]
 
         def half_expert(e, half):
             f, u = divmod(e * C2, C1)
@@ -249,14 +246,15 @@ def tile_moe_hib_silu_kernel(tc, dy_words, dy_scales, wet_words, wet_scales, wgt
             return acc2
 
         sort_columns(nc.vector.tensor_copy, 1, 1, kept([P, PASSES, 2 * H], U8, "wet1"))
-        derivative_pair(0, 0, kept([P, PAIR, C1], F32, "slope0_0", "raw0"))
-        derivative_pair(0, 1, placed([P, PAIR, C1], F32, "slope0_1", AT_H00))
+        derivative_pair(0, 0, kept([P, PAIR, C1], F32, "slope0_0", "dyw1"))
+        derivative_pair(0, 1, kept([P, PAIR, C1], F32, "slope0_1", "raw0"))
         sigmoid(1, 1, placed([P, PAIR, C1], F32, "sg1_1", AT_SG11))
         sigmoid(1, 0, placed([P, PAIR, C1], F32, "sg1_0", AT_SG10))
         expert(0)
         expert(1)
+        derivative_pair(1, 1, placed([P, PAIR, C1], F32, "slope1_1", AT_SLOPE11))
+        derivative_pair(1, 0, kept([P, PAIR, C1], F32, "slope1_0"))
         sort_columns(nc.vector.tensor_copy, 2, 2, placed([P, 2 * PASSES, 2 * H], U8, "wet_late", AT_WET_LATE))
-        derivative_pair(1, 1, placed([P, PAIR, C1], F32, "slope1_1", AT_RAW1))
         zw0 = [placed([P, T], F32, "zw0_0", AT_ZW00), kept([P, C1], F32, "zw0_1"), kept([P, C1], F32, "zw0_2"), placed([P, C1], F32, "zw0_3", AT_LAST0)]
         by_vector(zw0[0], offs2_t, 0, C1, zs[0][:, 0, :])
         gate_late = placed([P, C1], F32, "gate_late", AT_GATE1)
@@ -276,15 +274,11 @@ def tile_moe_hib_silu_kernel(tc, dy_words, dy_scales, wet_words, wet_scales, wgt
         grouped0 = kept([P, C1, PACK], BF16, "grouped0", "grouped")
         gradient(0, zw0, grouped0, (1, 2, 0, 3))
 
-        zw1 = [kept([P, T], F32, "zw1_0"), placed([P, T], F32, "zw1_1", AT_W10), kept([P, T], F32, "zw1_2"), kept([P, T], F32, "zw1_3")]
+        zw1 = [kept([P, T], F32, "zw1_0"), placed([P, T], F32, "zw1_1", AT_LAST1), kept([P, T], F32, "zw1_2"), kept([P, T], F32, "zw1_3")]
         by_vector(zw1[0], offs2_t, C1, T, zs[1][:, 0, :])
         for e, r in ((2, 2), (2, 3), (3, 2), (3, 3)):
             scatter_z(by_scalar, zw1, e, r)
-        acc2 = second_product(0, grouped0, placed([P, C1], U32, "codes0", AT_CODES0))
-        last = placed([P, PAIR, C1], F32, "slope1_0", AT_LAST0)
-        for r in range(PAIR):
-            slope[1, r] = last[:, r, :]
-            derivative(last[:, r, :], ns_last[r][:], sg[1, 0][:, r, :])
+        acc2 = second_product(0, grouped0, placed([P, C1], U32, "codes0", AT_GATE1))
         by_vector(zw1[1], offs2_t, C1, T, zs[1][:, 1, :])
         grouped1 = kept([P, C1, PACK], BF16, "grouped1", "grouped")
         gradient(1, zw1, grouped1, (0, 2, 3, 1))
@@ -305,9 +299,9 @@ def tile_moe_hib_silu_kernel(tc, dy_words, dy_scales, wet_words, wet_scales, wgt
         for lo in (0, C2):
             for c in (2, 3):
                 scatter_dx(by_scalar, 0, c, lo, lo + C2)
-        acc2 = second_product(1, grouped1, kept([P, C1], U32, "codes1"))
-        dx_late = placed([P, C1 - EARLY], F32, "dx_late", AT_W10)
+        dx_late = placed([P, C1 - EARLY], F32, "dx_late", AT_LAST1)
         nc.vector.tensor_copy(dx_late[:], held[:, EARLY:])
+        acc2 = second_product(1, grouped1, kept([P, C1], U32, "codes1"))
         by_vector(ow[1], offs_t, EARLY, C1, dx_late[:])
         for c in (0, 2, 3):
             nc.scalar.activation(dxs[1][c][:], acc2[c][:], ACT.Copy)

@@ -24,7 +24,7 @@ LIST = 16
 BY_PORT = (0, 2, 1, 3)
 QUADS = 4
 KIB = 1024
-EARLY = 224
+EARLY = 192
 AT_A11 = 0
 AT_DYS = AT_A11 + 4 * KIB - 64
 AT_SC_SORTED = AT_DYS + T - 64
@@ -85,9 +85,6 @@ def tile_moe_hib_silu_kernel(tc, dy_words, dy_scales, wet_words, wet_scales, wgt
         dys = placed([P, T], U8, "dys", AT_DYS)
         gs = [kept([P, PASSES, C1], U8, "gs0")]
         nc.vector.memset(wet_sc[0][:].bitcast(I32), 0)
-        unread = kept([P, 2], F32, "unread")
-        nc.gpsimd.memset(unread[:, 0:1], 0.0)
-        nc.scalar.activation(unread[:, 1:2], unread[:, 0:1], ACT.Silu)
         nc.gpsimd.memset(dys[32:64, :].bitcast(I32), 0)
         nc.gpsimd.memset(dys[64:P, :].bitcast(I32), 0)
         nc.gpsimd.memset(gs[0][:].bitcast(I32), 0)
@@ -165,7 +162,8 @@ def tile_moe_hib_silu_kernel(tc, dy_words, dy_scales, wet_words, wet_scales, wgt
             nc.scalar.activation(th[f, h][:], av[f, h][:], ACT.Tanh, scale=0.5)
             nc.scalar.activation(ns[f, h][:], av[f, h][:], ACT.Silu, scale=-1.0)
 
-        functions(0, 0)
+        nc.scalar.activation(ns[0, 0][:], av[0, 0][:], ACT.Silu, scale=-1.0)
+        nc.scalar.activation(th[0, 0][:], av[0, 0][:], ACT.Tanh, scale=0.5)
         functions(0, 1)
         sort_columns(nc.scalar.copy, 0, 1, kept([P, PASSES, 2 * H], U8, "wet0"))
         functions(1, 1)

from contextlib import ExitStack

import concourse.mybir as mybir

K, T, G, C1, E, C2, H, N = 512, 1024, 2, 512, 4, 256, 512, 1024
FLOPS = 2 * T * N * H + 2 * T * H * K

F32 = mybir.dt.float32
BF16 = mybir.dt.bfloat16
I32 = mybir.dt.int32
U32 = mybir.dt.uint32
U16 = mybir.dt.uint16
U8 = mybir.dt.uint8
FP8X4 = mybir.dt.float8_e4m3fn_x4
FP4X4 = mybir.dt.float4_e2m1fn_x4
ACT = mybir.ActivationFunctionType
ALU = mybir.AluOpType

P = 128
PACK = 4
PAIR = 2
PASSES = N // (P * PACK)
LIST = 16
BY_PORT = (0, 2, 1, 3)
QUADS = 4
KIB = 1024
EARLY = 192
AT_A11 = 0
AT_DYS = AT_A11 + 4 * KIB - 64
AT_SC_SORTED = AT_DYS + T - 64
AT_A01 = 16 * KIB
AT_GATE0 = AT_A01 - 2 * KIB + 64
AT_WET_SC1 = AT_A01 + 64
AT_GS1 = AT_WET_SC1 + 2 * KIB
AT_RAW1 = AT_GS1 + KIB
AT_SG10 = 34 * KIB
AT_H01 = AT_SG10 - 64
AT_SG11 = AT_H01 - 4 * KIB + 64
AT_ZW00 = AT_SG10
AT_W10 = 42 * KIB
AT_LAST0 = AT_W10 - 2 * KIB + 64
AT_LAST1 = AT_LAST0 - 2 * KIB
AT_ZS1 = AT_W10 + 64
AT_W01 = 54 * KIB
AT_GATE1 = AT_W01 - 2 * KIB + 64
AT_WGT = AT_W01 + 64
AT_ZS0 = AT_WGT + 3 * KIB
AT_A00 = 72 * KIB
AT_SLOPE11 = AT_A00 - 4 * KIB + 64
AT_WET_LATE = AT_A00 + 4 * KIB - 64


def tile_moe_hib_silu_kernel(tc, dy_words, dy_scales, wet_words, wet_scales, wgt_words, wgt_scales, a, gate, offs, offs2, dst, out):
    nc = tc.nc
    with ExitStack() as ctx:
        lists = ctx.enter_context(tc.tile_pool(name="lists", bufs=1))
        chain = ctx.enter_context(tc.tile_pool(name="chain", bufs=1))
        keep = ctx.enter_context(tc.tile_pool(name="keep", bufs=1))
        ps = ctx.enter_context(tc.psum_pool(name="ps", bufs=1))

        def kept(shape, dtype, name, tag=None):
            return keep.tile(shape, dtype, name=name, tag=tag or name, align_bytes=64)

        def placed(shape, dtype, name, at):
            return chain.tile(shape, dtype, name=name, offset=at, align_bytes=64)

        def bank(shape, name, n):
            return ps.tile(shape, F32, name=name, tag="bank%d" % n)

        def load_words(tile, words):
            nc.sync.dma_start(tile.bitcast(I32), words.bitcast(I32))

        def load_scales(tile, scales):
            for q in BY_PORT:
                nc.sync.dma_start(tile[32 * q:32 * q + 4].bitcast(I32), scales[:, 4 * q:4 * q + 4, :].rearrange("s b t -> b s t").bitcast(I32))

        def columns(lo, hi):
            return slice(lo // LIST, hi // LIST)

        a_rows = a.rearrange("(p r) j -> p r j", r=PACK)
        wet_rows = wet_words.rearrange("e s p c -> p (e s) c")
        dy_rows = dy_words.rearrange("s p t d -> p s (t d)")

        wet_sc = [kept([P, 2 * PASSES, H], U8, "wet_sc0")]
        dys = placed([P, T], U8, "dys", AT_DYS)
        gs = [kept([P, PASSES, C1], U8, "gs0")]
        nc.vector.memset(wet_sc[0][:].bitcast(I32), 0)
        nc.gpsimd.memset(dys[32:64, :].bitcast(I32), 0)
        nc.gpsimd.memset(dys[64:P, :].bitcast(I32), 0)
        nc.gpsimd.memset(gs[0][:].bitcast(I32), 0)

        dst_t = lists.tile([P, T // LIST], U16, name="dst_t")
        offs2_t = lists.tile([P, T // LIST], U16, name="offs2_t")
        offs_t = lists.tile([P, T // LIST], U16, name="offs_t")
        nc.sync.dma_start(dst_t[:], dst)
        nc.sync.dma_start(dys[0:32, :].bitcast(I32), dy_scales.rearrange("s r t -> r s t").bitcast(I32))

        sc_rows = kept([P, H], U8, "sc_rows")
        for f in range(G):
            nc.sync.dma_start(sc_rows[64 * f:64 * (f + 1), :].bitcast(I32), wet_scales[2 * f:2 * (f + 1)].rearrange("e s b i -> b (e s) i").bitcast(I32))

        av = {}

        def load_a(f, h, tile):
            av[f, h] = tile
            nc.sync.dma_start(av[f, h][:], a_rows[:, PAIR * h:PAIR * (h + 1), f * C1:(f + 1) * C1])

        dyw = [kept([P, T], I32, "dyw%d" % s) for s in range(PASSES)]
        load_a(0, 0, placed([P, PAIR, C1], F32, "a0_0", AT_A00))
        load_words(dyw[0][:], dy_rows[:, 0, :])
        nc.sync.dma_start(offs2_t[:], offs2)
        load_a(0, 1, placed([P, PAIR, C1], F32, "a0_1", AT_A01))
        load_words(dyw[1][:], dy_rows[:, 1, :])
        raw = [kept([P, 2 * PASSES, 2 * H], U8, "raw0"), placed([P, 2 * PASSES, 2 * H], U8, "raw1", AT_RAW1)]
        load_words(raw[0][:], wet_rows[:, 0:2 * PASSES, :])
        nc.sync.dma_start(offs_t[:], offs)

        picked = [kept([P, C1], U8, "picked%d" % f) for f in range(G)]
        for f in range(G):
            nc.vector.tensor_copy(picked[f][:], dys[:].indirect(dst_t[:, columns(f * C1, (f + 1) * C1)]))
        sc_sorted = placed([P, H], U8, "sc_sorted", AT_SC_SORTED)
        nc.gpsimd.tensor_copy(sc_sorted[:].rearrange("p (r m) -> p r m", r=PACK), sc_rows[:].rearrange("p (m r) -> p r m", r=PACK))

        def place_picked(f):
            for q in BY_PORT:
                nc.sync.dma_start(gs[f][32 * q:32 * q + 4].bitcast(I32), picked[f][8 * q:8 * q + 8, :].bitcast(I32))

        def place_sorted(f):
            for q in BY_PORT:
                nc.sync.dma_start(wet_sc[f][32 * q:32 * q + 4].bitcast(I32), sc_sorted[64 * f + 16 * q:64 * f + 16 * (q + 1), :].bitcast(I32))

        place_picked(0)
        load_a(1, 1, placed([P, PAIR, C1], F32, "a1_1", AT_A11))
        place_sorted(0)

        gw = {}
        for s in range(PASSES):
            for f in range(G):
                tile = kept([P, C1], U32, "gw%d_%d" % (s, f))
                nc.vector.tensor_copy(tile[:], dyw[s][:].bitcast(U32).indirect(dst_t[:, columns(f * C1, (f + 1) * C1)]))
                for u in (0, C2):
                    gw[s, (f * C1 + u) // C2] = tile[:, u:u + C2]

        load_a(1, 0, placed([P, PAIR, C1], F32, "a1_0", AT_A00))

        wet = {}

        def sort_columns(copy, e, count, tile):
            first_pass = PASSES * (e % 2)
            words = raw[e // 2][:, first_pass:first_pass + PASSES * count, :].bitcast(U16)
            copy(tile[:].bitcast(U16).rearrange("p s (r m) -> p s r m", r=PACK), words.rearrange("p s (m r) -> p s r m", r=PACK))
            for n in range(count):
                wet[e + n] = tile[:, PASSES * n:PASSES * (n + 1), :]

        th = {(0, 0): kept([P, PAIR, C1], F32, "th0_0"), (0, 1): placed([P, PAIR, C1], F32, "th0_1", AT_H01),
              (1, 1): kept([P, PAIR, C1], F32, "th1_1"), (1, 0): kept([P, PAIR, C1], F32, "th1_0", "grouped")}
        ns = {(0, 0): kept([P, PAIR, C1], F32, "ns0_0"), (0, 1): placed([P, PAIR, C1], F32, "ns0_1", AT_W01),
              (1, 1): kept([P, PAIR, C1], F32, "ns1_1"), (1, 0): placed([P, PAIR, C1], F32, "ns1_0", AT_W10)}
        sg = {}

        def functions(f, h):
            nc.scalar.activation(th[f, h][:], av[f, h][:], ACT.Tanh, scale=0.5)
            nc.scalar.activation(ns[f, h][:], av[f, h][:], ACT.Silu, scale=-1.0)

        nc.scalar.activation(ns[0, 0][:], av[0, 0][:], ACT.Silu, scale=-1.0)
        nc.scalar.activation(th[0, 0][:], av[0, 0][:], ACT.Tanh, scale=0.5)
        functions(0, 1)
        sort_columns(nc.scalar.copy, 0, 1, kept([P, PASSES, 2 * H], U8, "wet0"))
        functions(1, 1)
        functions(1, 0)

        def sigmoid(f, h, tile):
            sg[f, h] = tile
            nc.gpsimd.tensor_scalar(tile[:], th[f, h][:], 0.5, 0.5, ALU.mult, ALU.add)

        for h in range(2):
            sigmoid(0, h, th[0, h])

        gate_early = placed([P, C1], F32, "gate_early", AT_GATE0)
        nc.sync.dma_start(gate_early[:], gate[:, 0:C1])
        gates = [gate_early[:, 0:C2], gate_early[:, C2:]]
        load_words(raw[1][:], wet_rows[:, 2 * PASSES:, :])
        wet_sc.append(placed([P, 2 * PASSES, H], U8, "wet_sc1", AT_WET_SC1))
        gs.append(placed([P, PASSES, C1], U8, "gs1", AT_GS1))
        nc.gpsimd.memset(wet_sc[1][:].bitcast(I32), 0)
        nc.gpsimd.memset(gs[1][:].bitcast(I32), 0)
        place_sorted(1)
        place_picked(1)

        zs = [placed([P, PACK, C1], F32, "zs0", AT_ZS0)]

        def half_expert(e, half):
            f, u = divmod(e * C2, C1)
            acc = bank([P, PAIR, C2], "acc", 2 * e + half)
            for n in range(PAIR):
                r = PAIR * half + n
                for s in range(PASSES):
                    nc.tensor.matmul_mx(
                        out=acc[:, n, :],
                        lhsT=wet[e][:, s, 2 * P * r:2 * P * (r + 1)].bitcast(FP4X4), lhsT_scale=wet_sc[f][:, PASSES * (e % 2) + s, P * r:P * (r + 1)],
                        rhs=gw[s, e].bitcast(FP8X4), rhs_scale=gs[f][:, s, u:u + C2],
                        start=(s == 0), stop=(s == PASSES - 1))
            weight = gates[e].unsqueeze(1).to_broadcast([P, PAIR, C2])
            nc.vector.scalar_tensor_tensor(zs[f][:, PAIR * half:PAIR * (half + 1), u:u + C2], acc[:], -1.0, weight, ALU.mult, ALU.mult)

        def expert(e):
            for half in range(2):
                half_expert(e, half)

        slope = {}

        def derivative(tile, minus_silu, sigm):
            nc.vector.scalar_tensor_tensor(tile, minus_silu, 1.0, sigm, ALU.subtract, ALU.mult)

        def derivative_pair(f, h, tile):
            derivative(tile[:], ns[f, h][:], sg[f, h][:])
            for n in range(PAIR):
                slope[f, PAIR * h + n] = tile[:, n, :]

        def by_vector(window, offsets, lo, hi, values):
            nc.vector.tensor_copy(window[:].indirect(offsets[:, columns(lo, hi)]), values)

        def by_scalar(window, offsets, lo, hi, values):
            nc.scalar.activation(window[:].indirect(offsets[:, columns(lo, hi)]), values, ACT.Copy)

        def scatter_z(by, zw, e, r):
            f, u = divmod(e * C2, C1)
            by(zw[r], offs2_t, e * C2, (e + 1) * C2, zs[f][:, r, u:u + C2])

        def gradient(f, zw, grouped, planes):
            for r in planes:
                nc.gpsimd.tensor_tensor(grouped[:, :, r], zw[r][:, f * C1:(f + 1) * C1], slope[f, r], ALU.mult)

        def second_product(f, grouped, codes):
            scales = kept([P, C1], U8, "scales%d" % f)
            nc.vector.quantize_mx(out=codes[:].bitcast(FP8X4), scales=scales[:], in_=grouped[:].rearrange("p j r -> p (j r)"))
            acc2 = [bank([P, C1], "acc2", 4 * f + c) for c in range(K // P)]
            for c in (0, 2, 1, 3):
                nc.tensor.matmul_mx(
                    out=acc2[c][:],
                    lhsT=wgt[:, f, 2 * P * c:2 * P * (c + 1)].bitcast(FP4X4), lhsT_scale=wgt_sc[:, f, P * c:P * (c + 1)],
                    rhs=codes[:].bitcast(FP8X4), rhs_scale=scales[:],
                    start=True, stop=True)
            return acc2

        sort_columns(nc.vector.tensor_copy, 1, 1, kept([P, PASSES, 2 * H], U8, "wet1"))
        derivative_pair(0, 0, kept([P, PAIR, C1], F32, "slope0_0", "dyw1"))
        derivative_pair(0, 1, kept([P, PAIR, C1], F32, "slope0_1", "raw0"))
        sigmoid(1, 1, placed([P, PAIR, C1], F32, "sg1_1", AT_SG11))
        sigmoid(1, 0, placed([P, PAIR, C1], F32, "sg1_0", AT_SG10))
        expert(0)
        expert(1)
        derivative_pair(1, 1, placed([P, PAIR, C1], F32, "slope1_1", AT_SLOPE11))
        derivative_pair(1, 0, kept([P, PAIR, C1], F32, "slope1_0"))
        sort_columns(nc.vector.tensor_copy, 2, 2, placed([P, 2 * PASSES, 2 * H], U8, "wet_late", AT_WET_LATE))
        zw0 = [placed([P, T], F32, "zw0_0", AT_ZW00), kept([P, C1], F32, "zw0_1"), kept([P, C1], F32, "zw0_2"), placed([P, C1], F32, "zw0_3", AT_LAST0)]
        by_vector(zw0[0], offs2_t, 0, C1, zs[0][:, 0, :])
        gate_late = placed([P, C1], F32, "gate_late", AT_GATE1)
        nc.sync.dma_start(gate_late[:], gate[:, C1:])
        gates.extend([gate_late[:, 0:C2], gate_late[:, C2:]])
        zs.append(placed([P, PACK, C1], F32, "zs1", AT_ZS1))
        expert(2)
        expert(3)
        wgt = placed([P, G, 2 * K], U8, "wgt", AT_WGT)
        load_words(wgt[:], wgt_words.rearrange("f s p c -> p (f s) c"))
        wgt_sc = placed([P, G, K], U8, "wgt_sc", AT_WGT + 2 * KIB)
        nc.gpsimd.memset(wgt_sc[:].bitcast(I32), 0)
        load_scales(wgt_sc, wgt_scales.rearrange("f s b k -> (f s) b k"))

        for e, r in ((0, 1), (0, 2), (1, 1), (1, 2), (0, 3), (1, 3)):
            scatter_z(by_scalar, zw0, e, r)
        grouped0 = kept([P, C1, PACK], BF16, "grouped0", "grouped")
        gradient(0, zw0, grouped0, (1, 2, 0, 3))

        zw1 = [kept([P, T], F32, "zw1_0"), placed([P, T], F32, "zw1_1", AT_LAST1), kept([P, T], F32, "zw1_2"), kept([P, T], F32, "zw1_3")]
        by_vector(zw1[0], offs2_t, C1, T, zs[1][:, 0, :])
        for e, r in ((2, 2), (2, 3), (3, 2), (3, 3)):
            scatter_z(by_scalar, zw1, e, r)
        acc2 = second_product(0, grouped0, placed([P, C1], U32, "codes0", AT_GATE1))
        by_vector(zw1[1], offs2_t, C1, T, zs[1][:, 1, :])
        grouped1 = kept([P, C1, PACK], BF16, "grouped1", "grouped")
        gradient(1, zw1, grouped1, (0, 2, 3, 1))

        ow = [kept([P, T], F32, "ow%d" % c) for c in range(K // P)]
        dxs = [[kept([P, C1], F32, "dxs%d_%d" % (f, c)) for c in range(K // P)] for f in range(G)]

        def scatter_dx(by, f, c, lo, hi):
            by(ow[c], offs_t, f * C1 + lo, f * C1 + hi, dxs[f][c][:, lo:hi])

        held = acc2[1]
        for c in (0, 2):
            nc.scalar.activation(dxs[0][c][:], acc2[c][:], ACT.Copy)
        nc.scalar.activation(dxs[0][1][:, 0:EARLY], held[:, 0:EARLY], ACT.Copy)
        nc.scalar.activation(dxs[0][3][:], acc2[3][:], ACT.Copy)
        scatter_dx(by_vector, 0, 0, 0, C1)
        scatter_dx(by_vector, 0, 1, 0, EARLY)
        for lo in (0, C2):
            for c in (2, 3):
                scatter_dx(by_scalar, 0, c, lo, lo + C2)
        dx_late = placed([P, C1 - EARLY], F32, "dx_late", AT_LAST1)
        nc.vector.tensor_copy(dx_late[:], held[:, EARLY:])
        acc2 = second_product(1, grouped1, kept([P, C1], U32, "codes1"))
        by_vector(ow[1], offs_t, EARLY, C1, dx_late[:])
        for c in (0, 2, 3):
            nc.scalar.activation(dxs[1][c][:], acc2[c][:], ACT.Copy)
        nc.vector.tensor_copy(dxs[1][1][:], acc2[1][:])
        for c in (2, 3):
            for lo in (0, C2):
                scatter_dx(by_scalar, 1, c, lo, lo + C2)
        for c in (0, 1):
            scatter_dx(by_vector, 1, c, 0, C1)
        for c in (0, 2, 1, 3):
            (nc.scalar if c >= 2 else nc.sync).dma_start(out[c * P:(c + 1) * P, :], ow[c][:])
